import numpy as np
import ml_dtypes


def mxq(x, axis, fmt="e4m3"):
    dtype, down = {"e4m3": (ml_dtypes.float8_e4m3fn, 7), "e5m2": (ml_dtypes.float8_e5m2, 14)}[fmt]
    v = np.moveaxis(np.asarray(x, np.float32).astype(ml_dtypes.bfloat16).astype(np.float64), axis, -1)
    blocks = v.reshape(v.shape[:-1] + (-1, 32))
    amax = np.abs(blocks).max(-1, keepdims=True)
    byte = np.maximum(np.where(amax > 0, np.frexp(amax)[1] - 1 + 127, 0) - down, 1)
    scale = np.exp2(byte - 127.0)
    codes = (blocks / scale).astype(np.float32).astype(dtype).astype(np.float64)
    return np.moveaxis((codes * scale).reshape(v.shape), -1, axis)


WIDE = False


def mx_kscale(k):
    if not WIDE:
        return np.ones(k)
    levels = np.array([10, -10, 5, -5, 0])
    if k % 512:
        return np.exp2(np.random.permutation(np.resize(levels, k // 32))).repeat(32)
    a = np.empty((k // 512, 16))
    for p in range(k // 512):
        a[p, :8] = np.random.permutation(np.resize(levels, 8))
        for g in range(8):
            far = levels[np.abs(levels - a[p, g]) >= 10]
            a[p, g + 8] = far[np.random.randint(len(far))]
    return np.exp2(a.ravel()).repeat(32)


def f64(x):
    return np.asarray(x).astype(np.float64)


def striped8(idx):
    return np.concatenate([x.reshape(-1, 16).T for x in idx]).astype(np.uint16)


def runs(offs, k):
    lists = np.stack([offs[16 * r : 16 * r + 16].T.reshape(-1) for r in range(8)]).astype(np.int64)
    return lists[np.arange(k) % 512 // 64]


def pack_weight(w):
    k, n = w.shape
    w = f64(np.asarray(w, np.float32).astype(ml_dtypes.bfloat16)).reshape(k // 32, 32, n)
    amax = np.abs(w).max(1)
    byte = np.clip(np.where(amax > 0, np.frexp(amax)[1] - 1 + 127 - 7, 1), 1, 254)
    scaled = (w * np.exp2(127.0 - byte)[:, None, :]).reshape(k, n).astype(np.float32)
    words = np.ascontiguousarray(scaled.reshape(k // 512, 128, 4, n).transpose(0, 1, 3, 2)).astype(ml_dtypes.float8_e4m3fn).view(np.uint8)
    return words, np.ascontiguousarray(byte.astype(np.uint8).reshape(k // 512, 16, n))


def unpack_weight(words, scales):
    g, p, n, _ = words.shape
    vals = np.ascontiguousarray(words).view(ml_dtypes.float8_e4m3fn).astype(np.float64) * np.repeat(np.exp2(scales.astype(np.float64) - 127.0), 8, axis=1)[..., None]
    return vals.transpose(0, 1, 3, 2).reshape(g * 512, n)


def relu(v):
    return np.maximum(v, 0.0)

def planes(y):
    n, m = y.shape
    v = y.astype(np.float32).astype(ml_dtypes.bfloat16).astype(np.float64).reshape(n // 32, 32, m)
    top = np.abs(v).max(1)
    byte = np.clip(np.where(top > 0, np.frexp(top)[1] - 1 + 127 - 7, 1), 1, 254)
    codes = (v * np.exp2(127.0 - byte)[:, None, :]).reshape(n, m).astype(np.float32).astype(ml_dtypes.float8_e4m3fn).view(np.uint8)
    words = codes.reshape(n // 512, 128, 4, m).transpose(0, 1, 3, 2)
    return np.ascontiguousarray(words), np.ascontiguousarray(byte.astype(np.uint8).reshape(n // 512, 16, m))


K, T, S, N, H, U = 512, 2048, 512, 512, 512, 512


def setup_inputs():
    n = np.random.standard_normal
    s = mx_kscale(K)[:, None]
    u = mx_kscale(H)
    packed_xT = pack_weight(n((K, T)) * s)
    packed_w2 = pack_weight(n((H, N)) / np.sqrt(H) / u[:, None])
    return {
        "x_words": packed_xT[0],
        "x_scales": packed_xT[1],
        "w1": (n((K, H)) / np.sqrt(K) / s * u).astype(np.float32),
        "b1": (0.5 * n((H, 1)) * u[:, None]).astype(np.float32),
        "w2_words": packed_w2[0],
        "w2_scales": packed_w2[1],
        "scl": np.random.uniform(0.5, 1.5, (N, U)).astype(np.float32),
        "shf": n((N, U)).astype(np.float32),
        "offs": striped8(np.random.randint(0, T, (8, S))),
        "rg": striped8(np.random.randint(0, U, (8, S))),
    }


def reference(x_words, x_scales, w1, b1, w2_words, w2_scales, scl, shf, offs, rg):
    xq = unpack_weight(x_words, x_scales)[np.arange(K)[:, None], runs(offs, K)]
    h = relu((mxq(f64(w1), 0, "e4m3").T @ xq) + f64(b1))
    y = unpack_weight(w2_words, w2_scales).T @ mxq(h, 0, "e4m3")
    out_0 = y * (f64(scl)[np.arange(N)[:, None], runs(rg, N)]) + f64(shf)[np.arange(N)[:, None], runs(rg, N)]
    return (out_0,) + planes(out_0)

@@ -1,0 +1,229 @@
+from contextlib import ExitStack
+
+import concourse.mybir as mybir
+
+K, T, S, H, N, U = 512, 2048, 512, 512, 512, 512
+FLOPS = 2 * K * H * S + 2 * H * N * S
+
+F32 = mybir.dt.float32
+BF16 = mybir.dt.bfloat16
+I32 = mybir.dt.int32
+U32 = mybir.dt.uint32
+U16 = mybir.dt.uint16
+U8 = mybir.dt.uint8
+FP8X4 = mybir.dt.float8_e4m3fn_x4
+MULT = mybir.AluOpType.mult
+ADD = mybir.AluOpType.add
+RELU = mybir.ActivationFunctionType.Relu
+
+P = 128
+PACK = 4
+HALF = 256
+CHUNK = 128
+LIST = 16
+
+
+def tile_picked_decode2_relu_po_kernel(
+    tc, x_words, x_scales, w1, b1, w2_words, w2_scales, scl, shf, offs, rg, out_0, out_1, out_2
+):
+    nc = tc.nc
+    with ExitStack() as ctx:
+        keep = ctx.enter_context(tc.tile_pool(name="keep", bufs=1))
+        psum = ctx.enter_context(tc.psum_pool(name="psum", bufs=1))
+
+        def held(shape, dtype, name, tag=None):
+            return keep.tile(shape, dtype, name=name, tag=tag or name, align_bytes=64)
+
+        offs_sb = held([P, S // LIST], U16, "offs_sb")
+        rg_sb = held([P, S // LIST], U16, "rg_sb")
+        xs_table = held([P, T], U8, "xs_table")
+        xw_table = held([P, T], I32, "xw_table")
+        w1_raw = [held([P, PACK, HALF], F32, "w1_raw%d" % i) for i in range(2)]
+        b1_sb = held([P, PACK], F32, "b1_sb")
+        scl_sb = [held([P, U], F32, "scl_sb%d" % t) for t in range(2)]
+
+        nc.vector.memset(xs_table[:].bitcast(I32), 0)
+
+        xs_rows = x_scales[0].bitcast(I32).rearrange("(m r) c -> r m c", r=2)
+        w2s_rows = w2_scales[0].bitcast(I32).rearrange("(q b) c -> b q c", b=PACK)
+        w1_rows = w1.rearrange("(p j) c -> p j c", j=PACK)
+        scl_rows = scl.rearrange("(p t) u -> t p u", t=PACK)
+        shf_rows = shf.rearrange("(p t) u -> t p u", t=PACK)
+
+        nc.sync.dma_start(offs_sb[:], offs)
+        nc.sync.dma_start(rg_sb[:], rg)
+        nc.sync.dma_start(scl_sb[0][:], scl_rows[0])
+        for r in range(2):
+            nc.sync.dma_start(xs_table[r:P:LIST, :].bitcast(I32), xs_rows[r])
+        for i in range(2):
+            nc.sync.dma_start(w1_raw[i][:], w1_rows[:, :, i * HALF : (i + 1) * HALF])
+        nc.sync.dma_start(scl_sb[1][:], scl_rows[1])
+        nc.sync.dma_start(xw_table[:], x_words[0].rearrange("p n t -> p (n t)").bitcast(I32))
+        nc.sync.dma_start(b1_sb[:], b1.rearrange("(p t) o -> p (t o)", t=PACK))
+
+        def list_slice(lists, start, count):
+            return lists[:, start // LIST : (start + count) // LIST]
+
+        scl_picked = [held([P, PACK, HALF], F32, "scl_picked%d" % i) for i in range(2)]
+
+        def pick_scl(t):
+            for i in range(2):
+                nc.vector.tensor_copy(
+                    scl_picked[i][:, t, :], scl_sb[t][:].indirect(list_slice(rg_sb, i * HALF, HALF))
+                )
+
+        pick_scl(0)
+
+        xs_picked = held([P, S], U8, "xs_picked")
+        nc.vector.tensor_copy(xs_picked[:], xs_table[:].indirect(offs_sb[:]))
+        xs_plane = held([P, S], U8, "xs_plane")
+        nc.vector.tensor_copy(xs_plane[:].bitcast(I32), xs_picked[:].bitcast(I32))
+        for r in range(2):
+            nc.sync.dma_start(
+                xs_plane[2 + r : P : 32, :].bitcast(I32), xs_picked[LIST + r : P : 32, :].bitcast(I32)
+            )
+
+        scl_sb.append(held([P, U], F32, "scl_sb2", "scl_sb0"))
+        nc.sync.dma_start(scl_sb[2][:], scl_rows[2])
+        w2s_raw = held([P, N], U8, "w2s_raw", "xs_picked")
+        nc.gpsimd.memset(w2s_raw[:].bitcast(I32), 0)
+        for b in range(PACK):
+            nc.sync.dma_start(w2s_raw[b:P:32, :].bitcast(I32), w2s_rows[b])
+        pick_scl(1)
+
+        w1_grouped = held([P, PACK, P, PACK], BF16, "w1_grouped")
+        for i in range(2):
+            m_cols = slice(i * HALF // PACK, (i + 1) * HALF // PACK)
+            nc.scalar.copy(
+                w1_grouped[:, :, m_cols, :].rearrange("p t m j -> p m j t"),
+                w1_raw[i][:].rearrange("p j (m t) -> p m j t", t=PACK),
+            )
+        scl_sb.append(held([P, U], F32, "scl_sb3", "w1_raw0"))
+        nc.sync.dma_start(scl_sb[3][:], scl_rows[3])
+        w2w_raw = held([P, N], I32, "w2w_raw", "w1_raw1")
+        nc.sync.dma_start(w2w_raw[:], w2_words[0].rearrange("p n t -> p (n t)").bitcast(I32))
+        w1_codes = held([P, H], U32, "w1_codes")
+        w1_scales = held([P, H], U8, "w1_scales")
+        nc.vector.quantize_mx(
+            out=w1_codes[:].bitcast(FP8X4),
+            scales=w1_scales[:],
+            in_=w1_grouped[:].rearrange("p t m j -> p (t m j)"),
+        )
+
+        xw_picked = [held([P, HALF], U32, "xw_picked%d" % i) for i in range(2)]
+        for i in range(2):
+            nc.vector.tensor_copy(
+                xw_picked[i][:], xw_table[:].bitcast(U32).indirect(list_slice(offs_sb, i * HALF, HALF))
+            )
+
+        shf_sb = []
+
+        def load_shf(t, tag):
+            shf_sb.append(held([P, U], F32, "shf_sb%d" % t, tag))
+            nc.sync.dma_start(shf_sb[t][:], shf_rows[t])
+
+        for t, tag in enumerate(["scl_sb1", "w1_grouped", "xw_table"]):
+            load_shf(t, tag)
+
+        w2_codes = held([P, N], I32, "w2_codes")
+        w2_plane = held([P, N], U8, "w2_plane")
+        nc.vector.tensor_copy(
+            w2_codes[:].rearrange("p (t a i) -> p a t i", t=PACK, i=4),
+            w2w_raw[:].rearrange("p (a i t) -> p a t i", t=PACK, i=4),
+        )
+        nc.vector.tensor_copy(
+            w2_plane[:].rearrange("p (t a i) -> p a t i", t=PACK, i=16),
+            w2s_raw[:].rearrange("p (a i t) -> p a t i", t=PACK, i=16),
+        )
+
+        h_codes = [held([P, HALF], U32, "h_codes%d" % i) for i in range(2)]
+        h_scales = [held([P, HALF], U8, "h_scales%d" % i) for i in range(2)]
+
+        def first_layer(i):
+            cols = slice(i * HALF, (i + 1) * HALF)
+            banks = [psum.tile([P, 2, HALF], F32, name="h_bank%d_%d" % (i, u)) for u in range(2)]
+            h_rows = held([P, PACK, HALF], BF16, "h_rows%d" % i)
+            for t in range(PACK):
+                nc.tensor.matmul_mx(
+                    out=banks[t // 2][:, t % 2, :],
+                    lhsT=w1_codes[:, t * P : (t + 1) * P].bitcast(FP8X4),
+                    lhsT_scale=w1_scales[:, t * P : (t + 1) * P],
+                    rhs=xw_picked[i][:].bitcast(FP8X4),
+                    rhs_scale=xs_plane[:, cols],
+                    start=True,
+                    stop=True,
+                )
+            for t in range(PACK):
+                nc.scalar.activation(h_rows[:, t, :], banks[t // 2][:, t % 2, :], RELU, bias=b1_sb[:, t : t + 1])
+            h_grouped = held([P, HALF, PACK], BF16, "h_grouped%d" % i)
+            nc.scalar.copy(
+                h_grouped[:].rearrange("p (c i) t -> p c t i", i=4),
+                h_rows[:].rearrange("p t (c i) -> p c t i", i=4),
+            )
+            nc.vector.quantize_mx(
+                out=h_codes[i][:].bitcast(FP8X4),
+                scales=h_scales[i][:],
+                in_=h_grouped[:].rearrange("p c t -> p (c t)"),
+            )
+
+        first_layer(0)
+        pick_scl(2)
+        load_shf(3, "scl_sb0")
+        first_layer(1)
+        pick_scl(3)
+
+        out_codes = held([P, S], U32, "out_codes")
+        out_scales = held([P, S], U8, "out_scales")
+        out_rows = out_0.rearrange("(p t) j -> p t j", t=PACK)
+        out_words = out_1[0].rearrange("p n t -> p (n t)").bitcast(I32)
+        out_planes = out_2[0].bitcast(I32).rearrange("(q b) c -> b q c", b=PACK)
+        grouped = []
+
+        def second_layer(c):
+            i, inner = divmod(c * CHUNK, HALF)
+            inner_cols = slice(inner, inner + CHUNK)
+            cols = slice(c * CHUNK, (c + 1) * CHUNK)
+            bank = psum.tile([P, PACK, CHUNK], F32, name="y_bank%d" % c)
+            for t in range(PACK):
+                nc.tensor.matmul_mx(
+                    out=bank[:, t, :],
+                    lhsT=w2_codes[:, t * P : (t + 1) * P].bitcast(FP8X4),
+                    lhsT_scale=w2_plane[:, t * P : (t + 1) * P],
+                    rhs=h_codes[i][:, inner_cols].bitcast(FP8X4),
+                    rhs_scale=h_scales[i][:, inner_cols],
+                    start=True,
+                    stop=True,
+                )
+            scaled = held([P, PACK, CHUNK], F32, "scaled%d" % c)
+            nc.vector.tensor_tensor(scaled[:], bank[:], scl_picked[i][:, :, inner_cols], MULT)
+            result = held([P, PACK, CHUNK], F32, "result%d" % c)
+            for t in range(PACK):
+                nc.vector.tensor_tensor(
+                    result[:, t, :], shf_sb[t][:].indirect(list_slice(rg_sb, c * CHUNK, CHUNK)), scaled[:, t, :], ADD
+                )
+            nc.sync.dma_start(out_rows[:, :, cols], result[:])
+            rounded = held([P, CHUNK, PACK], BF16, "rounded%d" % c)
+            nc.scalar.copy(
+                rounded[:].rearrange("p (c i) t -> p c t i", i=4),
+                result[:].rearrange("p t (c i) -> p c t i", i=4),
+            )
+            grouped.append(rounded)
+
+        def quantise_result(c):
+            cols = slice(c * CHUNK, (c + 1) * CHUNK)
+            nc.vector.quantize_mx(
+                out=out_codes[:, cols].bitcast(FP8X4),
+                scales=out_scales[:, cols],
+                in_=grouped[c][:].rearrange("p c t -> p (c t)"),
+            )
+            nc.sync.dma_start(out_words[:, cols], out_codes[:, cols].bitcast(I32))
+
+        chunks = S // CHUNK
+        for c in range(chunks):
+            second_layer(c)
+            if c > 0:
+                quantise_result(c - 1)
+        quantise_result(chunks - 1)
+        for b in range(PACK):
+            queue = nc.scalar if b % 2 else nc.sync
+            queue.dma_start(out_planes[b], out_scales[b:P:32, :].bitcast(I32))

@@ -29,6 +29,8 @@ def tile_picked_decode2_relu_po_kernel(
     nc = tc.nc
     with ExitStack() as ctx:
         keep = ctx.enter_context(tc.tile_pool(name="keep", bufs=1))
+        shared = ctx.enter_context(tc.tile_pool(name="shared", bufs=1))
+        moved = ctx.enter_context(tc.tile_pool(name="moved", bufs=1))
         psum = ctx.enter_context(tc.psum_pool(name="psum", bufs=1))
 
         def held(shape, dtype, name, tag=None):
@@ -36,13 +38,15 @@ def tile_picked_decode2_relu_po_kernel(
 
         offs_sb = held([P, S // LIST], U16, "offs_sb")
         rg_sb = held([P, S // LIST], U16, "rg_sb")
-        xs_table = held([P, T], U8, "xs_table")
+        xs_table = shared.tile([P, T], U8, name="xs_table", align_bytes=64, offset=4 * S - 64)
         xw_table = held([P, T], I32, "xw_table")
-        w1_raw = [held([P, PACK, HALF], F32, "w1_raw%d" % i) for i in range(2)]
+        w1_raw = held([P, PACK, H], F32, "w1_raw")
+        w2s_raw = held([P, N], U8, "w2s_raw")
         b1_sb = held([P, PACK], F32, "b1_sb")
         scl_sb = [held([P, U], F32, "scl_sb%d" % t) for t in range(2)]
 
         nc.vector.memset(xs_table[:].bitcast(I32), 0)
+        nc.gpsimd.memset(w2s_raw[:].bitcast(I32), 0)
 
         xs_rows = x_scales[0].bitcast(I32).rearrange("(m r) c -> r m c", r=2)
         w2s_rows = w2_scales[0].bitcast(I32).rearrange("(q b) c -> b q c", b=PACK)
@@ -52,29 +56,20 @@ def tile_picked_decode2_relu_po_kernel(
 
         nc.sync.dma_start(offs_sb[:], offs)
         nc.sync.dma_start(rg_sb[:], rg)
-        nc.sync.dma_start(scl_sb[0][:], scl_rows[0])
         for r in range(2):
-            nc.sync.dma_start(xs_table[r:P:LIST, :].bitcast(I32), xs_rows[r])
-        for i in range(2):
-            nc.sync.dma_start(w1_raw[i][:], w1_rows[:, :, i * HALF : (i + 1) * HALF])
-        nc.sync.dma_start(scl_sb[1][:], scl_rows[1])
+            nc.scalar.dma_start(xs_table[r:P:LIST, :].bitcast(I32), xs_rows[r])
+        nc.sync.dma_start(w1_raw[:], w1_rows)
+        for t in range(2):
+            nc.sync.dma_start(scl_sb[t][:], scl_rows[t])
         nc.sync.dma_start(xw_table[:], x_words[0].rearrange("p n t -> p (n t)").bitcast(I32))
-        nc.sync.dma_start(b1_sb[:], b1.rearrange("(p t) o -> p (t o)", t=PACK))
+        nc.gpsimd.dma_start(b1_sb[:], b1.rearrange("(p t) o -> p (t o)", t=PACK))
+        for b in range(PACK):
+            nc.gpsimd.dma_start(w2s_raw[b:P:32, :].bitcast(I32), w2s_rows[b])
 
         def list_slice(lists, start, count):
             return lists[:, start // LIST : (start + count) // LIST]
 
-        scl_picked = [held([P, PACK, HALF], F32, "scl_picked%d" % i) for i in range(2)]
-
-        def pick_scl(t):
-            for i in range(2):
-                nc.vector.tensor_copy(
-                    scl_picked[i][:, t, :], scl_sb[t][:].indirect(list_slice(rg_sb, i * HALF, HALF))
-                )
-
-        pick_scl(0)
-
-        xs_picked = held([P, S], U8, "xs_picked")
+        xs_picked = moved.tile([P, S], U8, name="xs_picked", align_bytes=64, offset=4 * N - 64)
         nc.vector.tensor_copy(xs_picked[:], xs_table[:].indirect(offs_sb[:]))
         xs_plane = held([P, S], U8, "xs_plane")
         nc.vector.tensor_copy(xs_plane[:].bitcast(I32), xs_picked[:].bitcast(I32))
@@ -83,37 +78,40 @@ def tile_picked_decode2_relu_po_kernel(
                 xs_plane[2 + r : P : 32, :].bitcast(I32), xs_picked[LIST + r : P : 32, :].bitcast(I32)
             )
 
+        scl_picked = shared.tile([P, PACK, S], F32, name="scl_picked", align_bytes=64, offset=4 * S + T - 128)
+
+        def pick_scl(t):
+            for i in range(2):
+                nc.vector.tensor_copy(
+                    scl_picked[:, t, i * HALF : (i + 1) * HALF], scl_sb[t][:].indirect(list_slice(rg_sb, i * HALF, HALF))
+                )
+
+        pick_scl(0)
         scl_sb.append(held([P, U], F32, "scl_sb2", "scl_sb0"))
         nc.sync.dma_start(scl_sb[2][:], scl_rows[2])
-        w2s_raw = held([P, N], U8, "w2s_raw", "xs_picked")
-        nc.gpsimd.memset(w2s_raw[:].bitcast(I32), 0)
-        for b in range(PACK):
-            nc.sync.dma_start(w2s_raw[b:P:32, :].bitcast(I32), w2s_rows[b])
+        w2w_raw = moved.tile([P, N], I32, name="w2w_raw", align_bytes=64, offset=0)
+        nc.sync.dma_start(w2w_raw[:], w2_words[0].rearrange("p n t -> p (n t)").bitcast(I32))
         pick_scl(1)
+        scl_sb.append(held([P, U], F32, "scl_sb3", "scl_sb1"))
+        nc.sync.dma_start(scl_sb[3][:], scl_rows[3])
 
         w1_grouped = held([P, PACK, P, PACK], BF16, "w1_grouped")
-        for i in range(2):
-            m_cols = slice(i * HALF // PACK, (i + 1) * HALF // PACK)
-            nc.scalar.copy(
-                w1_grouped[:, :, m_cols, :].rearrange("p t m j -> p m j t"),
-                w1_raw[i][:].rearrange("p j (m t) -> p m j t", t=PACK),
-            )
-        scl_sb.append(held([P, U], F32, "scl_sb3", "w1_raw0"))
-        nc.sync.dma_start(scl_sb[3][:], scl_rows[3])
-        w2w_raw = held([P, N], I32, "w2w_raw", "w1_raw1")
-        nc.sync.dma_start(w2w_raw[:], w2_words[0].rearrange("p n t -> p (n t)").bitcast(I32))
+        nc.scalar.copy(
+            w1_grouped[:].rearrange("p t m j -> p m j t"),
+            w1_raw[:].rearrange("p j (m t) -> p m j t", t=PACK),
+        )
         w1_codes = held([P, H], U32, "w1_codes")
-        w1_scales = held([P, H], U8, "w1_scales")
+        w1_scales = shared.tile([P, H], U8, name="w1_scales", align_bytes=64, offset=4 * S)
         nc.vector.quantize_mx(
             out=w1_codes[:].bitcast(FP8X4),
             scales=w1_scales[:],
             in_=w1_grouped[:].rearrange("p t m j -> p (t m j)"),
         )
 
-        xw_picked = [held([P, HALF], U32, "xw_picked%d" % i) for i in range(2)]
+        xw_picked = shared.tile([P, S], U32, name="xw_picked", align_bytes=64, offset=0)
         for i in range(2):
             nc.vector.tensor_copy(
-                xw_picked[i][:], xw_table[:].bitcast(U32).indirect(list_slice(offs_sb, i * HALF, HALF))
+                xw_picked[:, i * HALF : (i + 1) * HALF], xw_table[:].bitcast(U32).indirect(list_slice(offs_sb, i * HALF, HALF))
             )
 
         shf_sb = []
@@ -122,55 +120,60 @@ def tile_picked_decode2_relu_po_kernel(
             shf_sb.append(held([P, U], F32, "shf_sb%d" % t, tag))
             nc.sync.dma_start(shf_sb[t][:], shf_rows[t])
 
-        for t, tag in enumerate(["scl_sb1", "w1_grouped", "xw_table"]):
-            load_shf(t, tag)
+        load_shf(0, "w1_grouped")
+        shf_sb.append(moved.tile([P, U], F32, name="shf_sb1", align_bytes=64, offset=4 * N + S - 128))
+        nc.sync.dma_start(shf_sb[1][:], shf_rows[1])
+        load_shf(2, "xw_table")
 
         w2_codes = held([P, N], I32, "w2_codes")
         w2_plane = held([P, N], U8, "w2_plane")
         nc.vector.tensor_copy(
-            w2_codes[:].rearrange("p (t a i) -> p a t i", t=PACK, i=4),
-            w2w_raw[:].rearrange("p (a i t) -> p a t i", t=PACK, i=4),
-        )
-        nc.vector.tensor_copy(
             w2_plane[:].rearrange("p (t a i) -> p a t i", t=PACK, i=16),
             w2s_raw[:].rearrange("p (a i t) -> p a t i", t=PACK, i=16),
         )
+        nc.vector.tensor_copy(
+            w2_codes[:].rearrange("p (t a i) -> p a t i", t=PACK, i=4),
+            w2w_raw[:].rearrange("p (a i t) -> p a t i", t=PACK, i=4),
+        )
 
-        h_codes = [held([P, HALF], U32, "h_codes%d" % i) for i in range(2)]
-        h_scales = [held([P, HALF], U8, "h_scales%d" % i) for i in range(2)]
+        h_banks = [psum.tile([P, S], F32, name="h_bank%d" % t) for t in range(PACK)]
+        h_parts = []
 
-        def first_layer(i):
-            cols = slice(i * HALF, (i + 1) * HALF)
-            banks = [psum.tile([P, 2, HALF], F32, name="h_bank%d_%d" % (i, u)) for u in range(2)]
-            h_rows = held([P, PACK, HALF], BF16, "h_rows%d" % i)
+        def first_layer(start, width):
+            cols = slice(start, start + width)
+            h_rows = held([P, PACK, width], BF16, "h_rows%d" % start)
             for t in range(PACK):
                 nc.tensor.matmul_mx(
-                    out=banks[t // 2][:, t % 2, :],
+                    out=h_banks[t][:, cols],
                     lhsT=w1_codes[:, t * P : (t + 1) * P].bitcast(FP8X4),
                     lhsT_scale=w1_scales[:, t * P : (t + 1) * P],
-                    rhs=xw_picked[i][:].bitcast(FP8X4),
+                    rhs=xw_picked[:, cols].bitcast(FP8X4),
                     rhs_scale=xs_plane[:, cols],
                     start=True,
                     stop=True,
                 )
-            for t in range(PACK):
-                nc.scalar.activation(h_rows[:, t, :], banks[t // 2][:, t % 2, :], RELU, bias=b1_sb[:, t : t + 1])
-            h_grouped = held([P, HALF, PACK], BF16, "h_grouped%d" % i)
+                nc.scalar.activation(h_rows[:, t, :], h_banks[t][:, cols], RELU, bias=b1_sb[:, t : t + 1])
+            h_grouped = held([P, width, PACK], BF16, "h_grouped%d" % start)
             nc.scalar.copy(
                 h_grouped[:].rearrange("p (c i) t -> p c t i", i=4),
                 h_rows[:].rearrange("p t (c i) -> p c t i", i=4),
             )
+            h_codes = held([P, width], U32, "h_codes%d" % start)
+            h_scales = held([P, width], U8, "h_scales%d" % start)
             nc.vector.quantize_mx(
-                out=h_codes[i][:].bitcast(FP8X4),
-                scales=h_scales[i][:],
+                out=h_codes[:].bitcast(FP8X4),
+                scales=h_scales[:],
                 in_=h_grouped[:].rearrange("p c t -> p (c t)"),
             )
+            for inner in range(0, width, CHUNK):
+                h_parts.append((h_codes[:, inner : inner + CHUNK], h_scales[:, inner : inner + CHUNK]))
 
-        first_layer(0)
+        first_layer(0, CHUNK)
         pick_scl(2)
         load_shf(3, "scl_sb0")
-        first_layer(1)
+        first_layer(CHUNK, CHUNK)
         pick_scl(3)
+        first_layer(HALF, HALF)
 
         out_codes = held([P, S], U32, "out_codes")
         out_scales = held([P, S], U8, "out_scales")
@@ -178,10 +181,9 @@ def tile_picked_decode2_relu_po_kernel(
         out_words = out_1[0].rearrange("p n t -> p (n t)").bitcast(I32)
         out_planes = out_2[0].bitcast(I32).rearrange("(q b) c -> b q c", b=PACK)
         grouped = []
+        chunks = S // CHUNK
 
         def second_layer(c):
-            i, inner = divmod(c * CHUNK, HALF)
-            inner_cols = slice(inner, inner + CHUNK)
             cols = slice(c * CHUNK, (c + 1) * CHUNK)
             bank = psum.tile([P, PACK, CHUNK], F32, name="y_bank%d" % c)
             for t in range(PACK):
@@ -189,13 +191,13 @@ def tile_picked_decode2_relu_po_kernel(
                     out=bank[:, t, :],
                     lhsT=w2_codes[:, t * P : (t + 1) * P].bitcast(FP8X4),
                     lhsT_scale=w2_plane[:, t * P : (t + 1) * P],
-                    rhs=h_codes[i][:, inner_cols].bitcast(FP8X4),
-                    rhs_scale=h_scales[i][:, inner_cols],
+                    rhs=h_parts[c][0].bitcast(FP8X4),
+                    rhs_scale=h_parts[c][1],
                     start=True,
                     stop=True,
                 )
             scaled = held([P, PACK, CHUNK], F32, "scaled%d" % c)
-            nc.vector.tensor_tensor(scaled[:], bank[:], scl_picked[i][:, :, inner_cols], MULT)
+            nc.vector.tensor_tensor(scaled[:], bank[:], scl_picked[:, :, cols], MULT)
             result = held([P, PACK, CHUNK], F32, "result%d" % c)
             for t in range(PACK):
                 nc.vector.tensor_tensor(
@@ -203,7 +205,8 @@ def tile_picked_decode2_relu_po_kernel(
                 )
             nc.sync.dma_start(out_rows[:, :, cols], result[:])
             rounded = held([P, CHUNK, PACK], BF16, "rounded%d" % c)
-            nc.scalar.copy(
+            copy = nc.vector.tensor_copy if c == chunks - 1 else nc.scalar.copy
+            copy(
                 rounded[:].rearrange("p (c i) t -> p c t i", i=4),
                 result[:].rearrange("p t (c i) -> p c t i", i=4),
             )
@@ -218,7 +221,6 @@ def tile_picked_decode2_relu_po_kernel(
             )
             nc.sync.dma_start(out_words[:, cols], out_codes[:, cols].bitcast(I32))
 
-        chunks = S // CHUNK
         for c in range(chunks):
             second_layer(c)
             if c > 0:

@@ -19,7 +19,9 @@ RELU = mybir.ActivationFunctionType.Relu
 P = 128
 PACK = 4
 HALF = 256
-CHUNK = 128
+HIDDEN_CHUNKS = ((0, 128), (128, 128), (256, 256))
+CHUNKS = ((0, 128), (128, 128), (256, 128), (384, 128))
+BANK = 512
 LIST = 16
 
 
@@ -29,8 +31,7 @@ def tile_picked_decode2_relu_po_kernel(
     nc = tc.nc
     with ExitStack() as ctx:
         keep = ctx.enter_context(tc.tile_pool(name="keep", bufs=1))
-        shared = ctx.enter_context(tc.tile_pool(name="shared", bufs=1))
-        moved = ctx.enter_context(tc.tile_pool(name="moved", bufs=1))
+        words = ctx.enter_context(tc.tile_pool(name="words", bufs=1))
         psum = ctx.enter_context(tc.psum_pool(name="psum", bufs=1))
 
         def held(shape, dtype, name, tag=None):
@@ -38,15 +39,14 @@ def tile_picked_decode2_relu_po_kernel(
 
         offs_sb = held([P, S // LIST], U16, "offs_sb")
         rg_sb = held([P, S // LIST], U16, "rg_sb")
-        xs_table = shared.tile([P, T], U8, name="xs_table", align_bytes=64, offset=4 * S - 64)
-        xw_table = held([P, T], I32, "xw_table")
-        w1_raw = held([P, PACK, H], F32, "w1_raw")
-        w2s_raw = held([P, N], U8, "w2s_raw")
+        xs_table = held([P, T], U8, "xs_table")
+        xw_table = words.tile([P, T], I32, name="xw_table", align_bytes=64, offset=0)
+        w1_raw = [held([P, PACK, HALF], F32, "w1_raw%d" % i) for i in range(2)]
         b1_sb = held([P, PACK], F32, "b1_sb")
         scl_sb = [held([P, U], F32, "scl_sb%d" % t) for t in range(2)]
 
-        nc.vector.memset(xs_table[:].bitcast(I32), 0)
-        nc.gpsimd.memset(w2s_raw[:].bitcast(I32), 0)
+        nc.vector.memset(xs_table[:, : 3 * T // 4].bitcast(I32), 0)
+        nc.gpsimd.memset(xs_table[:, 3 * T // 4 :].bitcast(I32), 0)
 
         xs_rows = x_scales[0].bitcast(I32).rearrange("(m r) c -> r m c", r=2)
         w2s_rows = w2_scales[0].bitcast(I32).rearrange("(q b) c -> b q c", b=PACK)
@@ -54,22 +54,38 @@ def tile_picked_decode2_relu_po_kernel(
         scl_rows = scl.rearrange("(p t) u -> t p u", t=PACK)
         shf_rows = shf.rearrange("(p t) u -> t p u", t=PACK)
 
-        nc.sync.dma_start(offs_sb[:], offs)
         nc.sync.dma_start(rg_sb[:], rg)
+        nc.sync.dma_start(scl_sb[0][:], scl_rows[0])
+        nc.sync.dma_start(offs_sb[:], offs)
+        nc.sync.dma_start(b1_sb[:], b1.rearrange("(p t) o -> p (t o)", t=PACK))
+        nc.sync.dma_start(w1_raw[0][:], w1_rows[:, :, :HALF])
         for r in range(2):
-            nc.scalar.dma_start(xs_table[r:P:LIST, :].bitcast(I32), xs_rows[r])
-        nc.sync.dma_start(w1_raw[:], w1_rows)
-        for t in range(2):
-            nc.sync.dma_start(scl_sb[t][:], scl_rows[t])
+            nc.sync.dma_start(xs_table[r:P:LIST, :].bitcast(I32), xs_rows[r])
+        nc.sync.dma_start(scl_sb[1][:], scl_rows[1])
+        nc.sync.dma_start(w1_raw[1][:], w1_rows[:, :, HALF:])
         nc.sync.dma_start(xw_table[:], x_words[0].rearrange("p n t -> p (n t)").bitcast(I32))
-        nc.gpsimd.dma_start(b1_sb[:], b1.rearrange("(p t) o -> p (t o)", t=PACK))
-        for b in range(PACK):
-            nc.gpsimd.dma_start(w2s_raw[b:P:32, :].bitcast(I32), w2s_rows[b])
 
         def list_slice(lists, start, count):
             return lists[:, start // LIST : (start + count) // LIST]
 
-        xs_picked = moved.tile([P, S], U8, name="xs_picked", align_bytes=64, offset=4 * N - 64)
+        scl_picked = {}
+
+        def pick_scl(t, halves=(0, 1), tag=None):
+            for i in halves:
+                if (t // 2, i) not in scl_picked:
+                    scl_picked[t // 2, i] = held([P, 2, HALF], F32, "scl_picked%d_%d" % (t // 2, i), tag)
+                nc.vector.tensor_copy(
+                    scl_picked[t // 2, i][:, t % 2, :],
+                    scl_sb[t][:].indirect(list_slice(rg_sb, i * HALF, HALF)),
+                )
+
+        pick_scl(0)
+        w2s_raw = held([P, N], U8, "w2s_raw", "scl_sb0")
+        nc.vector.memset(w2s_raw[:].bitcast(I32), 0)
+        for b in range(PACK):
+            nc.sync.dma_start(w2s_raw[b:P:32, :].bitcast(I32), w2s_rows[b])
+
+        xs_picked = held([P, S], U8, "xs_picked")
         nc.vector.tensor_copy(xs_picked[:], xs_table[:].indirect(offs_sb[:]))
         xs_plane = held([P, S], U8, "xs_plane")
         nc.vector.tensor_copy(xs_plane[:].bitcast(I32), xs_picked[:].bitcast(I32))
@@ -77,38 +93,29 @@ def tile_picked_decode2_relu_po_kernel(
             nc.sync.dma_start(
                 xs_plane[2 + r : P : 32, :].bitcast(I32), xs_picked[LIST + r : P : 32, :].bitcast(I32)
             )
-
-        scl_picked = shared.tile([P, PACK, S], F32, name="scl_picked", align_bytes=64, offset=4 * S + T - 128)
-
-        def pick_scl(t):
-            for i in range(2):
-                nc.vector.tensor_copy(
-                    scl_picked[:, t, i * HALF : (i + 1) * HALF], scl_sb[t][:].indirect(list_slice(rg_sb, i * HALF, HALF))
-                )
-
-        pick_scl(0)
-        scl_sb.append(held([P, U], F32, "scl_sb2", "scl_sb0"))
-        nc.sync.dma_start(scl_sb[2][:], scl_rows[2])
-        w2w_raw = moved.tile([P, N], I32, name="w2w_raw", align_bytes=64, offset=0)
-        nc.sync.dma_start(w2w_raw[:], w2_words[0].rearrange("p n t -> p (n t)").bitcast(I32))
         pick_scl(1)
-        scl_sb.append(held([P, U], F32, "scl_sb3", "scl_sb1"))
-        nc.sync.dma_start(scl_sb[3][:], scl_rows[3])
 
         w1_grouped = held([P, PACK, P, PACK], BF16, "w1_grouped")
-        nc.scalar.copy(
-            w1_grouped[:].rearrange("p t m j -> p m j t"),
-            w1_raw[:].rearrange("p j (m t) -> p m j t", t=PACK),
-        )
+        for i in range(2):
+            m_cols = slice(i * HALF // PACK, (i + 1) * HALF // PACK)
+            nc.scalar.copy(
+                w1_grouped[:, :, m_cols, :].rearrange("p t m j -> p m j t"),
+                w1_raw[i][:].rearrange("p j (m t) -> p m j t", t=PACK),
+            )
+        for t, tag in ((2, "w1_raw0"), (3, "scl_sb1")):
+            scl_sb.append(held([P, U], F32, "scl_sb%d" % t, tag))
+            nc.sync.dma_start(scl_sb[t][:], scl_rows[t])
+        w2w_raw = held([P, N], I32, "w2w_raw", "w1_raw1")
+        nc.sync.dma_start(w2w_raw[:], w2_words[0].rearrange("p n t -> p (n t)").bitcast(I32))
         w1_codes = held([P, H], U32, "w1_codes")
-        w1_scales = shared.tile([P, H], U8, name="w1_scales", align_bytes=64, offset=4 * S)
+        w1_scales = held([P, H], U8, "w1_scales")
         nc.vector.quantize_mx(
             out=w1_codes[:].bitcast(FP8X4),
             scales=w1_scales[:],
             in_=w1_grouped[:].rearrange("p t m j -> p (t m j)"),
         )
 
-        xw_picked = shared.tile([P, S], U32, name="xw_picked", align_bytes=64, offset=0)
+        xw_picked = held([P, S], U32, "xw_picked")
         for i in range(2):
             nc.vector.tensor_copy(
                 xw_picked[:, i * HALF : (i + 1) * HALF], xw_table[:].bitcast(U32).indirect(list_slice(offs_sb, i * HALF, HALF))
@@ -120,10 +127,11 @@ def tile_picked_decode2_relu_po_kernel(
             shf_sb.append(held([P, U], F32, "shf_sb%d" % t, tag))
             nc.sync.dma_start(shf_sb[t][:], shf_rows[t])
 
-        load_shf(0, "w1_grouped")
-        shf_sb.append(moved.tile([P, U], F32, name="shf_sb1", align_bytes=64, offset=4 * N + S - 128))
-        nc.sync.dma_start(shf_sb[1][:], shf_rows[1])
-        load_shf(2, "xw_table")
+        for t, tag in enumerate(["w1_grouped", "xs_picked"]):
+            load_shf(t, tag)
+        for t in (2, 3):
+            shf_sb.append(words.tile([P, U], F32, name="shf_sb%d" % t, align_bytes=64, offset=4 * U * (t - 2)))
+            nc.sync.dma_start(shf_sb[t][:], shf_rows[t])
 
         w2_codes = held([P, N], I32, "w2_codes")
         w2_plane = held([P, N], U8, "w2_plane")
@@ -137,7 +145,8 @@ def tile_picked_decode2_relu_po_kernel(
         )
 
         h_banks = [psum.tile([P, S], F32, name="h_bank%d" % t) for t in range(PACK)]
-        h_parts = []
+        h_codes = held([P, S], U32, "h_codes")
+        h_scales = held([P, S], U8, "h_scales")
 
         def first_layer(start, width):
             cols = slice(start, start + width)
@@ -158,22 +167,19 @@ def tile_picked_decode2_relu_po_kernel(
                 h_grouped[:].rearrange("p (c i) t -> p c t i", i=4),
                 h_rows[:].rearrange("p t (c i) -> p c t i", i=4),
             )
-            h_codes = held([P, width], U32, "h_codes%d" % start)
-            h_scales = held([P, width], U8, "h_scales%d" % start)
             nc.vector.quantize_mx(
-                out=h_codes[:].bitcast(FP8X4),
-                scales=h_scales[:],
+                out=h_codes[:, cols].bitcast(FP8X4),
+                scales=h_scales[:, cols],
                 in_=h_grouped[:].rearrange("p c t -> p (c t)"),
             )
-            for inner in range(0, width, CHUNK):
-                h_parts.append((h_codes[:, inner : inner + CHUNK], h_scales[:, inner : inner + CHUNK]))
 
-        first_layer(0, CHUNK)
-        pick_scl(2)
-        load_shf(3, "scl_sb0")
-        first_layer(CHUNK, CHUNK)
-        pick_scl(3)
-        first_layer(HALF, HALF)
+        pick_scl(2, (0,))
+        pick_scl(3, (0,))
+        first_layer(*HIDDEN_CHUNKS[0])
+        pick_scl(2, (1,), "h_grouped0")
+        first_layer(*HIDDEN_CHUNKS[1])
+        pick_scl(3, (1,))
+        first_layer(*HIDDEN_CHUNKS[2])
 
         out_codes = held([P, S], U32, "out_codes")
         out_scales = held([P, S], U8, "out_scales")
@@ -181,30 +187,39 @@ def tile_picked_decode2_relu_po_kernel(
         out_words = out_1[0].rearrange("p n t -> p (n t)").bitcast(I32)
         out_planes = out_2[0].bitcast(I32).rearrange("(q b) c -> b q c", b=PACK)
         grouped = []
-        chunks = S // CHUNK
+        chunks = len(CHUNKS)
 
         def second_layer(c):
-            cols = slice(c * CHUNK, (c + 1) * CHUNK)
-            bank = psum.tile([P, PACK, CHUNK], F32, name="y_bank%d" % c)
-            for t in range(PACK):
-                nc.tensor.matmul_mx(
-                    out=bank[:, t, :],
-                    lhsT=w2_codes[:, t * P : (t + 1) * P].bitcast(FP8X4),
-                    lhsT_scale=w2_plane[:, t * P : (t + 1) * P],
-                    rhs=h_parts[c][0].bitcast(FP8X4),
-                    rhs_scale=h_parts[c][1],
-                    start=True,
-                    stop=True,
-                )
-            scaled = held([P, PACK, CHUNK], F32, "scaled%d" % c)
-            nc.vector.tensor_tensor(scaled[:], bank[:], scl_picked[:, :, cols], MULT)
-            result = held([P, PACK, CHUNK], F32, "result%d" % c)
+            start, width = CHUNKS[c]
+            cols = slice(start, start + width)
+            per_bank = BANK // width
+            scaled = held([P, PACK, width], F32, "scaled%d" % c)
+            for first in range(0, PACK, per_bank):
+                bank = psum.tile([P, per_bank, width], F32, name="y_bank%d_%d" % (c, first))
+                for t in range(first, first + per_bank):
+                    nc.tensor.matmul_mx(
+                        out=bank[:, t - first, :],
+                        lhsT=w2_codes[:, t * P : (t + 1) * P].bitcast(FP8X4),
+                        lhsT_scale=w2_plane[:, t * P : (t + 1) * P],
+                        rhs=h_codes[:, cols].bitcast(FP8X4),
+                        rhs_scale=h_scales[:, cols],
+                        start=True,
+                        stop=True,
+                    )
+                for pair in range(0, per_bank, 2):
+                    planes = slice(first + pair, first + pair + 2)
+                    half, inner = divmod(start, HALF)
+                    picked = scl_picked[(first + pair) // 2, half]
+                    nc.vector.tensor_tensor(
+                        scaled[:, planes, :], bank[:, pair : pair + 2, :], picked[:, :, inner : inner + width], MULT
+                    )
+            result = held([P, PACK, width], F32, "result%d" % c, "h_grouped256" if c == 1 else None)
             for t in range(PACK):
                 nc.vector.tensor_tensor(
-                    result[:, t, :], shf_sb[t][:].indirect(list_slice(rg_sb, c * CHUNK, CHUNK)), scaled[:, t, :], ADD
+                    result[:, t, :], shf_sb[t][:].indirect(list_slice(rg_sb, start, width)), scaled[:, t, :], ADD
                 )
             nc.sync.dma_start(out_rows[:, :, cols], result[:])
-            rounded = held([P, CHUNK, PACK], BF16, "rounded%d" % c)
+            rounded = held([P, width, PACK], BF16, "rounded%d" % c, "h_rows256" if c == 0 else None)
             copy = nc.vector.tensor_copy if c == chunks - 1 else nc.scalar.copy
             copy(
                 rounded[:].rearrange("p (c i) t -> p c t i", i=4),
@@ -213,7 +228,8 @@ def tile_picked_decode2_relu_po_kernel(
             grouped.append(rounded)
 
         def quantise_result(c):
-            cols = slice(c * CHUNK, (c + 1) * CHUNK)
+            start, width = CHUNKS[c]
+            cols = slice(start, start + width)
             nc.vector.quantize_mx(
                 out=out_codes[:, cols].bitcast(FP8X4),
                 scales=out_scales[:, cols],

@@ -31,17 +31,25 @@ def tile_picked_decode2_relu_po_kernel(
     nc = tc.nc
     with ExitStack() as ctx:
         keep = ctx.enter_context(tc.tile_pool(name="keep", bufs=1))
-        words = ctx.enter_context(tc.tile_pool(name="words", bufs=1))
+        shared = ctx.enter_context(tc.tile_pool(name="shared", bufs=1))
         psum = ctx.enter_context(tc.psum_pool(name="psum", bufs=1))
 
         def held(shape, dtype, name, tag=None):
             return keep.tile(shape, dtype, name=name, tag=tag or name, align_bytes=64)
 
+        def placed(shape, dtype, name, offset):
+            return shared.tile(shape, dtype, name=name, align_bytes=64, offset=offset)
+
+        plane_bytes = 4 * U
+        w1_at = 0
+        grouped_at = w1_at + 4 * plane_bytes
+        xw_at = grouped_at + 2 * plane_bytes
+
         offs_sb = held([P, S // LIST], U16, "offs_sb")
         rg_sb = held([P, S // LIST], U16, "rg_sb")
         xs_table = held([P, T], U8, "xs_table")
-        xw_table = words.tile([P, T], I32, name="xw_table", align_bytes=64, offset=0)
-        w1_raw = [held([P, PACK, HALF], F32, "w1_raw%d" % i) for i in range(2)]
+        xw_table = placed([P, T], I32, "xw_table", xw_at)
+        w1_raw = [placed([P, PACK, HALF], F32, "w1_raw%d" % i, w1_at + 2 * i * plane_bytes) for i in range(2)]
         b1_sb = held([P, PACK], F32, "b1_sb")
         scl_sb = [held([P, U], F32, "scl_sb%d" % t) for t in range(2)]
 
@@ -58,12 +66,17 @@ def tile_picked_decode2_relu_po_kernel(
         nc.sync.dma_start(scl_sb[0][:], scl_rows[0])
         nc.sync.dma_start(offs_sb[:], offs)
         nc.sync.dma_start(b1_sb[:], b1.rearrange("(p t) o -> p (t o)", t=PACK))
-        nc.sync.dma_start(w1_raw[0][:], w1_rows[:, :, :HALF])
         for r in range(2):
             nc.sync.dma_start(xs_table[r:P:LIST, :].bitcast(I32), xs_rows[r])
+        nc.sync.dma_start(w1_raw[0][:], w1_rows[:, :, :HALF])
         nc.sync.dma_start(scl_sb[1][:], scl_rows[1])
         nc.sync.dma_start(w1_raw[1][:], w1_rows[:, :, HALF:])
         nc.sync.dma_start(xw_table[:], x_words[0].rearrange("p n t -> p (n t)").bitcast(I32))
+
+        w2s_raw = held([P, N], U8, "w2s_raw")
+        nc.gpsimd.memset(w2s_raw[:].bitcast(I32), 0)
+        for b in range(PACK):
+            nc.gpsimd.dma_start(w2s_raw[b:P:32, :].bitcast(I32), w2s_rows[b])
 
         def list_slice(lists, start, count):
             return lists[:, start // LIST : (start + count) // LIST]
@@ -80,10 +93,6 @@ def tile_picked_decode2_relu_po_kernel(
                 )
 
         pick_scl(0)
-        w2s_raw = held([P, N], U8, "w2s_raw", "scl_sb0")
-        nc.vector.memset(w2s_raw[:].bitcast(I32), 0)
-        for b in range(PACK):
-            nc.sync.dma_start(w2s_raw[b:P:32, :].bitcast(I32), w2s_rows[b])
 
         xs_picked = held([P, S], U8, "xs_picked")
         nc.vector.tensor_copy(xs_picked[:], xs_table[:].indirect(offs_sb[:]))
@@ -95,18 +104,18 @@ def tile_picked_decode2_relu_po_kernel(
             )
         pick_scl(1)
 
-        w1_grouped = held([P, PACK, P, PACK], BF16, "w1_grouped")
+        w1_grouped = placed([P, PACK, P, PACK], BF16, "w1_grouped", grouped_at)
         for i in range(2):
             m_cols = slice(i * HALF // PACK, (i + 1) * HALF // PACK)
             nc.scalar.copy(
                 w1_grouped[:, :, m_cols, :].rearrange("p t m j -> p m j t"),
                 w1_raw[i][:].rearrange("p j (m t) -> p m j t", t=PACK),
             )
-        for t, tag in ((2, "w1_raw0"), (3, "scl_sb1")):
-            scl_sb.append(held([P, U], F32, "scl_sb%d" % t, tag))
-            nc.sync.dma_start(scl_sb[t][:], scl_rows[t])
-        w2w_raw = held([P, N], I32, "w2w_raw", "w1_raw1")
+        w2w_raw = placed([P, N], I32, "w2w_raw", w1_at)
         nc.sync.dma_start(w2w_raw[:], w2_words[0].rearrange("p n t -> p (n t)").bitcast(I32))
+        for t in (2, 3):
+            scl_sb.append(placed([P, U], F32, "scl_sb%d" % t, w1_at + (t - 1) * plane_bytes))
+            nc.sync.dma_start(scl_sb[t][:], scl_rows[t])
         w1_codes = held([P, H], U32, "w1_codes")
         w1_scales = held([P, H], U8, "w1_scales")
         nc.vector.quantize_mx(
@@ -115,33 +124,26 @@ def tile_picked_decode2_relu_po_kernel(
             in_=w1_grouped[:].rearrange("p t m j -> p (t m j)"),
         )
 
-        xw_picked = held([P, S], U32, "xw_picked")
+        xw_picked = [held([P, HALF], U32, "xw_picked%d" % i) for i in range(2)]
         for i in range(2):
             nc.vector.tensor_copy(
-                xw_picked[:, i * HALF : (i + 1) * HALF], xw_table[:].bitcast(U32).indirect(list_slice(offs_sb, i * HALF, HALF))
+                xw_picked[i][:], xw_table[:].bitcast(U32).indirect(list_slice(offs_sb, i * HALF, HALF))
             )
 
         shf_sb = []
-
-        def load_shf(t, tag):
-            shf_sb.append(held([P, U], F32, "shf_sb%d" % t, tag))
-            nc.sync.dma_start(shf_sb[t][:], shf_rows[t])
-
-        for t, tag in enumerate(["w1_grouped", "xs_picked"]):
-            load_shf(t, tag)
-        for t in (2, 3):
-            shf_sb.append(words.tile([P, U], F32, name="shf_sb%d" % t, align_bytes=64, offset=4 * U * (t - 2)))
+        for t in range(PACK):
+            shf_sb.append(placed([P, U], F32, "shf_sb%d" % t, grouped_at + (t - 1) * plane_bytes))
             nc.sync.dma_start(shf_sb[t][:], shf_rows[t])
 
         w2_codes = held([P, N], I32, "w2_codes")
-        w2_plane = held([P, N], U8, "w2_plane")
-        nc.vector.tensor_copy(
-            w2_plane[:].rearrange("p (t a i) -> p a t i", t=PACK, i=16),
-            w2s_raw[:].rearrange("p (a i t) -> p a t i", t=PACK, i=16),
-        )
+        w2_plane = placed([P, N], U8, "w2_plane", xw_at + plane_bytes)
         nc.vector.tensor_copy(
             w2_codes[:].rearrange("p (t a i) -> p a t i", t=PACK, i=4),
             w2w_raw[:].rearrange("p (a i t) -> p a t i", t=PACK, i=4),
+        )
+        nc.vector.tensor_copy(
+            w2_plane[:].rearrange("p (t a i) -> p a t i", t=PACK, i=16),
+            w2s_raw[:].rearrange("p (a i t) -> p a t i", t=PACK, i=16),
         )
 
         h_banks = [psum.tile([P, S], F32, name="h_bank%d" % t) for t in range(PACK)]
@@ -156,7 +158,7 @@ def tile_picked_decode2_relu_po_kernel(
                     out=h_banks[t][:, cols],
                     lhsT=w1_codes[:, t * P : (t + 1) * P].bitcast(FP8X4),
                     lhsT_scale=w1_scales[:, t * P : (t + 1) * P],
-                    rhs=xw_picked[:, cols].bitcast(FP8X4),
+                    rhs=xw_picked[start // HALF][:, start % HALF : start % HALF + width].bitcast(FP8X4),
                     rhs_scale=xs_plane[:, cols],
                     start=True,
                     stop=True,

@@ -49,7 +49,7 @@ def tile_picked_decode2_relu_po_kernel(
         rg_sb = held([P, S // LIST], U16, "rg_sb")
         xs_table = held([P, T], U8, "xs_table")
         xw_table = placed([P, T], I32, "xw_table", xw_at)
-        w1_raw = [placed([P, PACK, HALF], F32, "w1_raw%d" % i, w1_at + 2 * i * plane_bytes) for i in range(2)]
+        w1_raw = placed([P, PACK, H], F32, "w1_raw", w1_at)
         b1_sb = held([P, PACK], F32, "b1_sb")
         scl_sb = [held([P, U], F32, "scl_sb%d" % t) for t in range(2)]
 
@@ -68,9 +68,8 @@ def tile_picked_decode2_relu_po_kernel(
         nc.sync.dma_start(b1_sb[:], b1.rearrange("(p t) o -> p (t o)", t=PACK))
         for r in range(2):
             nc.sync.dma_start(xs_table[r:P:LIST, :].bitcast(I32), xs_rows[r])
-        nc.sync.dma_start(w1_raw[0][:], w1_rows[:, :, :HALF])
+        nc.sync.dma_start(w1_raw[:], w1_rows)
         nc.sync.dma_start(scl_sb[1][:], scl_rows[1])
-        nc.sync.dma_start(w1_raw[1][:], w1_rows[:, :, HALF:])
         nc.sync.dma_start(xw_table[:], x_words[0].rearrange("p n t -> p (n t)").bitcast(I32))
 
         w2s_raw = held([P, N], U8, "w2s_raw")
@@ -104,27 +103,28 @@ def tile_picked_decode2_relu_po_kernel(
             )
         pick_scl(1)
 
-        w1_grouped = placed([P, PACK, P, PACK], BF16, "w1_grouped", grouped_at)
-        for i in range(2):
-            m_cols = slice(i * HALF // PACK, (i + 1) * HALF // PACK)
-            nc.scalar.copy(
-                w1_grouped[:, :, m_cols, :].rearrange("p t m j -> p m j t"),
-                w1_raw[i][:].rearrange("p j (m t) -> p m j t", t=PACK),
-            )
-        w2w_raw = placed([P, N], I32, "w2w_raw", w1_at)
+        w2w_raw = held([P, N], I32, "w2w_raw", "scl_sb0")
         nc.sync.dma_start(w2w_raw[:], w2_words[0].rearrange("p n t -> p (n t)").bitcast(I32))
-        for t in (2, 3):
-            scl_sb.append(placed([P, U], F32, "scl_sb%d" % t, w1_at + (t - 1) * plane_bytes))
-            nc.sync.dma_start(scl_sb[t][:], scl_rows[t])
+        scl_sb.append(held([P, U], F32, "scl_sb2", "scl_sb1"))
+        nc.sync.dma_start(scl_sb[2][:], scl_rows[2])
+
         w1_codes = held([P, H], U32, "w1_codes")
         w1_scales = held([P, H], U8, "w1_scales")
-        nc.vector.quantize_mx(
-            out=w1_codes[:].bitcast(FP8X4),
-            scales=w1_scales[:],
-            in_=w1_grouped[:].rearrange("p t m j -> p (t m j)"),
-        )
+        for i in range(2):
+            w1_grouped = placed([P, 2, P, PACK], BF16, "w1_grouped%d" % i, grouped_at + i * plane_bytes)
+            nc.scalar.copy(
+                w1_grouped[:].rearrange("p t m j -> p m j t"),
+                w1_raw[:].rearrange("p j (m t) -> p m j t", t=PACK)[:, :, :, 2 * i : 2 * i + 2],
+            )
+            nc.vector.quantize_mx(
+                out=w1_codes[:, i * HALF : (i + 1) * HALF].bitcast(FP8X4),
+                scales=w1_scales[:, i * HALF : (i + 1) * HALF],
+                in_=w1_grouped[:].rearrange("p t m j -> p (t m j)"),
+            )
+        scl_sb.append(placed([P, U], F32, "scl_sb3", w1_at))
+        nc.sync.dma_start(scl_sb[3][:], scl_rows[3])
 
-        xw_picked = [held([P, HALF], U32, "xw_picked%d" % i) for i in range(2)]
+        xw_picked = [placed([P, HALF], U32, "xw_picked%d" % i, grouped_at + plane_bytes + 4 * HALF * i) for i in range(2)]
         for i in range(2):
             nc.vector.tensor_copy(
                 xw_picked[i][:], xw_table[:].bitcast(U32).indirect(list_slice(offs_sb, i * HALF, HALF))
@@ -132,7 +132,7 @@ def tile_picked_decode2_relu_po_kernel(
 
         shf_sb = []
         for t in range(PACK):
-            shf_sb.append(placed([P, U], F32, "shf_sb%d" % t, grouped_at + (t - 1) * plane_bytes))
+            shf_sb.append(placed([P, U], F32, "shf_sb%d" % t, w1_at + (t + 1) * plane_bytes if t < 3 else xw_at))
             nc.sync.dma_start(shf_sb[t][:], shf_rows[t])
 
         w2_codes = held([P, N], I32, "w2_codes")

@@ -18,11 +18,19 @@ RELU = mybir.ActivationFunctionType.Relu
 
 P = 128
 PACK = 4
-HALF = 256
-HIDDEN_CHUNKS = ((0, 128), (128, 128), (256, 256))
-CHUNKS = ((0, 128), (128, 128), (256, 128), (384, 128))
-BANK = 512
+QUADRANT = 32
 LIST = 16
+HALF = 256
+HIDDEN_STEPS = ((0, 128), (128, 128), (256, 256))
+WIDTH = 128
+CHUNKS = S // WIDTH
+CLEARED_BY_VECTOR = 3 * T // 4
+
+PLANE = 4 * U
+W1_AT = 0
+ROUNDED_W1_AT = W1_AT + 4 * PLANE
+WORDS_AT = ROUNDED_W1_AT + 2 * PLANE
+LAST_ROWS_AT = WORDS_AT + 4 * PLANE + PLANE // 2
 
 
 def tile_picked_decode2_relu_po_kernel(
@@ -40,21 +48,16 @@ def tile_picked_decode2_relu_po_kernel(
         def placed(shape, dtype, name, offset):
             return shared.tile(shape, dtype, name=name, align_bytes=64, offset=offset)
 
-        plane_bytes = 4 * U
-        w1_at = 0
-        grouped_at = w1_at + 4 * plane_bytes
-        xw_at = grouped_at + 2 * plane_bytes
-
         offs_sb = held([P, S // LIST], U16, "offs_sb")
         rg_sb = held([P, S // LIST], U16, "rg_sb")
         xs_table = held([P, T], U8, "xs_table")
-        xw_table = placed([P, T], I32, "xw_table", xw_at)
-        w1_raw = placed([P, PACK, H], F32, "w1_raw", w1_at)
+        xw_table = placed([P, T], I32, "xw_table", WORDS_AT)
+        w1_raw = placed([P, PACK, H], F32, "w1_raw", W1_AT)
         b1_sb = held([P, PACK], F32, "b1_sb")
         scl_sb = [held([P, U], F32, "scl_sb%d" % t) for t in range(2)]
 
-        nc.vector.memset(xs_table[:, : 3 * T // 4].bitcast(I32), 0)
-        nc.gpsimd.memset(xs_table[:, 3 * T // 4 :].bitcast(I32), 0)
+        nc.vector.memset(xs_table[:, :CLEARED_BY_VECTOR].bitcast(I32), 0)
+        nc.gpsimd.memset(xs_table[:, CLEARED_BY_VECTOR:].bitcast(I32), 0)
 
         xs_rows = x_scales[0].bitcast(I32).rearrange("(m r) c -> r m c", r=2)
         w2s_rows = w2_scales[0].bitcast(I32).rearrange("(q b) c -> b q c", b=PACK)
@@ -75,23 +78,24 @@ def tile_picked_decode2_relu_po_kernel(
         w2s_raw = held([P, N], U8, "w2s_raw")
         nc.gpsimd.memset(w2s_raw[:].bitcast(I32), 0)
         for b in range(PACK):
-            nc.gpsimd.dma_start(w2s_raw[b:P:32, :].bitcast(I32), w2s_rows[b])
+            nc.gpsimd.dma_start(w2s_raw[b:P:QUADRANT, :].bitcast(I32), w2s_rows[b])
 
         def list_slice(lists, start, count):
             return lists[:, start // LIST : (start + count) // LIST]
 
         scl_picked = {}
 
-        def pick_scl(t, halves=(0, 1), tag=None):
-            for i in halves:
-                if (t // 2, i) not in scl_picked:
-                    scl_picked[t // 2, i] = held([P, 2, HALF], F32, "scl_picked%d_%d" % (t // 2, i), tag)
-                nc.vector.tensor_copy(
-                    scl_picked[t // 2, i][:, t % 2, :],
-                    scl_sb[t][:].indirect(list_slice(rg_sb, i * HALF, HALF)),
-                )
+        def pick_scl(t, half, tag=None):
+            pair = t // 2
+            if (pair, half) not in scl_picked:
+                scl_picked[pair, half] = held([P, 2, HALF], F32, "scl_picked%d_%d" % (pair, half), tag)
+            nc.vector.tensor_copy(
+                scl_picked[pair, half][:, t % 2, :],
+                scl_sb[t][:].indirect(list_slice(rg_sb, half * HALF, HALF)),
+            )
 
-        pick_scl(0)
+        for half in range(2):
+            pick_scl(0, half)
 
         xs_picked = held([P, S], U8, "xs_picked")
         nc.vector.tensor_copy(xs_picked[:], xs_table[:].indirect(offs_sb[:]))
@@ -99,9 +103,10 @@ def tile_picked_decode2_relu_po_kernel(
         nc.vector.tensor_copy(xs_plane[:].bitcast(I32), xs_picked[:].bitcast(I32))
         for r in range(2):
             nc.sync.dma_start(
-                xs_plane[2 + r : P : 32, :].bitcast(I32), xs_picked[LIST + r : P : 32, :].bitcast(I32)
+                xs_plane[2 + r : P : QUADRANT, :].bitcast(I32), xs_picked[LIST + r : P : QUADRANT, :].bitcast(I32)
             )
-        pick_scl(1)
+        for half in range(2):
+            pick_scl(1, half)
 
         w2w_raw = held([P, N], I32, "w2w_raw", "scl_sb0")
         nc.sync.dma_start(w2w_raw[:], w2_words[0].rearrange("p n t -> p (n t)").bitcast(I32))
@@ -110,33 +115,38 @@ def tile_picked_decode2_relu_po_kernel(
 
         w1_codes = held([P, H], U32, "w1_codes")
         w1_scales = held([P, H], U8, "w1_scales")
-        for i in range(2):
-            w1_grouped = placed([P, 2, P, PACK], BF16, "w1_grouped%d" % i, grouped_at + i * plane_bytes)
+        for pair in range(2):
+            w1_grouped = placed([P, 2, P, PACK], BF16, "w1_grouped%d" % pair, ROUNDED_W1_AT + pair * PLANE)
+            code_cols = slice(2 * pair * P, 2 * (pair + 1) * P)
             nc.scalar.copy(
                 w1_grouped[:].rearrange("p t m j -> p m j t"),
-                w1_raw[:].rearrange("p j (m t) -> p m j t", t=PACK)[:, :, :, 2 * i : 2 * i + 2],
+                w1_raw[:].rearrange("p j (m t) -> p m j t", t=PACK)[:, :, :, 2 * pair : 2 * pair + 2],
             )
             nc.vector.quantize_mx(
-                out=w1_codes[:, i * HALF : (i + 1) * HALF].bitcast(FP8X4),
-                scales=w1_scales[:, i * HALF : (i + 1) * HALF],
+                out=w1_codes[:, code_cols].bitcast(FP8X4),
+                scales=w1_scales[:, code_cols],
                 in_=w1_grouped[:].rearrange("p t m j -> p (t m j)"),
             )
-        scl_sb.append(placed([P, U], F32, "scl_sb3", w1_at))
+        scl_sb.append(placed([P, U], F32, "scl_sb3", W1_AT))
         nc.sync.dma_start(scl_sb[3][:], scl_rows[3])
 
-        xw_picked = [placed([P, HALF], U32, "xw_picked%d" % i, grouped_at + plane_bytes + 4 * HALF * i) for i in range(2)]
-        for i in range(2):
+        xw_picked = [
+            placed([P, HALF], U32, "xw_picked%d" % half, ROUNDED_W1_AT + PLANE + half * PLANE // 2)
+            for half in range(2)
+        ]
+        for half in range(2):
             nc.vector.tensor_copy(
-                xw_picked[i][:], xw_table[:].bitcast(U32).indirect(list_slice(offs_sb, i * HALF, HALF))
+                xw_picked[half][:], xw_table[:].bitcast(U32).indirect(list_slice(offs_sb, half * HALF, HALF))
             )
 
         shf_sb = []
         for t in range(PACK):
-            shf_sb.append(placed([P, U], F32, "shf_sb%d" % t, w1_at + (t + 1) * plane_bytes if t < 3 else xw_at))
+            shf_at = W1_AT + (t + 1) * PLANE if t + 1 < PACK else WORDS_AT
+            shf_sb.append(placed([P, U], F32, "shf_sb%d" % t, shf_at))
             nc.sync.dma_start(shf_sb[t][:], shf_rows[t])
 
         w2_codes = held([P, N], I32, "w2_codes")
-        w2_plane = placed([P, N], U8, "w2_plane", xw_at + plane_bytes)
+        w2_plane = placed([P, N], U8, "w2_plane", WORDS_AT + PLANE)
         nc.vector.tensor_copy(
             w2_codes[:].rearrange("p (t a i) -> p a t i", t=PACK, i=4),
             w2w_raw[:].rearrange("p (a i t) -> p a t i", t=PACK, i=4),
@@ -146,104 +156,106 @@ def tile_picked_decode2_relu_po_kernel(
             w2s_raw[:].rearrange("p (a i t) -> p a t i", t=PACK, i=16),
         )
 
+        def interleave(copy, grouped, planes):
+            copy(
+                grouped[:].rearrange("p (c i) t -> p c t i", i=4),
+                planes[:].rearrange("p t (c i) -> p c t i", i=4),
+            )
+
         h_banks = [psum.tile([P, S], F32, name="h_bank%d" % t) for t in range(PACK)]
         h_codes = held([P, S], U32, "h_codes")
         h_scales = held([P, S], U8, "h_scales")
 
         def first_layer(start, width):
             cols = slice(start, start + width)
-            h_rows = held([P, PACK, width], BF16, "h_rows%d" % start)
+            half, inner = divmod(start, HALF)
+            if start + width == S:
+                h_rows = placed([P, PACK, width], BF16, "h_rows%d" % start, LAST_ROWS_AT)
+            else:
+                h_rows = held([P, PACK, width], BF16, "h_rows%d" % start)
             for t in range(PACK):
                 nc.tensor.matmul_mx(
                     out=h_banks[t][:, cols],
                     lhsT=w1_codes[:, t * P : (t + 1) * P].bitcast(FP8X4),
                     lhsT_scale=w1_scales[:, t * P : (t + 1) * P],
-                    rhs=xw_picked[start // HALF][:, start % HALF : start % HALF + width].bitcast(FP8X4),
+                    rhs=xw_picked[half][:, inner : inner + width].bitcast(FP8X4),
                     rhs_scale=xs_plane[:, cols],
                     start=True,
                     stop=True,
                 )
                 nc.scalar.activation(h_rows[:, t, :], h_banks[t][:, cols], RELU, bias=b1_sb[:, t : t + 1])
             h_grouped = held([P, width, PACK], BF16, "h_grouped%d" % start)
-            nc.scalar.copy(
-                h_grouped[:].rearrange("p (c i) t -> p c t i", i=4),
-                h_rows[:].rearrange("p t (c i) -> p c t i", i=4),
-            )
+            interleave(nc.scalar.copy, h_grouped, h_rows)
             nc.vector.quantize_mx(
                 out=h_codes[:, cols].bitcast(FP8X4),
                 scales=h_scales[:, cols],
                 in_=h_grouped[:].rearrange("p c t -> p (c t)"),
             )
 
-        pick_scl(2, (0,))
-        pick_scl(3, (0,))
-        first_layer(*HIDDEN_CHUNKS[0])
-        pick_scl(2, (1,), "h_grouped0")
-        first_layer(*HIDDEN_CHUNKS[1])
-        pick_scl(3, (1,))
-        first_layer(*HIDDEN_CHUNKS[2])
+        pick_scl(2, 0)
+        pick_scl(3, 0)
+        first_layer(*HIDDEN_STEPS[0])
+        pick_scl(2, 1, "h_rows0")
+        first_layer(*HIDDEN_STEPS[1])
+        pick_scl(3, 1)
+        first_layer(*HIDDEN_STEPS[2])
 
         out_codes = held([P, S], U32, "out_codes")
         out_scales = held([P, S], U8, "out_scales")
         out_rows = out_0.rearrange("(p t) j -> p t j", t=PACK)
         out_words = out_1[0].rearrange("p n t -> p (n t)").bitcast(I32)
-        out_planes = out_2[0].bitcast(I32).rearrange("(q b) c -> b q c", b=PACK)
-        grouped = []
-        chunks = len(CHUNKS)
+        out_scale_rows = out_2[0].bitcast(I32).rearrange("(q b) c -> b q c", b=PACK)
+        rounded = []
 
         def second_layer(c):
-            start, width = CHUNKS[c]
-            cols = slice(start, start + width)
-            per_bank = BANK // width
-            scaled = held([P, PACK, width], F32, "scaled%d" % c)
-            for first in range(0, PACK, per_bank):
-                bank = psum.tile([P, per_bank, width], F32, name="y_bank%d_%d" % (c, first))
-                for t in range(first, first + per_bank):
-                    nc.tensor.matmul_mx(
-                        out=bank[:, t - first, :],
-                        lhsT=w2_codes[:, t * P : (t + 1) * P].bitcast(FP8X4),
-                        lhsT_scale=w2_plane[:, t * P : (t + 1) * P],
-                        rhs=h_codes[:, cols].bitcast(FP8X4),
-                        rhs_scale=h_scales[:, cols],
-                        start=True,
-                        stop=True,
-                    )
-                for pair in range(0, per_bank, 2):
-                    planes = slice(first + pair, first + pair + 2)
-                    half, inner = divmod(start, HALF)
-                    picked = scl_picked[(first + pair) // 2, half]
-                    nc.vector.tensor_tensor(
-                        scaled[:, planes, :], bank[:, pair : pair + 2, :], picked[:, :, inner : inner + width], MULT
-                    )
-            result = held([P, PACK, width], F32, "result%d" % c, "h_grouped256" if c == 1 else None)
+            start = c * WIDTH
+            cols = slice(start, start + WIDTH)
+            half, inner = divmod(start, HALF)
+            scaled = held([P, PACK, WIDTH], F32, "scaled%d" % c)
+            bank = psum.tile([P, PACK, WIDTH], F32, name="y_bank%d" % c)
+            for t in range(PACK):
+                nc.tensor.matmul_mx(
+                    out=bank[:, t, :],
+                    lhsT=w2_codes[:, t * P : (t + 1) * P].bitcast(FP8X4),
+                    lhsT_scale=w2_plane[:, t * P : (t + 1) * P],
+                    rhs=h_codes[:, cols].bitcast(FP8X4),
+                    rhs_scale=h_scales[:, cols],
+                    start=True,
+                    stop=True,
+                )
+            for pair in range(2):
+                planes = slice(2 * pair, 2 * pair + 2)
+                picked = scl_picked[pair, half][:, :, inner : inner + WIDTH]
+                nc.vector.tensor_tensor(scaled[:, planes, :], bank[:, planes, :], picked, MULT)
+            if c == 1:
+                result = placed([P, PACK, WIDTH], F32, "result1", LAST_ROWS_AT - PLANE // 2)
+            else:
+                result = held([P, PACK, WIDTH], F32, "result%d" % c)
             for t in range(PACK):
                 nc.vector.tensor_tensor(
-                    result[:, t, :], shf_sb[t][:].indirect(list_slice(rg_sb, start, width)), scaled[:, t, :], ADD
+                    result[:, t, :], shf_sb[t][:].indirect(list_slice(rg_sb, start, WIDTH)), scaled[:, t, :], ADD
                 )
             nc.sync.dma_start(out_rows[:, :, cols], result[:])
-            rounded = held([P, width, PACK], BF16, "rounded%d" % c, "h_rows256" if c == 0 else None)
-            copy = nc.vector.tensor_copy if c == chunks - 1 else nc.scalar.copy
-            copy(
-                rounded[:].rearrange("p (c i) t -> p c t i", i=4),
-                result[:].rearrange("p t (c i) -> p c t i", i=4),
-            )
-            grouped.append(rounded)
+            if c == 0:
+                rounded.append(placed([P, WIDTH, PACK], BF16, "rounded0", LAST_ROWS_AT + PLANE // 2))
+            else:
+                rounded.append(held([P, WIDTH, PACK], BF16, "rounded%d" % c))
+            interleave(nc.vector.tensor_copy if c == CHUNKS - 1 else nc.scalar.copy, rounded[c], result)
 
         def quantise_result(c):
-            start, width = CHUNKS[c]
-            cols = slice(start, start + width)
+            cols = slice(c * WIDTH, (c + 1) * WIDTH)
             nc.vector.quantize_mx(
                 out=out_codes[:, cols].bitcast(FP8X4),
                 scales=out_scales[:, cols],
-                in_=grouped[c][:].rearrange("p c t -> p (c t)"),
+                in_=rounded[c][:].rearrange("p c t -> p (c t)"),
             )
             nc.sync.dma_start(out_words[:, cols], out_codes[:, cols].bitcast(I32))
 
-        for c in range(chunks):
+        for c in range(CHUNKS):
             second_layer(c)
             if c > 0:
                 quantise_result(c - 1)
-        quantise_result(chunks - 1)
+        quantise_result(CHUNKS - 1)
         for b in range(PACK):
             queue = nc.scalar if b % 2 else nc.sync
-            queue.dma_start(out_planes[b], out_scales[b:P:32, :].bitcast(I32))
+            queue.dma_start(out_scale_rows[b], out_scales[b:P:QUADRANT, :].bitcast(I32))

@@ -19,6 +19,7 @@ RELU = mybir.ActivationFunctionType.Relu
 P = 128
 PACK = 4
 QUADRANT = 32
+BLOCK = 8
 LIST = 16
 HALF = 256
 HIDDEN_STEPS = ((0, 128), (128, 128), (256, 256))
@@ -59,7 +60,10 @@ def tile_picked_decode2_relu_po_kernel(
         nc.vector.memset(xs_table[:, :CLEARED_BY_VECTOR].bitcast(I32), 0)
         nc.gpsimd.memset(xs_table[:, CLEARED_BY_VECTOR:].bitcast(I32), 0)
 
-        xs_rows = x_scales[0].bitcast(I32).rearrange("(m r) c -> r m c", r=2)
+        xs_plane = held([P, S], U8, "xs_plane")
+        nc.vector.memset(xs_plane[:].bitcast(I32), 0)
+
+        xs_rows = x_scales[0].bitcast(I32)
         w2s_rows = w2_scales[0].bitcast(I32).rearrange("(q b) c -> b q c", b=PACK)
         w1_rows = w1.rearrange("(p j) c -> p j c", j=PACK)
         scl_rows = scl.rearrange("(p t) u -> t p u", t=PACK)
@@ -69,8 +73,7 @@ def tile_picked_decode2_relu_po_kernel(
         nc.sync.dma_start(scl_sb[0][:], scl_rows[0])
         nc.sync.dma_start(offs_sb[:], offs)
         nc.sync.dma_start(b1_sb[:], b1.rearrange("(p t) o -> p (t o)", t=PACK))
-        for r in range(2):
-            nc.sync.dma_start(xs_table[r:P:LIST, :].bitcast(I32), xs_rows[r])
+        nc.sync.dma_start(xs_table[0:P:BLOCK, :].bitcast(I32), xs_rows)
         nc.sync.dma_start(w1_raw[:], w1_rows)
         nc.sync.dma_start(scl_sb[1][:], scl_rows[1])
         nc.sync.dma_start(xw_table[:], x_words[0].rearrange("p n t -> p (n t)").bitcast(I32))
@@ -99,11 +102,9 @@ def tile_picked_decode2_relu_po_kernel(
 
         xs_picked = held([P, S], U8, "xs_picked")
         nc.vector.tensor_copy(xs_picked[:], xs_table[:].indirect(offs_sb[:]))
-        xs_plane = held([P, S], U8, "xs_plane")
-        nc.vector.tensor_copy(xs_plane[:].bitcast(I32), xs_picked[:].bitcast(I32))
-        for r in range(2):
+        for b in range(PACK):
             nc.sync.dma_start(
-                xs_plane[2 + r : P : QUADRANT, :].bitcast(I32), xs_picked[LIST + r : P : QUADRANT, :].bitcast(I32)
+                xs_plane[b:P:QUADRANT, :].bitcast(I32), xs_picked[BLOCK * b : P : QUADRANT, :].bitcast(I32)
             )
         for half in range(2):
             pick_scl(1, half)
@@ -146,7 +147,7 @@ def tile_picked_decode2_relu_po_kernel(
             nc.sync.dma_start(shf_sb[t][:], shf_rows[t])
 
         w2_codes = held([P, N], I32, "w2_codes")
-        w2_plane = placed([P, N], U8, "w2_plane", WORDS_AT + PLANE)
+        w2_plane = held([P, N], U8, "w2_plane", "xs_picked")
         nc.vector.tensor_copy(
             w2_codes[:].rearrange("p (t a i) -> p a t i", t=PACK, i=4),
             w2w_raw[:].rearrange("p (a i t) -> p a t i", t=PACK, i=4),
@@ -207,11 +208,12 @@ def tile_picked_decode2_relu_po_kernel(
         out_scale_rows = out_2[0].bitcast(I32).rearrange("(q b) c -> b q c", b=PACK)
         rounded = []
 
+        scaled = []
+
         def second_layer(c):
-            start = c * WIDTH
-            cols = slice(start, start + WIDTH)
-            half, inner = divmod(start, HALF)
-            scaled = held([P, PACK, WIDTH], F32, "scaled%d" % c)
+            cols = slice(c * WIDTH, (c + 1) * WIDTH)
+            half, inner = divmod(c * WIDTH, HALF)
+            scaled.append(held([P, PACK, WIDTH], F32, "scaled%d" % c))
             bank = psum.tile([P, PACK, WIDTH], F32, name="y_bank%d" % c)
             for t in range(PACK):
                 nc.tensor.matmul_mx(
@@ -226,14 +228,18 @@ def tile_picked_decode2_relu_po_kernel(
             for pair in range(2):
                 planes = slice(2 * pair, 2 * pair + 2)
                 picked = scl_picked[pair, half][:, :, inner : inner + WIDTH]
-                nc.vector.tensor_tensor(scaled[:, planes, :], bank[:, planes, :], picked, MULT)
+                nc.vector.tensor_tensor(scaled[c][:, planes, :], bank[:, planes, :], picked, MULT)
+
+        def shift(c):
+            start = c * WIDTH
+            cols = slice(start, start + WIDTH)
             if c == 1:
                 result = placed([P, PACK, WIDTH], F32, "result1", LAST_ROWS_AT - PLANE // 2)
             else:
                 result = held([P, PACK, WIDTH], F32, "result%d" % c)
             for t in range(PACK):
                 nc.vector.tensor_tensor(
-                    result[:, t, :], shf_sb[t][:].indirect(list_slice(rg_sb, start, WIDTH)), scaled[:, t, :], ADD
+                    result[:, t, :], shf_sb[t][:].indirect(list_slice(rg_sb, start, WIDTH)), scaled[c][:, t, :], ADD
                 )
             nc.sync.dma_start(out_rows[:, :, cols], result[:])
             if c == 0:
@@ -251,10 +257,16 @@ def tile_picked_decode2_relu_po_kernel(
             )
             nc.sync.dma_start(out_words[:, cols], out_codes[:, cols].bitcast(I32))
 
-        for c in range(CHUNKS):
+        first_chunks, last_chunks = range(CHUNKS // 2), range(CHUNKS // 2, CHUNKS)
+        for c in first_chunks:
             second_layer(c)
-            if c > 0:
-                quantise_result(c - 1)
+            shift(c)
+        quantise_result(0)
+        for c in last_chunks:
+            second_layer(c)
+        for c in last_chunks:
+            shift(c)
+            quantise_result(c - 1)
         quantise_result(CHUNKS - 1)
         for b in range(PACK):
             queue = nc.scalar if b % 2 else nc.sync

@@ -72,11 +72,11 @@ def tile_picked_decode2_relu_po_kernel(
         nc.sync.dma_start(rg_sb[:], rg)
         nc.sync.dma_start(scl_sb[0][:], scl_rows[0])
         nc.sync.dma_start(offs_sb[:], offs)
-        nc.sync.dma_start(b1_sb[:], b1.rearrange("(p t) o -> p (t o)", t=PACK))
         nc.sync.dma_start(xs_table[0:P:BLOCK, :].bitcast(I32), xs_rows)
         nc.sync.dma_start(w1_raw[:], w1_rows)
         nc.sync.dma_start(scl_sb[1][:], scl_rows[1])
         nc.sync.dma_start(xw_table[:], x_words[0].rearrange("p n t -> p (n t)").bitcast(I32))
+        nc.sync.dma_start(b1_sb[:], b1.rearrange("(p t) o -> p (t o)", t=PACK))
 
         w2s_raw = held([P, N], U8, "w2s_raw")
         nc.gpsimd.memset(w2s_raw[:].bitcast(I32), 0)
@@ -163,30 +163,39 @@ def tile_picked_decode2_relu_po_kernel(
                 planes[:].rearrange("p t (c i) -> p c t i", i=4),
             )
 
-        h_banks = [psum.tile([P, S], F32, name="h_bank%d" % t) for t in range(PACK)]
         h_codes = held([P, S], U32, "h_codes")
         h_scales = held([P, S], U8, "h_scales")
 
-        def first_layer(start, width):
-            cols = slice(start, start + width)
-            half, inner = divmod(start, HALF)
-            if start + width == S:
-                h_rows = placed([P, PACK, width], BF16, "h_rows%d" % start, LAST_ROWS_AT)
-            else:
-                h_rows = held([P, PACK, width], BF16, "h_rows%d" % start)
-            for t in range(PACK):
+        sums = {}
+
+        def first_products(tag, items):
+            bank = psum.tile([P, len(items), WIDTH], F32, name="sums%d_%d" % items[0], tag=tag)
+            for i, (c, t) in enumerate(items):
+                half, inner = divmod(c * WIDTH, HALF)
                 nc.tensor.matmul_mx(
-                    out=h_banks[t][:, cols],
+                    out=bank[:, i, :],
                     lhsT=w1_codes[:, t * P : (t + 1) * P].bitcast(FP8X4),
                     lhsT_scale=w1_scales[:, t * P : (t + 1) * P],
-                    rhs=xw_picked[half][:, inner : inner + width].bitcast(FP8X4),
-                    rhs_scale=xs_plane[:, cols],
+                    rhs=xw_picked[half][:, inner : inner + WIDTH].bitcast(FP8X4),
+                    rhs_scale=xs_plane[:, c * WIDTH : (c + 1) * WIDTH],
                     start=True,
                     stop=True,
                 )
-                nc.scalar.activation(h_rows[:, t, :], h_banks[t][:, cols], RELU, bias=b1_sb[:, t : t + 1])
-            h_grouped = held([P, width, PACK], BF16, "h_grouped%d" % start)
-            interleave(nc.scalar.copy, h_grouped, h_rows)
+                sums[c, t] = bank[:, i, :]
+
+        h_rows = []
+
+        def relu(c, t):
+            if t == 0 and c == CHUNKS - 1:
+                h_rows.append(placed([P, PACK, WIDTH], BF16, "h_rows%d" % c, LAST_ROWS_AT + PLANE // 4))
+            elif t == 0:
+                h_rows.append(held([P, PACK, WIDTH], BF16, "h_rows%d" % c))
+            nc.scalar.activation(h_rows[c][:, t, :], sums[c, t], RELU, bias=b1_sb[:, t : t + 1])
+
+        def quantise_hidden(c):
+            cols = slice(c * WIDTH, (c + 1) * WIDTH)
+            h_grouped = held([P, WIDTH, PACK], BF16, "h_grouped%d" % c)
+            interleave(nc.scalar.copy, h_grouped, h_rows[c])
             nc.vector.quantize_mx(
                 out=h_codes[:, cols].bitcast(FP8X4),
                 scales=h_scales[:, cols],
@@ -195,13 +204,21 @@ def tile_picked_decode2_relu_po_kernel(
 
         pick_scl(2, 0)
         pick_scl(3, 0)
-        first_layer(*HIDDEN_STEPS[0])
-        pick_scl(2, 1, "h_rows0")
-        first_layer(*HIDDEN_STEPS[1])
-        pick_scl(3, 1)
-        first_layer(*HIDDEN_STEPS[2])
+        first_products("first", [(0, 0)])
+        for c in range(CHUNKS):
+            first_products("middle", [(c, 1), (c, 2)])
+            first_products("border", [(c, 3), (c + 1, 0)] if c + 1 < CHUNKS else [(c, 3)])
+            if c == 0:
+                relu(0, 0)
+            for t in range(1, PACK):
+                relu(c, t)
+            if c + 1 < CHUNKS:
+                relu(c + 1, 0)
+            quantise_hidden(c)
+            if c == 0:
+                pick_scl(2, 1, "h_rows0")
+                pick_scl(3, 1)
 
-        out_codes = held([P, S], U32, "out_codes")
         out_scales = held([P, S], U8, "out_scales")
         out_rows = out_0.rearrange("(p t) j -> p t j", t=PACK)
         out_words = out_1[0].rearrange("p n t -> p (n t)").bitcast(I32)
@@ -213,11 +230,15 @@ def tile_picked_decode2_relu_po_kernel(
         def second_layer(c):
             cols = slice(c * WIDTH, (c + 1) * WIDTH)
             half, inner = divmod(c * WIDTH, HALF)
-            scaled.append(held([P, PACK, WIDTH], F32, "scaled%d" % c))
-            bank = psum.tile([P, PACK, WIDTH], F32, name="y_bank%d" % c)
+            scaled.append([held([P, 2, WIDTH], F32, "scaled%d_%d" % (c, pair)) for pair in range(2)])
+            if c == 0:
+                pairs = [psum.tile([P, 2, WIDTH], F32, name="y_pair%d" % pair)[:] for pair in range(2)]
+            else:
+                bank = psum.tile([P, PACK, WIDTH], F32, name="y_bank%d" % c)
+                pairs = [bank[:, :2, :], bank[:, 2:, :]]
             for t in range(PACK):
                 nc.tensor.matmul_mx(
-                    out=bank[:, t, :],
+                    out=pairs[t // 2][:, t % 2, :],
                     lhsT=w2_codes[:, t * P : (t + 1) * P].bitcast(FP8X4),
                     lhsT_scale=w2_plane[:, t * P : (t + 1) * P],
                     rhs=h_codes[:, cols].bitcast(FP8X4),
@@ -226,20 +247,19 @@ def tile_picked_decode2_relu_po_kernel(
                     stop=True,
                 )
             for pair in range(2):
-                planes = slice(2 * pair, 2 * pair + 2)
                 picked = scl_picked[pair, half][:, :, inner : inner + WIDTH]
-                nc.vector.tensor_tensor(scaled[c][:, planes, :], bank[:, planes, :], picked, MULT)
+                nc.vector.tensor_tensor(scaled[c][pair][:], pairs[pair], picked, MULT)
 
         def shift(c):
             start = c * WIDTH
             cols = slice(start, start + WIDTH)
-            if c == 1:
-                result = placed([P, PACK, WIDTH], F32, "result1", LAST_ROWS_AT - PLANE // 2)
-            else:
-                result = held([P, PACK, WIDTH], F32, "result%d" % c)
+            result = held([P, PACK, WIDTH], F32, "result%d" % c)
             for t in range(PACK):
                 nc.vector.tensor_tensor(
-                    result[:, t, :], shf_sb[t][:].indirect(list_slice(rg_sb, start, WIDTH)), scaled[c][:, t, :], ADD
+                    result[:, t, :],
+                    shf_sb[t][:].indirect(list_slice(rg_sb, start, WIDTH)),
+                    scaled[c][t // 2][:, t % 2, :],
+                    ADD,
                 )
             nc.sync.dma_start(out_rows[:, :, cols], result[:])
             if c == 0:
@@ -250,23 +270,22 @@ def tile_picked_decode2_relu_po_kernel(
 
         def quantise_result(c):
             cols = slice(c * WIDTH, (c + 1) * WIDTH)
+            tag = "scaled%d_%d" % (CHUNKS - 1, c - 1) if c in (1, 2) else None
+            out_codes = held([P, WIDTH], U32, "out_codes%d" % c, tag)
             nc.vector.quantize_mx(
-                out=out_codes[:, cols].bitcast(FP8X4),
+                out=out_codes[:].bitcast(FP8X4),
                 scales=out_scales[:, cols],
                 in_=rounded[c][:].rearrange("p c t -> p (c t)"),
             )
-            nc.sync.dma_start(out_words[:, cols], out_codes[:, cols].bitcast(I32))
+            nc.sync.dma_start(out_words[:, cols], out_codes[:].bitcast(I32))
 
-        first_chunks, last_chunks = range(CHUNKS // 2), range(CHUNKS // 2, CHUNKS)
-        for c in first_chunks:
+        for c in range(CHUNKS):
             second_layer(c)
             shift(c)
-        quantise_result(0)
-        for c in last_chunks:
-            second_layer(c)
-        for c in last_chunks:
-            shift(c)
-            quantise_result(c - 1)
+            if c == 1:
+                quantise_result(0)
+        quantise_result(1)
+        quantise_result(2)
         quantise_result(CHUNKS - 1)
         for b in range(PACK):
             queue = nc.scalar if b % 2 else nc.sync

@@ -163,7 +163,7 @@ def tile_picked_decode2_relu_po_kernel(
                 planes[:].rearrange("p t (c i) -> p c t i", i=4),
             )
 
-        h_codes = held([P, S], U32, "h_codes")
+        h_codes = []
         h_scales = held([P, S], U8, "h_scales")
 
         sums = {}
@@ -196,34 +196,19 @@ def tile_picked_decode2_relu_po_kernel(
             cols = slice(c * WIDTH, (c + 1) * WIDTH)
             h_grouped = held([P, WIDTH, PACK], BF16, "h_grouped%d" % c)
             interleave(nc.scalar.copy, h_grouped, h_rows[c])
+            h_codes.append(held([P, WIDTH], U32, "h_codes%d" % c, "h_codes"))
             nc.vector.quantize_mx(
-                out=h_codes[:, cols].bitcast(FP8X4),
+                out=h_codes[c][:].bitcast(FP8X4),
                 scales=h_scales[:, cols],
                 in_=h_grouped[:].rearrange("p c t -> p (c t)"),
             )
-
-        pick_scl(2, 0)
-        pick_scl(3, 0)
-        first_products("first", [(0, 0)])
-        for c in range(CHUNKS):
-            first_products("middle", [(c, 1), (c, 2)])
-            first_products("border", [(c, 3), (c + 1, 0)] if c + 1 < CHUNKS else [(c, 3)])
-            if c == 0:
-                relu(0, 0)
-            for t in range(1, PACK):
-                relu(c, t)
-            if c + 1 < CHUNKS:
-                relu(c + 1, 0)
-            quantise_hidden(c)
-            if c == 0:
-                pick_scl(2, 1, "h_rows0")
-                pick_scl(3, 1)
 
         out_scales = held([P, S], U8, "out_scales")
         out_rows = out_0.rearrange("(p t) j -> p t j", t=PACK)
         out_words = out_1[0].rearrange("p n t -> p (n t)").bitcast(I32)
         out_scale_rows = out_2[0].bitcast(I32).rearrange("(q b) c -> b q c", b=PACK)
         rounded = []
+        results = []
 
         scaled = []
 
@@ -231,17 +216,16 @@ def tile_picked_decode2_relu_po_kernel(
             cols = slice(c * WIDTH, (c + 1) * WIDTH)
             half, inner = divmod(c * WIDTH, HALF)
             scaled.append([held([P, 2, WIDTH], F32, "scaled%d_%d" % (c, pair)) for pair in range(2)])
-            if c == 0:
-                pairs = [psum.tile([P, 2, WIDTH], F32, name="y_pair%d" % pair)[:] for pair in range(2)]
-            else:
-                bank = psum.tile([P, PACK, WIDTH], F32, name="y_bank%d" % c)
-                pairs = [bank[:, :2, :], bank[:, 2:, :]]
+            pairs = [
+                psum.tile([P, 2, WIDTH], F32, name="y%d_%d" % (c, pair), tag="y%d_%d" % (c % 2, pair))[:]
+                for pair in range(2)
+            ]
             for t in range(PACK):
                 nc.tensor.matmul_mx(
                     out=pairs[t // 2][:, t % 2, :],
                     lhsT=w2_codes[:, t * P : (t + 1) * P].bitcast(FP8X4),
                     lhsT_scale=w2_plane[:, t * P : (t + 1) * P],
-                    rhs=h_codes[:, cols].bitcast(FP8X4),
+                    rhs=h_codes[c][:].bitcast(FP8X4),
                     rhs_scale=h_scales[:, cols],
                     start=True,
                     stop=True,
@@ -262,6 +246,10 @@ def tile_picked_decode2_relu_po_kernel(
                     ADD,
                 )
             nc.sync.dma_start(out_rows[:, :, cols], result[:])
+            results.append(result)
+
+        def round_result(c):
+            result = results[c]
             if c == 0:
                 rounded.append(placed([P, WIDTH, PACK], BF16, "rounded0", LAST_ROWS_AT + PLANE // 2))
             else:
@@ -270,7 +258,7 @@ def tile_picked_decode2_relu_po_kernel(
 
         def quantise_result(c):
             cols = slice(c * WIDTH, (c + 1) * WIDTH)
-            tag = "scaled%d_%d" % (CHUNKS - 1, c - 1) if c in (1, 2) else None
+            tag = "scaled%d_%d" % (CHUNKS - 1, c - 1) if c in (1, 2) else "h_codes" if c == 0 else None
             out_codes = held([P, WIDTH], U32, "out_codes%d" % c, tag)
             nc.vector.quantize_mx(
                 out=out_codes[:].bitcast(FP8X4),
@@ -279,14 +267,36 @@ def tile_picked_decode2_relu_po_kernel(
             )
             nc.sync.dma_start(out_words[:, cols], out_codes[:].bitcast(I32))
 
+        def hidden(c):
+            first_products("middle", [(c, 1), (c, 2)])
+            first_products("border", [(c, 3), (c + 1, 0)] if c + 1 < CHUNKS else [(c, 3)])
+            if c == 0:
+                relu(0, 0)
+            for t in range(1, PACK):
+                relu(c, t)
+            if c + 1 < CHUNKS:
+                relu(c + 1, 0)
+            quantise_hidden(c)
+
+        pick_scl(2, 0)
+        pick_scl(3, 0)
+        first_products("first", [(0, 0)])
+        hidden(0)
+        pick_scl(2, 1, "h_rows0")
+        pick_scl(3, 1)
         for c in range(CHUNKS):
             second_layer(c)
-            shift(c)
-            if c == 1:
+            if c + 1 < CHUNKS:
+                hidden(c + 1)
+            else:
                 quantise_result(0)
-        quantise_result(1)
-        quantise_result(2)
-        quantise_result(CHUNKS - 1)
+            shift(c)
+            if c == 2:
+                for done in range(3):
+                    round_result(done)
+        round_result(CHUNKS - 1)
+        for c in range(1, CHUNKS):
+            quantise_result(c)
         for b in range(PACK):
             queue = nc.scalar if b % 2 else nc.sync
             queue.dma_start(out_scale_rows[b], out_scales[b:P:QUADRANT, :].bitcast(I32))

@@ -148,13 +148,13 @@ def tile_picked_decode2_relu_po_kernel(
 
         w2_codes = held([P, N], I32, "w2_codes")
         w2_plane = held([P, N], U8, "w2_plane", "xs_picked")
-        nc.vector.tensor_copy(
-            w2_codes[:].rearrange("p (t a i) -> p a t i", t=PACK, i=4),
-            w2w_raw[:].rearrange("p (a i t) -> p a t i", t=PACK, i=4),
+        nc.gpsimd.tensor_copy(
+            w2_codes[:].rearrange("p (t m) -> p t m", t=PACK),
+            w2w_raw[:].rearrange("p (m t) -> p t m", t=PACK),
         )
-        nc.vector.tensor_copy(
-            w2_plane[:].rearrange("p (t a i) -> p a t i", t=PACK, i=16),
-            w2s_raw[:].rearrange("p (a i t) -> p a t i", t=PACK, i=16),
+        nc.gpsimd.tensor_copy(
+            w2_plane[:].rearrange("p (t m) -> p t m", t=PACK),
+            w2s_raw[:].rearrange("p (m t) -> p t m", t=PACK),
         )
 
         def interleave(copy, grouped, planes):

@@ -32,6 +32,7 @@ W1_AT = 0
 ROUNDED_W1_AT = W1_AT + 4 * PLANE
 WORDS_AT = ROUNDED_W1_AT + 2 * PLANE
 LAST_ROWS_AT = WORDS_AT + 4 * PLANE + PLANE // 2
+FIRST_ROWS_AT = LAST_ROWS_AT + 2 * PLANE
 
 
 def tile_picked_decode2_relu_po_kernel(
@@ -109,10 +110,10 @@ def tile_picked_decode2_relu_po_kernel(
         for half in range(2):
             pick_scl(1, half)
 
-        w2w_raw = held([P, N], I32, "w2w_raw", "scl_sb0")
-        nc.sync.dma_start(w2w_raw[:], w2_words[0].rearrange("p n t -> p (n t)").bitcast(I32))
-        scl_sb.append(held([P, U], F32, "scl_sb2", "scl_sb1"))
+        scl_sb.append(held([P, U], F32, "scl_sb2", "scl_sb0"))
         nc.sync.dma_start(scl_sb[2][:], scl_rows[2])
+        w2w_raw = held([P, N], I32, "w2w_raw", "scl_sb1")
+        nc.sync.dma_start(w2w_raw[:], w2_words[0].rearrange("p n t -> p (n t)").bitcast(I32))
 
         w1_codes = held([P, H], U32, "w1_codes")
         w1_scales = held([P, H], U8, "w1_scales")
@@ -188,6 +189,8 @@ def tile_picked_decode2_relu_po_kernel(
         def relu(c, t):
             if t == 0 and c == CHUNKS - 1:
                 h_rows.append(placed([P, PACK, WIDTH], BF16, "h_rows%d" % c, LAST_ROWS_AT + PLANE // 4))
+            elif t == 0 and c == 0:
+                h_rows.append(placed([P, PACK, WIDTH], BF16, "h_rows0", FIRST_ROWS_AT + PLANE // 4))
             elif t == 0:
                 h_rows.append(held([P, PACK, WIDTH], BF16, "h_rows%d" % c))
             nc.scalar.activation(h_rows[c][:, t, :], sums[c, t], RELU, bias=b1_sb[:, t : t + 1])
@@ -231,14 +234,21 @@ def tile_picked_decode2_relu_po_kernel(
                     stop=True,
                 )
             for pair in range(2):
-                picked = scl_picked[pair, half][:, :, inner : inner + WIDTH]
-                nc.vector.tensor_tensor(scaled[c][pair][:], pairs[pair], picked, MULT)
+                if pair and half:
+                    for u in range(2):
+                        picked = scl_late[u][:, inner : inner + WIDTH]
+                        nc.vector.tensor_tensor(scaled[c][pair][:, u, :], pairs[pair][:, u, :], picked, MULT)
+                else:
+                    picked = scl_picked[pair, half][:, :, inner : inner + WIDTH]
+                    nc.vector.tensor_tensor(scaled[c][pair][:], pairs[pair], picked, MULT)
 
         def shift(c):
             start = c * WIDTH
             cols = slice(start, start + WIDTH)
             result = held([P, PACK, WIDTH], F32, "result%d" % c)
-            for t in range(PACK):
+            if c == 0:
+                nc.vector.tensor_tensor(result[:, :2, :], shf_first[:], scaled[0][0][:], ADD)
+            for t in range(2 if c == 0 else 0, PACK):
                 nc.vector.tensor_tensor(
                     result[:, t, :],
                     shf_sb[t][:].indirect(list_slice(rg_sb, start, WIDTH)),
@@ -280,10 +290,16 @@ def tile_picked_decode2_relu_po_kernel(
 
         pick_scl(2, 0)
         pick_scl(3, 0)
+        scl_late = [held([P, HALF], F32, "scl_late2")]
+        nc.vector.tensor_copy(scl_late[0][:], scl_sb[2][:].indirect(list_slice(rg_sb, HALF, HALF)))
         first_products("first", [(0, 0)])
         hidden(0)
-        pick_scl(2, 1, "h_rows0")
-        pick_scl(3, 1)
+        late = placed([P, HALF], F32, "scl_late3", FIRST_ROWS_AT)
+        nc.vector.tensor_copy(late[:], scl_sb[3][:].indirect(list_slice(rg_sb, HALF, HALF)))
+        scl_late.append(late)
+        shf_first = placed([P, 2, WIDTH], F32, "shf_first", FIRST_ROWS_AT + PLANE // 2)
+        for t in range(2):
+            nc.vector.tensor_copy(shf_first[:, t, :], shf_sb[t][:].indirect(list_slice(rg_sb, 0, WIDTH)))
         for c in range(CHUNKS):
             second_layer(c)
             if c + 1 < CHUNKS:

@@ -247,8 +247,8 @@ def tile_picked_decode2_relu_po_kernel(
             cols = slice(start, start + WIDTH)
             result = held([P, PACK, WIDTH], F32, "result%d" % c)
             if c == 0:
-                nc.vector.tensor_tensor(result[:, :2, :], shf_first[:], scaled[0][0][:], ADD)
-            for t in range(2 if c == 0 else 0, PACK):
+                nc.vector.tensor_tensor(result[:, :1, :], shf_first[:], scaled[0][0][:, :1, :], ADD)
+            for t in range(1 if c == 0 else 0, PACK):
                 nc.vector.tensor_tensor(
                     result[:, t, :],
                     shf_sb[t][:].indirect(list_slice(rg_sb, start, WIDTH)),
@@ -297,8 +297,8 @@ def tile_picked_decode2_relu_po_kernel(
         late = placed([P, HALF], F32, "scl_late3", FIRST_ROWS_AT)
         nc.vector.tensor_copy(late[:], scl_sb[3][:].indirect(list_slice(rg_sb, HALF, HALF)))
         scl_late.append(late)
-        shf_first = placed([P, 2, WIDTH], F32, "shf_first", FIRST_ROWS_AT + PLANE // 2)
-        for t in range(2):
+        shf_first = placed([P, 1, WIDTH], F32, "shf_first", FIRST_ROWS_AT + PLANE // 2)
+        for t in range(1):
             nc.vector.tensor_copy(shf_first[:, t, :], shf_sb[t][:].indirect(list_slice(rg_sb, 0, WIDTH)))
         for c in range(CHUNKS):
             second_layer(c)

@@ -15,6 +15,7 @@ FP8X4 = mybir.dt.float8_e4m3fn_x4
 MULT = mybir.AluOpType.mult
 ADD = mybir.AluOpType.add
 RELU = mybir.ActivationFunctionType.Relu
+COPY = mybir.ActivationFunctionType.Copy
 
 P = 128
 PACK = 4
@@ -22,17 +23,14 @@ QUADRANT = 32
 BLOCK = 8
 LIST = 16
 HALF = 256
-HIDDEN_STEPS = ((0, 128), (128, 128), (256, 256))
 WIDTH = 128
 CHUNKS = S // WIDTH
 CLEARED_BY_VECTOR = 3 * T // 4
 
 PLANE = 4 * U
 W1_AT = 0
-ROUNDED_W1_AT = W1_AT + 4 * PLANE
-WORDS_AT = ROUNDED_W1_AT + 2 * PLANE
-LAST_ROWS_AT = WORDS_AT + 4 * PLANE + PLANE // 2
-FIRST_ROWS_AT = LAST_ROWS_AT + 2 * PLANE
+ROUNDED_W1_AT = W1_AT + PACK * PLANE
+SCALE_TABLE_AT = ROUNDED_W1_AT + 2 * PLANE
 
 
 def tile_picked_decode2_relu_po_kernel(
@@ -50,10 +48,22 @@ def tile_picked_decode2_relu_po_kernel(
         def placed(shape, dtype, name, offset):
             return shared.tile(shape, dtype, name=name, align_bytes=64, offset=offset)
 
+        def scalar_gather(out, window):
+            nc.scalar.activation(out, window, COPY)
+
+        def list_slice(lists, start, count):
+            return lists[:, start // LIST : (start + count) // LIST]
+
+        def interleave(copy, grouped, planes):
+            copy(
+                grouped.rearrange("p (c i) t -> p c t i", i=4),
+                planes.rearrange("p t (c i) -> p c t i", i=4),
+            )
+
         offs_sb = held([P, S // LIST], U16, "offs_sb")
         rg_sb = held([P, S // LIST], U16, "rg_sb")
-        xs_table = held([P, T], U8, "xs_table")
-        xw_table = placed([P, T], I32, "xw_table", WORDS_AT)
+        xs_table = placed([P, T], U8, "xs_table", SCALE_TABLE_AT)
+        xw_table = held([P, T], I32, "xw_table")
         w1_raw = placed([P, PACK, H], F32, "w1_raw", W1_AT)
         b1_sb = held([P, PACK], F32, "b1_sb")
         scl_sb = [held([P, U], F32, "scl_sb%d" % t) for t in range(2)]
@@ -84,22 +94,13 @@ def tile_picked_decode2_relu_po_kernel(
         for b in range(PACK):
             nc.gpsimd.dma_start(w2s_raw[b:P:QUADRANT, :].bitcast(I32), w2s_rows[b])
 
-        def list_slice(lists, start, count):
-            return lists[:, start // LIST : (start + count) // LIST]
+        scl_picked = [held([P, PACK, HALF], F32, "scl_picked%d" % half) for half in range(2)]
 
-        scl_picked = {}
-
-        def pick_scl(t, half, tag=None):
-            pair = t // 2
-            if (pair, half) not in scl_picked:
-                scl_picked[pair, half] = held([P, 2, HALF], F32, "scl_picked%d_%d" % (pair, half), tag)
-            nc.vector.tensor_copy(
-                scl_picked[pair, half][:, t % 2, :],
-                scl_sb[t][:].indirect(list_slice(rg_sb, half * HALF, HALF)),
-            )
+        def pick_scl(gather, t, half):
+            gather(scl_picked[half][:, t, :], scl_sb[t][:].indirect(list_slice(rg_sb, half * HALF, HALF)))
 
         for half in range(2):
-            pick_scl(0, half)
+            pick_scl(nc.vector.tensor_copy, 0, half)
 
         xs_picked = held([P, S], U8, "xs_picked")
         nc.vector.tensor_copy(xs_picked[:], xs_table[:].indirect(offs_sb[:]))
@@ -107,169 +108,134 @@ def tile_picked_decode2_relu_po_kernel(
             nc.sync.dma_start(
                 xs_plane[b:P:QUADRANT, :].bitcast(I32), xs_picked[BLOCK * b : P : QUADRANT, :].bitcast(I32)
             )
-        for half in range(2):
-            pick_scl(1, half)
 
-        scl_sb.append(held([P, U], F32, "scl_sb2", "scl_sb0"))
+        scl_sb.append(placed([P, U], F32, "scl_sb2", SCALE_TABLE_AT))
         nc.sync.dma_start(scl_sb[2][:], scl_rows[2])
-        w2w_raw = held([P, N], I32, "w2w_raw", "scl_sb1")
-        nc.sync.dma_start(w2w_raw[:], w2_words[0].rearrange("p n t -> p (n t)").bitcast(I32))
 
         w1_codes = held([P, H], U32, "w1_codes")
         w1_scales = held([P, H], U8, "w1_scales")
-        for pair in range(2):
-            w1_grouped = placed([P, 2, P, PACK], BF16, "w1_grouped%d" % pair, ROUNDED_W1_AT + pair * PLANE)
-            code_cols = slice(2 * pair * P, 2 * (pair + 1) * P)
-            nc.scalar.copy(
-                w1_grouped[:].rearrange("p t m j -> p m j t"),
+        w1_grouped = []
+        for pair, copy in enumerate((nc.scalar.copy, nc.scalar.copy)):
+            w1_grouped.append(
+                placed([P, 2, P, PACK], BF16, "w1_grouped%d" % pair, ROUNDED_W1_AT + pair * PLANE)
+            )
+            copy(
+                w1_grouped[pair][:].rearrange("p t m j -> p m j t"),
                 w1_raw[:].rearrange("p j (m t) -> p m j t", t=PACK)[:, :, :, 2 * pair : 2 * pair + 2],
             )
+        for pair in range(2):
+            code_cols = slice(2 * pair * P, 2 * (pair + 1) * P)
             nc.vector.quantize_mx(
                 out=w1_codes[:, code_cols].bitcast(FP8X4),
                 scales=w1_scales[:, code_cols],
-                in_=w1_grouped[:].rearrange("p t m j -> p (t m j)"),
+                in_=w1_grouped[pair][:].rearrange("p t m j -> p (t m j)"),
             )
-        scl_sb.append(placed([P, U], F32, "scl_sb3", W1_AT))
-        nc.sync.dma_start(scl_sb[3][:], scl_rows[3])
+            pick_scl(scalar_gather if pair else nc.vector.tensor_copy, 1, pair)
 
-        xw_picked = [
-            placed([P, HALF], U32, "xw_picked%d" % half, ROUNDED_W1_AT + PLANE + half * PLANE // 2)
-            for half in range(2)
-        ]
+        scl_sb.append(placed([P, U], F32, "scl_sb3", ROUNDED_W1_AT))
+        nc.sync.dma_start(scl_sb[3][:], scl_rows[3])
+        w2w_raw = placed([P, N], I32, "w2w_raw", W1_AT)
+        nc.sync.dma_start(w2w_raw[:], w2_words[0].rearrange("p n t -> p (n t)").bitcast(I32))
+        shf_sb = []
+        for t in range(PACK):
+            shf_sb.append(placed([P, U], F32, "shf_sb%d" % t, W1_AT + (t + 1 + t // 3) * PLANE))
+            nc.sync.dma_start(shf_sb[t][:], shf_rows[t])
+
+        xw_picked = [held([P, HALF], U32, "xw_picked%d" % half) for half in range(2)]
         for half in range(2):
             nc.vector.tensor_copy(
                 xw_picked[half][:], xw_table[:].bitcast(U32).indirect(list_slice(offs_sb, half * HALF, HALF))
             )
 
-        shf_sb = []
-        for t in range(PACK):
-            shf_at = W1_AT + (t + 1) * PLANE if t + 1 < PACK else WORDS_AT
-            shf_sb.append(placed([P, U], F32, "shf_sb%d" % t, shf_at))
-            nc.sync.dma_start(shf_sb[t][:], shf_rows[t])
-
         w2_codes = held([P, N], I32, "w2_codes")
         w2_plane = held([P, N], U8, "w2_plane", "xs_picked")
-        nc.gpsimd.tensor_copy(
-            w2_codes[:].rearrange("p (t m) -> p t m", t=PACK),
-            w2w_raw[:].rearrange("p (m t) -> p t m", t=PACK),
-        )
         nc.gpsimd.tensor_copy(
             w2_plane[:].rearrange("p (t m) -> p t m", t=PACK),
             w2s_raw[:].rearrange("p (m t) -> p t m", t=PACK),
         )
+        nc.gpsimd.tensor_copy(
+            w2_codes[:].rearrange("p (t m) -> p t m", t=PACK),
+            w2w_raw[:].rearrange("p (m t) -> p t m", t=PACK),
+        )
 
-        def interleave(copy, grouped, planes):
-            copy(
-                grouped[:].rearrange("p (c i) t -> p c t i", i=4),
-                planes[:].rearrange("p t (c i) -> p c t i", i=4),
-            )
-
-        h_codes = []
+        h_codes = held([P, S], U32, "h_codes")
         h_scales = held([P, S], U8, "h_scales")
 
-        sums = {}
+        def hidden_rows(start, width, banks):
+            half, inner = divmod(start, HALF)
+            per_bank = PACK // banks
+            rows = held([P, PACK, width], BF16, "h_rows%d" % start)
+            for bank in range(banks):
+                sums = psum.tile([P, per_bank, width], F32, name="sums%d_%d" % (start, bank))
+                for i in range(per_bank):
+                    t = bank * per_bank + i
+                    nc.tensor.matmul_mx(
+                        out=sums[:, i, :],
+                        lhsT=w1_codes[:, t * P : (t + 1) * P].bitcast(FP8X4),
+                        lhsT_scale=w1_scales[:, t * P : (t + 1) * P],
+                        rhs=xw_picked[half][:, inner : inner + width].bitcast(FP8X4),
+                        rhs_scale=xs_plane[:, start : start + width],
+                        start=True,
+                        stop=True,
+                    )
+                for i in range(per_bank):
+                    t = bank * per_bank + i
+                    nc.scalar.activation(rows[:, t, :], sums[:, i, :], RELU, bias=b1_sb[:, t : t + 1])
+            return rows
 
-        def first_products(tag, items):
-            bank = psum.tile([P, len(items), WIDTH], F32, name="sums%d_%d" % items[0], tag=tag)
-            for i, (c, t) in enumerate(items):
-                half, inner = divmod(c * WIDTH, HALF)
-                nc.tensor.matmul_mx(
-                    out=bank[:, i, :],
-                    lhsT=w1_codes[:, t * P : (t + 1) * P].bitcast(FP8X4),
-                    lhsT_scale=w1_scales[:, t * P : (t + 1) * P],
-                    rhs=xw_picked[half][:, inner : inner + WIDTH].bitcast(FP8X4),
-                    rhs_scale=xs_plane[:, c * WIDTH : (c + 1) * WIDTH],
-                    start=True,
-                    stop=True,
-                )
-                sums[c, t] = bank[:, i, :]
+        def group_hidden(copy, start, rows):
+            grouped = held([P, rows.shape[2], PACK], BF16, "h_grouped%d" % start)
+            interleave(copy, grouped[:], rows[:])
+            return grouped
 
-        h_rows = []
-
-        def relu(c, t):
-            if t == 0 and c == CHUNKS - 1:
-                h_rows.append(placed([P, PACK, WIDTH], BF16, "h_rows%d" % c, LAST_ROWS_AT + PLANE // 4))
-            elif t == 0 and c == 0:
-                h_rows.append(placed([P, PACK, WIDTH], BF16, "h_rows0", FIRST_ROWS_AT + PLANE // 4))
-            elif t == 0:
-                h_rows.append(held([P, PACK, WIDTH], BF16, "h_rows%d" % c))
-            nc.scalar.activation(h_rows[c][:, t, :], sums[c, t], RELU, bias=b1_sb[:, t : t + 1])
-
-        def quantise_hidden(c):
-            cols = slice(c * WIDTH, (c + 1) * WIDTH)
-            h_grouped = held([P, WIDTH, PACK], BF16, "h_grouped%d" % c)
-            interleave(nc.scalar.copy, h_grouped, h_rows[c])
-            h_codes.append(held([P, WIDTH], U32, "h_codes%d" % c, "h_codes"))
+        def quantise_hidden(start, grouped):
+            cols = slice(start, start + grouped.shape[1])
             nc.vector.quantize_mx(
-                out=h_codes[c][:].bitcast(FP8X4),
+                out=h_codes[:, cols].bitcast(FP8X4),
                 scales=h_scales[:, cols],
-                in_=h_grouped[:].rearrange("p c t -> p (c t)"),
+                in_=grouped[:].rearrange("p c t -> p (c t)"),
             )
 
         out_scales = held([P, S], U8, "out_scales")
         out_rows = out_0.rearrange("(p t) j -> p t j", t=PACK)
         out_words = out_1[0].rearrange("p n t -> p (n t)").bitcast(I32)
         out_scale_rows = out_2[0].bitcast(I32).rearrange("(q b) c -> b q c", b=PACK)
-        rounded = []
-        results = []
+        scaled, results, rounded = {}, {}, {}
 
-        scaled = []
-
-        def second_layer(c):
+        def scale(c):
             cols = slice(c * WIDTH, (c + 1) * WIDTH)
             half, inner = divmod(c * WIDTH, HALF)
-            scaled.append([held([P, 2, WIDTH], F32, "scaled%d_%d" % (c, pair)) for pair in range(2)])
-            pairs = [
-                psum.tile([P, 2, WIDTH], F32, name="y%d_%d" % (c, pair), tag="y%d_%d" % (c % 2, pair))[:]
-                for pair in range(2)
-            ]
+            y = psum.tile([P, PACK, WIDTH], F32, name="y%d" % c, tag="y%d" % (c % 3))
             for t in range(PACK):
                 nc.tensor.matmul_mx(
-                    out=pairs[t // 2][:, t % 2, :],
+                    out=y[:, t, :],
                     lhsT=w2_codes[:, t * P : (t + 1) * P].bitcast(FP8X4),
                     lhsT_scale=w2_plane[:, t * P : (t + 1) * P],
-                    rhs=h_codes[c][:].bitcast(FP8X4),
+                    rhs=h_codes[:, cols].bitcast(FP8X4),
                     rhs_scale=h_scales[:, cols],
                     start=True,
                     stop=True,
                 )
-            for pair in range(2):
-                if pair and half:
-                    for u in range(2):
-                        picked = scl_late[u][:, inner : inner + WIDTH]
-                        nc.vector.tensor_tensor(scaled[c][pair][:, u, :], pairs[pair][:, u, :], picked, MULT)
-                else:
-                    picked = scl_picked[pair, half][:, :, inner : inner + WIDTH]
-                    nc.vector.tensor_tensor(scaled[c][pair][:], pairs[pair], picked, MULT)
+            scaled[c] = held([P, PACK, WIDTH], F32, "scaled%d" % c)
+            nc.vector.tensor_tensor(scaled[c][:], y[:], scl_picked[half][:, :, inner : inner + WIDTH], MULT)
 
-        def shift(c):
-            start = c * WIDTH
-            cols = slice(start, start + WIDTH)
-            result = held([P, PACK, WIDTH], F32, "result%d" % c)
-            if c == 0:
-                nc.vector.tensor_tensor(result[:, :1, :], shf_first[:], scaled[0][0][:, :1, :], ADD)
-            for t in range(1 if c == 0 else 0, PACK):
-                nc.vector.tensor_tensor(
-                    result[:, t, :],
-                    shf_sb[t][:].indirect(list_slice(rg_sb, start, WIDTH)),
-                    scaled[c][t // 2][:, t % 2, :],
-                    ADD,
-                )
-            nc.sync.dma_start(out_rows[:, :, cols], result[:])
-            results.append(result)
-
-        def round_result(c):
-            result = results[c]
-            if c == 0:
-                rounded.append(placed([P, WIDTH, PACK], BF16, "rounded0", LAST_ROWS_AT + PLANE // 2))
+        def shift(c, picked=None, tag=None):
+            results[c] = held([P, PACK, WIDTH], F32, "result%d" % c, tag)
+            if picked is None:
+                for t in range(PACK):
+                    window = shf_sb[t][:].indirect(list_slice(rg_sb, c * WIDTH, WIDTH))
+                    nc.vector.tensor_tensor(results[c][:, t, :], window, scaled[c][:, t, :], ADD)
             else:
-                rounded.append(held([P, WIDTH, PACK], BF16, "rounded%d" % c))
-            interleave(nc.vector.tensor_copy if c == CHUNKS - 1 else nc.scalar.copy, rounded[c], result)
+                nc.vector.tensor_tensor(results[c][:], picked, scaled[c][:], ADD)
+            nc.sync.dma_start(out_rows[:, :, c * WIDTH : (c + 1) * WIDTH], results[c][:])
+
+        def round_result(copy, c):
+            rounded[c] = held([P, WIDTH, PACK], BF16, "rounded%d" % c)
+            interleave(copy, rounded[c][:], results[c][:])
 
         def quantise_result(c):
             cols = slice(c * WIDTH, (c + 1) * WIDTH)
-            tag = "scaled%d_%d" % (CHUNKS - 1, c - 1) if c in (1, 2) else "h_codes" if c == 0 else None
-            out_codes = held([P, WIDTH], U32, "out_codes%d" % c, tag)
+            out_codes = held([P, WIDTH], U32, "out_codes%d" % c)
             nc.vector.quantize_mx(
                 out=out_codes[:].bitcast(FP8X4),
                 scales=out_scales[:, cols],
@@ -277,42 +243,38 @@ def tile_picked_decode2_relu_po_kernel(
             )
             nc.sync.dma_start(out_words[:, cols], out_codes[:].bitcast(I32))
 
-        def hidden(c):
-            first_products("middle", [(c, 1), (c, 2)])
-            first_products("border", [(c, 3), (c + 1, 0)] if c + 1 < CHUNKS else [(c, 3)])
-            if c == 0:
-                relu(0, 0)
-            for t in range(1, PACK):
-                relu(c, t)
-            if c + 1 < CHUNKS:
-                relu(c + 1, 0)
-            quantise_hidden(c)
-
-        pick_scl(2, 0)
-        pick_scl(3, 0)
-        scl_late = [held([P, HALF], F32, "scl_late2")]
-        nc.vector.tensor_copy(scl_late[0][:], scl_sb[2][:].indirect(list_slice(rg_sb, HALF, HALF)))
-        first_products("first", [(0, 0)])
-        hidden(0)
-        late = placed([P, HALF], F32, "scl_late3", FIRST_ROWS_AT)
-        nc.vector.tensor_copy(late[:], scl_sb[3][:].indirect(list_slice(rg_sb, HALF, HALF)))
-        scl_late.append(late)
-        shf_first = placed([P, 1, WIDTH], F32, "shf_first", FIRST_ROWS_AT + PLANE // 2)
-        for t in range(1):
-            nc.vector.tensor_copy(shf_first[:, t, :], shf_sb[t][:].indirect(list_slice(rg_sb, 0, WIDTH)))
-        for c in range(CHUNKS):
-            second_layer(c)
-            if c + 1 < CHUNKS:
-                hidden(c + 1)
-            else:
-                quantise_result(0)
-            shift(c)
-            if c == 2:
-                for done in range(3):
-                    round_result(done)
-        round_result(CHUNKS - 1)
-        for c in range(1, CHUNKS):
-            quantise_result(c)
+        rows0 = hidden_rows(0, WIDTH, 2)
+        pick_scl(nc.vector.tensor_copy, 2, 0)
+        pick_scl(nc.vector.tensor_copy, 3, 0)
+        grouped0 = group_hidden(nc.vector.tensor_copy, 0, rows0)
+        rows1 = hidden_rows(WIDTH, WIDTH, 1)
+        quantise_hidden(0, grouped0)
+        pick_scl(nc.vector.tensor_copy, 2, 1)
+        grouped1 = group_hidden(nc.vector.tensor_copy, WIDTH, rows1)
+        scale(0)
+        quantise_hidden(WIDTH, grouped1)
+        rows2 = hidden_rows(HALF, HALF, 2)
+        grouped2 = group_hidden(nc.scalar.copy, HALF, rows2)
+        shift(0)
+        scale(1)
+        quantise_hidden(HALF, grouped2)
+        shift(1, tag="h_rows%d" % HALF)
+        pick_scl(scalar_gather, 3, 1)
+        shf_late = held([P, PACK, HALF], F32, "shf_late")
+        for t in range(PACK):
+            scalar_gather(shf_late[:, t, :], shf_sb[t][:].indirect(list_slice(rg_sb, HALF, HALF)))
+        scale(2)
+        scale(3)
+        shift(2, shf_late[:, :, :WIDTH])
+        round_result(nc.scalar.copy, 0)
+        quantise_result(0)
+        shift(3, shf_late[:, :, WIDTH:])
+        round_result(nc.scalar.copy, 1)
+        quantise_result(1)
+        round_result(nc.vector.tensor_copy, 3)
+        round_result(nc.scalar.copy, 2)
+        quantise_result(2)
+        quantise_result(3)
         for b in range(PACK):
             queue = nc.scalar if b % 2 else nc.sync
             queue.dma_start(out_scale_rows[b], out_scales[b:P:QUADRANT, :].bitcast(I32))

@@ -233,15 +233,18 @@ def tile_picked_decode2_relu_po_kernel(
             rounded[c] = held([P, WIDTH, PACK], BF16, "rounded%d" % c)
             interleave(copy, rounded[c][:], results[c][:])
 
+        out_codes = held([P, S], U32, "out_codes")
+
         def quantise_result(c):
             cols = slice(c * WIDTH, (c + 1) * WIDTH)
-            out_codes = held([P, WIDTH], U32, "out_codes%d" % c)
             nc.vector.quantize_mx(
-                out=out_codes[:].bitcast(FP8X4),
+                out=out_codes[:, cols].bitcast(FP8X4),
                 scales=out_scales[:, cols],
                 in_=rounded[c][:].rearrange("p c t -> p (c t)"),
             )
-            nc.sync.dma_start(out_words[:, cols], out_codes[:].bitcast(I32))
+
+        def store_codes(cols):
+            nc.sync.dma_start(out_words[:, cols], out_codes[:, cols].bitcast(I32))
 
         rows0 = hidden_rows(0, WIDTH, 2)
         pick_scl(nc.vector.tensor_copy, 2, 0)
@@ -274,7 +277,9 @@ def tile_picked_decode2_relu_po_kernel(
         round_result(nc.vector.tensor_copy, 3)
         round_result(nc.scalar.copy, 2)
         quantise_result(2)
+        store_codes(slice(0, S - WIDTH))
         quantise_result(3)
+        store_codes(slice(S - WIDTH, S))
         for b in range(PACK):
             queue = nc.scalar if b % 2 else nc.sync
             queue.dma_start(out_scale_rows[b], out_scales[b:P:QUADRANT, :].bitcast(I32))

@@ -24,13 +24,14 @@ BLOCK = 8
 LIST = 16
 HALF = 256
 WIDTH = 128
-CHUNKS = S // WIDTH
+AHEAD = 2
 CLEARED_BY_VECTOR = 3 * T // 4
 
 PLANE = 4 * U
 W1_AT = 0
 ROUNDED_W1_AT = W1_AT + PACK * PLANE
 SCALE_TABLE_AT = ROUNDED_W1_AT + 2 * PLANE
+LAST_ROWS_AT = SCALE_TABLE_AT + 2 * PLANE
 
 
 def tile_picked_decode2_relu_po_kernel(
@@ -66,7 +67,7 @@ def tile_picked_decode2_relu_po_kernel(
         xw_table = held([P, T], I32, "xw_table")
         w1_raw = placed([P, PACK, H], F32, "w1_raw", W1_AT)
         b1_sb = held([P, PACK], F32, "b1_sb")
-        scl_sb = [held([P, U], F32, "scl_sb%d" % t) for t in range(2)]
+        scl_sb = [held([P, U], F32, "scl_sb%d" % t) for t in range(PACK - 1)]
 
         nc.vector.memset(xs_table[:, :CLEARED_BY_VECTOR].bitcast(I32), 0)
         nc.gpsimd.memset(xs_table[:, CLEARED_BY_VECTOR:].bitcast(I32), 0)
@@ -88,16 +89,21 @@ def tile_picked_decode2_relu_po_kernel(
         nc.sync.dma_start(scl_sb[1][:], scl_rows[1])
         nc.sync.dma_start(xw_table[:], x_words[0].rearrange("p n t -> p (n t)").bitcast(I32))
         nc.sync.dma_start(b1_sb[:], b1.rearrange("(p t) o -> p (t o)", t=PACK))
+        nc.sync.dma_start(scl_sb[2][:], scl_rows[2])
 
         w2s_raw = held([P, N], U8, "w2s_raw")
         nc.gpsimd.memset(w2s_raw[:].bitcast(I32), 0)
         for b in range(PACK):
             nc.gpsimd.dma_start(w2s_raw[b:P:QUADRANT, :].bitcast(I32), w2s_rows[b])
 
-        scl_picked = [held([P, PACK, HALF], F32, "scl_picked%d" % half) for half in range(2)]
+        scl_picked = {}
 
-        def pick_scl(gather, t, half):
-            gather(scl_picked[half][:, t, :], scl_sb[t][:].indirect(list_slice(rg_sb, half * HALF, HALF)))
+        def pick_scl(gather, t, half, tag=None):
+            pair = t // 2
+            if (pair, half) not in scl_picked:
+                scl_picked[pair, half] = held([P, 2, HALF], F32, "scl_picked%d_%d" % (pair, half), tag)
+            window = scl_sb[t][:].indirect(list_slice(rg_sb, half * HALF, HALF))
+            gather(scl_picked[pair, half][:, t % 2, :], window)
 
         for half in range(2):
             pick_scl(nc.vector.tensor_copy, 0, half)
@@ -109,8 +115,8 @@ def tile_picked_decode2_relu_po_kernel(
                 xs_plane[b:P:QUADRANT, :].bitcast(I32), xs_picked[BLOCK * b : P : QUADRANT, :].bitcast(I32)
             )
 
-        scl_sb.append(placed([P, U], F32, "scl_sb2", SCALE_TABLE_AT))
-        nc.sync.dma_start(scl_sb[2][:], scl_rows[2])
+        w2w_raw = placed([P, N], I32, "w2w_raw", SCALE_TABLE_AT)
+        nc.sync.dma_start(w2w_raw[:], w2_words[0].rearrange("p n t -> p (n t)").bitcast(I32))
 
         w1_codes = held([P, H], U32, "w1_codes")
         w1_scales = held([P, H], U8, "w1_scales")
@@ -134,11 +140,9 @@ def tile_picked_decode2_relu_po_kernel(
 
         scl_sb.append(placed([P, U], F32, "scl_sb3", ROUNDED_W1_AT))
         nc.sync.dma_start(scl_sb[3][:], scl_rows[3])
-        w2w_raw = placed([P, N], I32, "w2w_raw", W1_AT)
-        nc.sync.dma_start(w2w_raw[:], w2_words[0].rearrange("p n t -> p (n t)").bitcast(I32))
         shf_sb = []
         for t in range(PACK):
-            shf_sb.append(placed([P, U], F32, "shf_sb%d" % t, W1_AT + (t + 1 + t // 3) * PLANE))
+            shf_sb.append(placed([P, U], F32, "shf_sb%d" % t, W1_AT + t * PLANE))
             nc.sync.dma_start(shf_sb[t][:], shf_rows[t])
 
         xw_picked = [held([P, HALF], U32, "xw_picked%d" % half) for half in range(2)]
@@ -158,30 +162,36 @@ def tile_picked_decode2_relu_po_kernel(
             w2w_raw[:].rearrange("p (m t) -> p t m", t=PACK),
         )
 
-        h_codes = held([P, S], U32, "h_codes")
+        h_codes = {}
         h_scales = held([P, S], U8, "h_scales")
 
-        def hidden_rows(start, width, banks):
-            half, inner = divmod(start, HALF)
-            per_bank = PACK // banks
-            rows = held([P, PACK, width], BF16, "h_rows%d" % start)
-            for bank in range(banks):
-                sums = psum.tile([P, per_bank, width], F32, name="sums%d_%d" % (start, bank))
-                for i in range(per_bank):
-                    t = bank * per_bank + i
-                    nc.tensor.matmul_mx(
-                        out=sums[:, i, :],
-                        lhsT=w1_codes[:, t * P : (t + 1) * P].bitcast(FP8X4),
-                        lhsT_scale=w1_scales[:, t * P : (t + 1) * P],
-                        rhs=xw_picked[half][:, inner : inner + width].bitcast(FP8X4),
-                        rhs_scale=xs_plane[:, start : start + width],
-                        start=True,
-                        stop=True,
-                    )
-                for i in range(per_bank):
-                    t = bank * per_bank + i
-                    nc.scalar.activation(rows[:, t, :], sums[:, i, :], RELU, bias=b1_sb[:, t : t + 1])
-            return rows
+        sums, rows = {}, {}
+
+        def first_products(tag, items):
+            bank = psum.tile([P, 2 * HALF], F32, name="sums%d_%d" % items[0][::2], tag=tag)
+            used = 0
+            for start, width, t in items:
+                half, inner = divmod(start, HALF)
+                sums[start, t] = bank[:, used : used + width]
+                used = used + width
+                nc.tensor.matmul_mx(
+                    out=sums[start, t],
+                    lhsT=w1_codes[:, t * P : (t + 1) * P].bitcast(FP8X4),
+                    lhsT_scale=w1_scales[:, t * P : (t + 1) * P],
+                    rhs=xw_picked[half][:, inner : inner + width].bitcast(FP8X4),
+                    rhs_scale=xs_plane[:, start : start + width],
+                    start=True,
+                    stop=True,
+                )
+
+        def relu(start, t):
+            if t == 0 and start == HALF:
+                rows[start] = placed([P, PACK, HALF], BF16, "h_rows_last", LAST_ROWS_AT)
+            elif t == 0 and start == 0:
+                rows[start] = placed([P, PACK, WIDTH], BF16, "h_rows_first", LAST_ROWS_AT)
+            elif t == 0:
+                rows[start] = held([P, PACK, sums[start, t].shape[1]], BF16, "h_rows%d" % start)
+            nc.scalar.activation(rows[start][:, t, :], sums[start, t], RELU, bias=b1_sb[:, t : t + 1])
 
         def group_hidden(copy, start, rows):
             grouped = held([P, rows.shape[2], PACK], BF16, "h_grouped%d" % start)
@@ -189,9 +199,13 @@ def tile_picked_decode2_relu_po_kernel(
             return grouped
 
         def quantise_hidden(start, grouped):
-            cols = slice(start, start + grouped.shape[1])
+            width = grouped.shape[1]
+            cols = slice(start, start + width)
+            codes = held([P, width], U32, "h_codes%d" % start, "h_codes%d" % width)
+            for at in range(0, width, WIDTH):
+                h_codes[(start + at) // WIDTH] = codes[:, at : at + WIDTH]
             nc.vector.quantize_mx(
-                out=h_codes[:, cols].bitcast(FP8X4),
+                out=codes[:].bitcast(FP8X4),
                 scales=h_scales[:, cols],
                 in_=grouped[:].rearrange("p c t -> p (c t)"),
             )
@@ -205,32 +219,35 @@ def tile_picked_decode2_relu_po_kernel(
         def scale(c):
             cols = slice(c * WIDTH, (c + 1) * WIDTH)
             half, inner = divmod(c * WIDTH, HALF)
-            y = psum.tile([P, PACK, WIDTH], F32, name="y%d" % c, tag="y%d" % (c % 3))
-            for t in range(PACK):
-                nc.tensor.matmul_mx(
-                    out=y[:, t, :],
-                    lhsT=w2_codes[:, t * P : (t + 1) * P].bitcast(FP8X4),
-                    lhsT_scale=w2_plane[:, t * P : (t + 1) * P],
-                    rhs=h_codes[:, cols].bitcast(FP8X4),
-                    rhs_scale=h_scales[:, cols],
-                    start=True,
-                    stop=True,
-                )
             scaled[c] = held([P, PACK, WIDTH], F32, "scaled%d" % c)
-            nc.vector.tensor_tensor(scaled[c][:], y[:], scl_picked[half][:, :, inner : inner + WIDTH], MULT)
+            for pair in range(2):
+                y = psum.tile([P, 2, WIDTH], F32, name="y%d_%d" % (c, pair), tag="y%d_%d" % (c % 2, pair))
+                for i in range(2):
+                    t = 2 * pair + i
+                    nc.tensor.matmul_mx(
+                        out=y[:, i, :],
+                        lhsT=w2_codes[:, t * P : (t + 1) * P].bitcast(FP8X4),
+                        lhsT_scale=w2_plane[:, t * P : (t + 1) * P],
+                        rhs=h_codes[c].bitcast(FP8X4),
+                        rhs_scale=h_scales[:, cols],
+                        start=True,
+                        stop=True,
+                    )
+                picked = scl_picked[pair, half][:, :, inner : inner + WIDTH]
+                nc.vector.tensor_tensor(scaled[c][:, 2 * pair : 2 * pair + 2, :], y[:], picked, MULT)
 
-        def shift(c, picked=None, tag=None):
-            results[c] = held([P, PACK, WIDTH], F32, "result%d" % c, tag)
-            if picked is None:
-                for t in range(PACK):
-                    window = shf_sb[t][:].indirect(list_slice(rg_sb, c * WIDTH, WIDTH))
-                    nc.vector.tensor_tensor(results[c][:, t, :], window, scaled[c][:, t, :], ADD)
-            else:
-                nc.vector.tensor_tensor(results[c][:], picked, scaled[c][:], ADD)
-            nc.sync.dma_start(out_rows[:, :, c * WIDTH : (c + 1) * WIDTH], results[c][:])
+        def shift(c, result, picked=None):
+            results[c] = result
+            ahead = 0 if picked is None else picked.shape[1]
+            if ahead:
+                nc.vector.tensor_tensor(result[:, :ahead, :], picked, scaled[c][:, :ahead, :], ADD)
+            for t in range(ahead, PACK):
+                window = shf_sb[t][:].indirect(list_slice(rg_sb, c * WIDTH, WIDTH))
+                nc.vector.tensor_tensor(result[:, t, :], window, scaled[c][:, t, :], ADD)
+            nc.sync.dma_start(out_rows[:, :, c * WIDTH : (c + 1) * WIDTH], result[:])
 
-        def round_result(copy, c):
-            rounded[c] = held([P, WIDTH, PACK], BF16, "rounded%d" % c)
+        def round_result(copy, c, tag=None):
+            rounded[c] = held([P, WIDTH, PACK], BF16, "rounded%d" % c, tag)
             interleave(copy, rounded[c][:], results[c][:])
 
         out_codes = held([P, S], U32, "out_codes")
@@ -246,35 +263,48 @@ def tile_picked_decode2_relu_po_kernel(
         def store_codes(cols):
             nc.sync.dma_start(out_words[:, cols], out_codes[:, cols].bitcast(I32))
 
-        rows0 = hidden_rows(0, WIDTH, 2)
+        first_products("first", [(0, WIDTH, 0)])
+        first_products("middle", [(0, WIDTH, 1), (0, WIDTH, 2)])
+        first_products("border", [(0, WIDTH, 3), (WIDTH, WIDTH, 0)])
+        for t in range(PACK):
+            relu(0, t)
+        relu(WIDTH, 0)
         pick_scl(nc.vector.tensor_copy, 2, 0)
-        pick_scl(nc.vector.tensor_copy, 3, 0)
-        grouped0 = group_hidden(nc.vector.tensor_copy, 0, rows0)
-        rows1 = hidden_rows(WIDTH, WIDTH, 1)
-        quantise_hidden(0, grouped0)
         pick_scl(nc.vector.tensor_copy, 2, 1)
-        grouped1 = group_hidden(nc.vector.tensor_copy, WIDTH, rows1)
+        pick_scl(nc.vector.tensor_copy, 3, 0)
+        pick_scl(nc.vector.tensor_copy, 3, 1)
+        grouped0 = group_hidden(nc.scalar.copy, 0, rows[0])
+        quantise_hidden(0, grouped0)
+        first_products("middle", [(WIDTH, WIDTH, t) for t in range(1, PACK)])
+        first_products("first", [(HALF, HALF, 0), (HALF, HALF, 1)])
+        first_products("last", [(HALF, HALF, 2), (HALF, HALF, 3)])
+        for t in range(1, PACK):
+            relu(WIDTH, t)
+        grouped1 = group_hidden(nc.vector.tensor_copy, WIDTH, rows[WIDTH])
         scale(0)
         quantise_hidden(WIDTH, grouped1)
-        rows2 = hidden_rows(HALF, HALF, 2)
-        grouped2 = group_hidden(nc.scalar.copy, HALF, rows2)
-        shift(0)
+        for t in range(PACK):
+            relu(HALF, t)
+        grouped2 = group_hidden(nc.scalar.copy, HALF, rows[HALF])
+        shift(0, held([P, PACK, WIDTH], F32, "result0"))
         scale(1)
         quantise_hidden(HALF, grouped2)
-        shift(1, tag="h_rows%d" % HALF)
-        pick_scl(scalar_gather, 3, 1)
-        shf_late = held([P, PACK, HALF], F32, "shf_late")
+        shift(1, placed([P, PACK, WIDTH], F32, "result1", LAST_ROWS_AT - PLANE // 2))
+        shf_third = placed([P, AHEAD, WIDTH], F32, "shf_third", LAST_ROWS_AT + PLANE // 2)
+        for t in range(AHEAD):
+            scalar_gather(shf_third[:, t, :], shf_sb[t][:].indirect(list_slice(rg_sb, HALF, WIDTH)))
+        shf_last = held([P, PACK, WIDTH], F32, "shf_last", "h_grouped%d" % HALF)
         for t in range(PACK):
-            scalar_gather(shf_late[:, t, :], shf_sb[t][:].indirect(list_slice(rg_sb, HALF, HALF)))
+            scalar_gather(shf_last[:, t, :], shf_sb[t][:].indirect(list_slice(rg_sb, S - WIDTH, WIDTH)))
         scale(2)
         scale(3)
-        shift(2, shf_late[:, :, :WIDTH])
-        round_result(nc.scalar.copy, 0)
+        shift(2, held([P, PACK, WIDTH], F32, "result2"), shf_third[:])
+        shift(3, held([P, PACK, WIDTH], F32, "result3"), shf_last[:])
+        round_result(nc.scalar.copy, 0, "h_codes%d" % HALF)
         quantise_result(0)
-        shift(3, shf_late[:, :, WIDTH:])
+        round_result(nc.vector.tensor_copy, 3)
         round_result(nc.scalar.copy, 1)
         quantise_result(1)
-        round_result(nc.vector.tensor_copy, 3)
         round_result(nc.scalar.copy, 2)
         quantise_result(2)
         store_codes(slice(0, S - WIDTH))

@@ -24,7 +24,6 @@ BLOCK = 8
 LIST = 16
 HALF = 256
 WIDTH = 128
-AHEAD = 2
 CLEARED_BY_VECTOR = 3 * T // 4
 
 PLANE = 4 * U
@@ -290,8 +289,8 @@ def tile_picked_decode2_relu_po_kernel(
         scale(1)
         quantise_hidden(HALF, grouped2)
         shift(1, placed([P, PACK, WIDTH], F32, "result1", LAST_ROWS_AT - PLANE // 2))
-        shf_third = placed([P, AHEAD, WIDTH], F32, "shf_third", LAST_ROWS_AT + PLANE // 2)
-        for t in range(AHEAD):
+        shf_third = placed([P, PACK, WIDTH], F32, "shf_third", LAST_ROWS_AT + PLANE // 2)
+        for t in range(PACK):
             scalar_gather(shf_third[:, t, :], shf_sb[t][:].indirect(list_slice(rg_sb, HALF, WIDTH)))
         shf_last = held([P, PACK, WIDTH], F32, "shf_last", "h_grouped%d" % HALF)
         for t in range(PACK):
@@ -303,7 +302,8 @@ def tile_picked_decode2_relu_po_kernel(
         round_result(nc.scalar.copy, 0, "h_codes%d" % HALF)
         quantise_result(0)
         round_result(nc.vector.tensor_copy, 3)
-        round_result(nc.scalar.copy, 1)
+        rounded[1] = held([P, WIDTH, PACK], BF16, "rounded1")
+        nc.gpsimd.tensor_scalar(rounded[1][:], results[1][:].rearrange("p t c -> p c t"), 1.0, 0.0, MULT, ADD)
         quantise_result(1)
         round_result(nc.scalar.copy, 2)
         quantise_result(2)

@@ -80,14 +80,14 @@ def tile_picked_decode2_relu_po_kernel(
         scl_rows = scl.rearrange("(p t) u -> t p u", t=PACK)
         shf_rows = shf.rearrange("(p t) u -> t p u", t=PACK)
 
-        nc.sync.dma_start(rg_sb[:], rg)
-        nc.sync.dma_start(scl_sb[0][:], scl_rows[0])
-        nc.sync.dma_start(offs_sb[:], offs)
-        nc.sync.dma_start(xs_table[0:P:BLOCK, :].bitcast(I32), xs_rows)
         nc.sync.dma_start(w1_raw[:], w1_rows)
+        nc.sync.dma_start(offs_sb[:], offs)
+        nc.sync.dma_start(rg_sb[:], rg)
+        nc.sync.dma_start(b1_sb[:], b1.rearrange("(p t) o -> p (t o)", t=PACK))
+        nc.sync.dma_start(xs_table[0:P:BLOCK, :].bitcast(I32), xs_rows)
+        nc.sync.dma_start(scl_sb[0][:], scl_rows[0])
         nc.sync.dma_start(scl_sb[1][:], scl_rows[1])
         nc.sync.dma_start(xw_table[:], x_words[0].rearrange("p n t -> p (n t)").bitcast(I32))
-        nc.sync.dma_start(b1_sb[:], b1.rearrange("(p t) o -> p (t o)", t=PACK))
         nc.sync.dma_start(scl_sb[2][:], scl_rows[2])
 
         w2s_raw = held([P, N], U8, "w2s_raw")
@@ -104,8 +104,6 @@ def tile_picked_decode2_relu_po_kernel(
             window = scl_sb[t][:].indirect(list_slice(rg_sb, half * HALF, HALF))
             gather(scl_picked[pair, half][:, t % 2, :], window)
 
-        for half in range(2):
-            pick_scl(nc.vector.tensor_copy, 0, half)
 
         xs_picked = held([P, S], U8, "xs_picked")
         nc.vector.tensor_copy(xs_picked[:], xs_table[:].indirect(offs_sb[:]))
@@ -135,7 +133,9 @@ def tile_picked_decode2_relu_po_kernel(
                 scales=w1_scales[:, code_cols],
                 in_=w1_grouped[pair][:].rearrange("p t m j -> p (t m j)"),
             )
-            pick_scl(scalar_gather if pair else nc.vector.tensor_copy, 1, pair)
+            pick_scl(nc.vector.tensor_copy, pair, 0)
+        for t in range(2):
+            pick_scl(scalar_gather, t, 1)
 
         scl_sb.append(placed([P, U], F32, "scl_sb3", ROUNDED_W1_AT))
         nc.sync.dma_start(scl_sb[3][:], scl_rows[3])

@@ -265,10 +265,10 @@ def tile_picked_decode2_relu_po_kernel(
         first_products("first", [(0, WIDTH, 0)])
         first_products("middle", [(0, WIDTH, 1), (0, WIDTH, 2)])
         first_products("border", [(0, WIDTH, 3), (WIDTH, WIDTH, 0)])
+        pick_scl(scalar_gather, 2, 0)
         for t in range(PACK):
             relu(0, t)
         relu(WIDTH, 0)
-        pick_scl(nc.vector.tensor_copy, 2, 0)
         pick_scl(nc.vector.tensor_copy, 2, 1)
         pick_scl(nc.vector.tensor_copy, 3, 0)
         pick_scl(nc.vector.tensor_copy, 3, 1)

@@ -194,13 +194,13 @@ def tile_picked_decode2_relu_po_kernel(
 
         def group_hidden(copy, start, rows):
             grouped = held([P, rows.shape[2], PACK], BF16, "h_grouped%d" % start)
-            interleave(copy, grouped[:], rows[:])
+            interleave(copy, grouped[:], rows)
             return grouped
 
         def quantise_hidden(start, grouped):
             width = grouped.shape[1]
             cols = slice(start, start + width)
-            codes = held([P, width], U32, "h_codes%d" % start, "h_codes%d" % width)
+            codes = held([P, width], U32, "h_codes%d" % start, "h_codes" if start < HALF else None)
             for at in range(0, width, WIDTH):
                 h_codes[(start + at) // WIDTH] = codes[:, at : at + WIDTH]
             nc.vector.quantize_mx(
@@ -272,34 +272,36 @@ def tile_picked_decode2_relu_po_kernel(
         pick_scl(nc.vector.tensor_copy, 2, 1)
         pick_scl(nc.vector.tensor_copy, 3, 0)
         pick_scl(nc.vector.tensor_copy, 3, 1)
-        grouped0 = group_hidden(nc.scalar.copy, 0, rows[0])
+        grouped0 = group_hidden(nc.scalar.copy, 0, rows[0][:])
         quantise_hidden(0, grouped0)
         first_products("middle", [(WIDTH, WIDTH, t) for t in range(1, PACK)])
         first_products("first", [(HALF, HALF, 0), (HALF, HALF, 1)])
         first_products("last", [(HALF, HALF, 2), (HALF, HALF, 3)])
         for t in range(1, PACK):
             relu(WIDTH, t)
-        grouped1 = group_hidden(nc.vector.tensor_copy, WIDTH, rows[WIDTH])
+        grouped1 = group_hidden(nc.vector.tensor_copy, WIDTH, rows[WIDTH][:])
         scale(0)
         quantise_hidden(WIDTH, grouped1)
         for t in range(PACK):
             relu(HALF, t)
-        grouped2 = group_hidden(nc.scalar.copy, HALF, rows[HALF])
+        grouped2 = group_hidden(nc.scalar.copy, HALF, rows[HALF][:, :, :WIDTH])
+        grouped3 = group_hidden(nc.scalar.copy, S - WIDTH, rows[HALF][:, :, WIDTH:])
         shift(0, held([P, PACK, WIDTH], F32, "result0"))
         scale(1)
         quantise_hidden(HALF, grouped2)
+        quantise_hidden(S - WIDTH, grouped3)
         shift(1, placed([P, PACK, WIDTH], F32, "result1", LAST_ROWS_AT - PLANE // 2))
-        shf_third = placed([P, PACK, WIDTH], F32, "shf_third", LAST_ROWS_AT + PLANE // 2)
-        for t in range(PACK):
+        shf_third = held([P, PACK - 1, WIDTH], F32, "shf_third", "scaled0")
+        for t in range(PACK - 1):
             scalar_gather(shf_third[:, t, :], shf_sb[t][:].indirect(list_slice(rg_sb, HALF, WIDTH)))
-        shf_last = held([P, PACK, WIDTH], F32, "shf_last", "h_grouped%d" % HALF)
+        shf_last = held([P, PACK, WIDTH], F32, "shf_last", "h_grouped%d" % (S - WIDTH))
         for t in range(PACK):
             scalar_gather(shf_last[:, t, :], shf_sb[t][:].indirect(list_slice(rg_sb, S - WIDTH, WIDTH)))
         scale(2)
         scale(3)
         shift(2, held([P, PACK, WIDTH], F32, "result2"), shf_third[:])
         shift(3, held([P, PACK, WIDTH], F32, "result3"), shf_last[:])
-        round_result(nc.scalar.copy, 0, "h_codes%d" % HALF)
+        round_result(nc.scalar.copy, 0, "h_codes%d" % (S - WIDTH))
         quantise_result(0)
         round_result(nc.vector.tensor_copy, 3)
         rounded[1] = held([P, WIDTH, PACK], BF16, "rounded1")

@@ -151,15 +151,17 @@ def tile_picked_decode2_relu_po_kernel(
             )
 
         w2_codes = held([P, N], I32, "w2_codes")
-        w2_plane = held([P, N], U8, "w2_plane", "xs_picked")
+        w2_plane = held([P, N], U8, "w2_plane")
         nc.gpsimd.tensor_copy(
             w2_plane[:].rearrange("p (t m) -> p t m", t=PACK),
             w2s_raw[:].rearrange("p (m t) -> p t m", t=PACK),
         )
-        nc.gpsimd.tensor_copy(
-            w2_codes[:].rearrange("p (t m) -> p t m", t=PACK),
-            w2w_raw[:].rearrange("p (m t) -> p t m", t=PACK),
-        )
+        for pair in range(2):
+            planes = slice(2 * pair, 2 * pair + 2)
+            nc.gpsimd.tensor_copy(
+                w2_codes[:].rearrange("p (t m) -> p t m", t=PACK)[:, planes, :],
+                w2w_raw[:].rearrange("p (m t) -> p t m", t=PACK)[:, planes, :],
+            )
 
         h_codes = {}
         h_scales = held([P, S], U8, "h_scales")

@@ -28,9 +28,7 @@ CLEARED_BY_VECTOR = 3 * T // 4
 
 PLANE = 4 * U
 W1_AT = 0
-ROUNDED_W1_AT = W1_AT + PACK * PLANE
-SCALE_TABLE_AT = ROUNDED_W1_AT + 2 * PLANE
-LAST_ROWS_AT = SCALE_TABLE_AT + 2 * PLANE
+ROUNDED_W1_AT = (W1_AT + PACK * PLANE, W1_AT + (PACK + 1) * PLANE)
 
 
 def tile_picked_decode2_relu_po_kernel(
@@ -51,8 +49,8 @@ def tile_picked_decode2_relu_po_kernel(
         def scalar_gather(out, window):
             nc.scalar.activation(out, window, COPY)
 
-        def list_slice(lists, start, count):
-            return lists[:, start // LIST : (start + count) // LIST]
+        def looked_up(table, lists, start, count):
+            return table.indirect(lists[:, start // LIST : (start + count) // LIST])
 
         def interleave(copy, grouped, planes):
             copy(
@@ -60,9 +58,20 @@ def tile_picked_decode2_relu_po_kernel(
                 planes.rearrange("p t (c i) -> p c t i", i=4),
             )
 
+        def product(out, codes, plane, t, moving, moving_scales):
+            nc.tensor.matmul_mx(
+                out=out,
+                lhsT=codes[:, t * P : (t + 1) * P].bitcast(FP8X4),
+                lhsT_scale=plane[:, t * P : (t + 1) * P],
+                rhs=moving.bitcast(FP8X4),
+                rhs_scale=moving_scales,
+                start=True,
+                stop=True,
+            )
+
         offs_sb = held([P, S // LIST], U16, "offs_sb")
         rg_sb = held([P, S // LIST], U16, "rg_sb")
-        xs_table = placed([P, T], U8, "xs_table", SCALE_TABLE_AT)
+        xs_table = held([P, T], U8, "xs_table")
         xw_table = held([P, T], I32, "xw_table")
         w1_raw = placed([P, PACK, H], F32, "w1_raw", W1_AT)
         b1_sb = held([P, PACK], F32, "b1_sb")
@@ -74,17 +83,15 @@ def tile_picked_decode2_relu_po_kernel(
         xs_plane = held([P, S], U8, "xs_plane")
         nc.vector.memset(xs_plane[:].bitcast(I32), 0)
 
-        xs_rows = x_scales[0].bitcast(I32)
         w2s_rows = w2_scales[0].bitcast(I32).rearrange("(q b) c -> b q c", b=PACK)
-        w1_rows = w1.rearrange("(p j) c -> p j c", j=PACK)
         scl_rows = scl.rearrange("(p t) u -> t p u", t=PACK)
         shf_rows = shf.rearrange("(p t) u -> t p u", t=PACK)
 
-        nc.sync.dma_start(w1_raw[:], w1_rows)
+        nc.sync.dma_start(w1_raw[:], w1.rearrange("(p j) c -> p j c", j=PACK))
         nc.sync.dma_start(offs_sb[:], offs)
         nc.sync.dma_start(rg_sb[:], rg)
         nc.sync.dma_start(b1_sb[:], b1.rearrange("(p t) o -> p (t o)", t=PACK))
-        nc.sync.dma_start(xs_table[0:P:BLOCK, :].bitcast(I32), xs_rows)
+        nc.sync.dma_start(xs_table[0:P:BLOCK, :].bitcast(I32), x_scales[0].bitcast(I32))
         nc.sync.dma_start(scl_sb[0][:], scl_rows[0])
         nc.sync.dma_start(scl_sb[1][:], scl_rows[1])
         nc.sync.dma_start(xw_table[:], x_words[0].rearrange("p n t -> p (n t)").bitcast(I32))
@@ -95,16 +102,6 @@ def tile_picked_decode2_relu_po_kernel(
         for b in range(PACK):
             nc.gpsimd.dma_start(w2s_raw[b:P:QUADRANT, :].bitcast(I32), w2s_rows[b])
 
-        scl_picked = {}
-
-        def pick_scl(gather, t, half, tag=None):
-            pair = t // 2
-            if (pair, half) not in scl_picked:
-                scl_picked[pair, half] = held([P, 2, HALF], F32, "scl_picked%d_%d" % (pair, half), tag)
-            window = scl_sb[t][:].indirect(list_slice(rg_sb, half * HALF, HALF))
-            gather(scl_picked[pair, half][:, t % 2, :], window)
-
-
         xs_picked = held([P, S], U8, "xs_picked")
         nc.vector.tensor_copy(xs_picked[:], xs_table[:].indirect(offs_sb[:]))
         for b in range(PACK):
@@ -112,42 +109,49 @@ def tile_picked_decode2_relu_po_kernel(
                 xs_plane[b:P:QUADRANT, :].bitcast(I32), xs_picked[BLOCK * b : P : QUADRANT, :].bitcast(I32)
             )
 
-        w2w_raw = placed([P, N], I32, "w2w_raw", SCALE_TABLE_AT)
-        nc.sync.dma_start(w2w_raw[:], w2_words[0].rearrange("p n t -> p (n t)").bitcast(I32))
-
         w1_codes = held([P, H], U32, "w1_codes")
         w1_scales = held([P, H], U8, "w1_scales")
         w1_grouped = []
-        for pair, copy in enumerate((nc.scalar.copy, nc.scalar.copy)):
+        for pair in range(2):
             w1_grouped.append(
-                placed([P, 2, P, PACK], BF16, "w1_grouped%d" % pair, ROUNDED_W1_AT + pair * PLANE)
+                placed([P, 2, P, PACK], BF16, "w1_grouped%d" % pair, ROUNDED_W1_AT[pair])
             )
-            copy(
+            nc.scalar.copy(
                 w1_grouped[pair][:].rearrange("p t m j -> p m j t"),
                 w1_raw[:].rearrange("p j (m t) -> p m j t", t=PACK)[:, :, :, 2 * pair : 2 * pair + 2],
             )
-        for pair in range(2):
+
+        def quantise_w1(pair):
             code_cols = slice(2 * pair * P, 2 * (pair + 1) * P)
             nc.vector.quantize_mx(
                 out=w1_codes[:, code_cols].bitcast(FP8X4),
                 scales=w1_scales[:, code_cols],
                 in_=w1_grouped[pair][:].rearrange("p t m j -> p (t m j)"),
             )
-            pick_scl(nc.vector.tensor_copy, pair, 0)
-        for t in range(2):
-            pick_scl(scalar_gather, t, 1)
 
-        scl_sb.append(placed([P, U], F32, "scl_sb3", ROUNDED_W1_AT))
+        scl_first = held([P, PACK - 1, HALF], F32, "scl_first")
+        scl_second = [held([P, PACK - 1, HALF], F32, "scl_second0")]
+
+        for pair in range(2):
+            nc.vector.tensor_copy(scl_first[:, pair, :], looked_up(scl_sb[pair][:], rg_sb, 0, HALF))
+            quantise_w1(pair)
+        for t in range(PACK - 1):
+            scalar_gather(scl_second[0][:, t, :], looked_up(scl_sb[t][:], rg_sb, HALF, HALF))
+
+        w2w_raw = placed([P, N], I32, "w2w_raw", ROUNDED_W1_AT[0])
+        nc.sync.dma_start(w2w_raw[:], w2_words[0].rearrange("p n t -> p (n t)").bitcast(I32))
+        scl_sb.append(placed([P, U], F32, "scl_sb3", W1_AT))
         nc.sync.dma_start(scl_sb[3][:], scl_rows[3])
         shf_sb = []
         for t in range(PACK):
-            shf_sb.append(placed([P, U], F32, "shf_sb%d" % t, W1_AT + t * PLANE))
+            at = W1_AT + (t + 1) * PLANE if t < PACK - 1 else ROUNDED_W1_AT[1]
+            shf_sb.append(placed([P, U], F32, "shf_sb%d" % t, at))
             nc.sync.dma_start(shf_sb[t][:], shf_rows[t])
 
         xw_picked = [held([P, HALF], U32, "xw_picked%d" % half) for half in range(2)]
         for half in range(2):
             nc.vector.tensor_copy(
-                xw_picked[half][:], xw_table[:].bitcast(U32).indirect(list_slice(offs_sb, half * HALF, HALF))
+                xw_picked[half][:], looked_up(xw_table[:].bitcast(U32), offs_sb, half * HALF, HALF)
             )
 
         w2_codes = held([P, N], I32, "w2_codes")
@@ -156,59 +160,39 @@ def tile_picked_decode2_relu_po_kernel(
             w2_plane[:].rearrange("p (t m) -> p t m", t=PACK),
             w2s_raw[:].rearrange("p (m t) -> p t m", t=PACK),
         )
-        for pair in range(2):
-            planes = slice(2 * pair, 2 * pair + 2)
-            nc.gpsimd.tensor_copy(
-                w2_codes[:].rearrange("p (t m) -> p t m", t=PACK)[:, planes, :],
-                w2w_raw[:].rearrange("p (m t) -> p t m", t=PACK)[:, planes, :],
-            )
 
-        h_codes = {}
+        def first_products(start, width, planes, tag):
+            bank = psum.tile([P, len(planes), width], F32, name="sums%d_%d" % (start, planes[0]), tag=tag)
+            for i, t in enumerate(planes):
+                for lo, hi in ((start, min(start + width, HALF)), (HALF, start + width)):
+                    if hi > lo:
+                        half, inner = divmod(lo, HALF)
+                        moving = xw_picked[half][:, inner : inner + hi - lo]
+                        out = bank[:, i, lo - start : hi - start]
+                        product(out, w1_codes, w1_scales, t, moving, xs_plane[:, lo:hi])
+            return bank
+
+        def hidden_rows(rows, start, planes, tag):
+            bank = first_products(start, rows.shape[2], planes, tag)
+            for i, t in enumerate(planes):
+                nc.scalar.activation(rows[:, t, :], bank[:, i, :], RELU, bias=b1_sb[:, t : t + 1])
+
         h_scales = held([P, S], U8, "h_scales")
+        h_grouped, h_codes = {}, {}
 
-        sums, rows = {}, {}
+        def group_hidden(start, rows):
+            h_grouped[start] = held([P, rows.shape[2], PACK], BF16, "h_grouped%d" % start)
+            interleave(nc.vector.tensor_copy, h_grouped[start][:], rows)
 
-        def first_products(tag, items):
-            bank = psum.tile([P, 2 * HALF], F32, name="sums%d_%d" % items[0][::2], tag=tag)
-            used = 0
-            for start, width, t in items:
-                half, inner = divmod(start, HALF)
-                sums[start, t] = bank[:, used : used + width]
-                used = used + width
-                nc.tensor.matmul_mx(
-                    out=sums[start, t],
-                    lhsT=w1_codes[:, t * P : (t + 1) * P].bitcast(FP8X4),
-                    lhsT_scale=w1_scales[:, t * P : (t + 1) * P],
-                    rhs=xw_picked[half][:, inner : inner + width].bitcast(FP8X4),
-                    rhs_scale=xs_plane[:, start : start + width],
-                    start=True,
-                    stop=True,
-                )
-
-        def relu(start, t):
-            if t == 0 and start == HALF:
-                rows[start] = placed([P, PACK, HALF], BF16, "h_rows_last", LAST_ROWS_AT)
-            elif t == 0 and start == 0:
-                rows[start] = placed([P, PACK, WIDTH], BF16, "h_rows_first", LAST_ROWS_AT)
-            elif t == 0:
-                rows[start] = held([P, PACK, sums[start, t].shape[1]], BF16, "h_rows%d" % start)
-            nc.scalar.activation(rows[start][:, t, :], sums[start, t], RELU, bias=b1_sb[:, t : t + 1])
-
-        def group_hidden(copy, start, rows):
-            grouped = held([P, rows.shape[2], PACK], BF16, "h_grouped%d" % start)
-            interleave(copy, grouped[:], rows)
-            return grouped
-
-        def quantise_hidden(start, grouped):
-            width = grouped.shape[1]
-            cols = slice(start, start + width)
-            codes = held([P, width], U32, "h_codes%d" % start, "h_codes" if start < HALF else None)
+        def quantise_hidden(start, tag=None):
+            width = h_grouped[start].shape[1]
+            codes = held([P, width], U32, "h_codes%d" % start, tag)
             for at in range(0, width, WIDTH):
                 h_codes[(start + at) // WIDTH] = codes[:, at : at + WIDTH]
             nc.vector.quantize_mx(
                 out=codes[:].bitcast(FP8X4),
-                scales=h_scales[:, cols],
-                in_=grouped[:].rearrange("p c t -> p (c t)"),
+                scales=h_scales[:, start : start + width],
+                in_=h_grouped[start][:].rearrange("p c t -> p (c t)"),
             )
 
         out_scales = held([P, S], U8, "out_scales")
@@ -217,41 +201,52 @@ def tile_picked_decode2_relu_po_kernel(
         out_scale_rows = out_2[0].bitcast(I32).rearrange("(q b) c -> b q c", b=PACK)
         scaled, results, rounded = {}, {}, {}
 
-        def scale(c):
+        def scale(c, parts, first=0):
             cols = slice(c * WIDTH, (c + 1) * WIDTH)
-            half, inner = divmod(c * WIDTH, HALF)
-            scaled[c] = held([P, PACK, WIDTH], F32, "scaled%d" % c)
-            for pair in range(2):
-                y = psum.tile([P, 2, WIDTH], F32, name="y%d_%d" % (c, pair), tag="y%d_%d" % (c % 2, pair))
-                for i in range(2):
-                    t = 2 * pair + i
-                    nc.tensor.matmul_mx(
-                        out=y[:, i, :],
-                        lhsT=w2_codes[:, t * P : (t + 1) * P].bitcast(FP8X4),
-                        lhsT_scale=w2_plane[:, t * P : (t + 1) * P],
-                        rhs=h_codes[c].bitcast(FP8X4),
-                        rhs_scale=h_scales[:, cols],
-                        start=True,
-                        stop=True,
+            inner = c * WIDTH % HALF
+            if first == 0:
+                scaled[c] = held([P, PACK, WIDTH], F32, "scaled%d" % c)
+            for bank_tag, factors in parts:
+                count = sum(picked.shape[1] for picked in factors)
+                y = psum.tile([P, count, WIDTH], F32, name="y%d_%d" % (c, first), tag=bank_tag)
+                for i in range(count):
+                    product(y[:, i, :], w2_codes, w2_plane, first + i, h_codes[c], h_scales[:, cols])
+                at = 0
+                for picked in factors:
+                    count = picked.shape[1]
+                    nc.vector.tensor_tensor(
+                        scaled[c][:, first : first + count, :],
+                        y[:, at : at + count, :],
+                        picked[:, :, inner : inner + WIDTH],
+                        MULT,
                     )
-                picked = scl_picked[pair, half][:, :, inner : inner + WIDTH]
-                nc.vector.tensor_tensor(scaled[c][:, 2 * pair : 2 * pair + 2, :], y[:], picked, MULT)
+                    at = at + count
+                    first = first + count
 
-        def shift(c, result, picked=None):
-            results[c] = result
-            ahead = 0 if picked is None else picked.shape[1]
-            if ahead:
-                nc.vector.tensor_tensor(result[:, :ahead, :], picked, scaled[c][:, :ahead, :], ADD)
-            for t in range(ahead, PACK):
-                window = shf_sb[t][:].indirect(list_slice(rg_sb, c * WIDTH, WIDTH))
-                nc.vector.tensor_tensor(result[:, t, :], window, scaled[c][:, t, :], ADD)
-            nc.sync.dma_start(out_rows[:, :, c * WIDTH : (c + 1) * WIDTH], result[:])
+        def add_plain(c, planes, picked):
+            nc.vector.tensor_tensor(results[c][:, planes, :], picked, scaled[c][:, planes, :], ADD)
 
-        def round_result(copy, c, tag=None):
-            rounded[c] = held([P, WIDTH, PACK], BF16, "rounded%d" % c, tag)
+        def add_looked_up(c, t):
+            window = looked_up(shf_sb[t][:], rg_sb, c * WIDTH, WIDTH)
+            nc.vector.tensor_tensor(results[c][:, t, :], window, scaled[c][:, t, :], ADD)
+
+        def store_result(c):
+            nc.sync.dma_start(out_rows[:, :, c * WIDTH : (c + 1) * WIDTH], results[c][:])
+
+        def shift(c, picked):
+            results[c] = held([P, PACK, WIDTH], F32, "result%d" % c)
+            add_plain(c, slice(0, PACK), picked)
+            store_result(c)
+
+        def pick_shf(start, count, tag):
+            picked = held([P, PACK, count], F32, "shf_picked%d" % start, tag)
+            for t in range(PACK):
+                scalar_gather(picked[:, t, :], looked_up(shf_sb[t][:], rg_sb, start, count))
+            return picked
+
+        def round_result(copy, c):
+            rounded[c] = held([P, WIDTH, PACK], BF16, "rounded%d" % c)
             interleave(copy, rounded[c][:], results[c][:])
-
-        out_codes = held([P, S], U32, "out_codes")
 
         def quantise_result(c):
             cols = slice(c * WIDTH, (c + 1) * WIDTH)
@@ -261,59 +256,58 @@ def tile_picked_decode2_relu_po_kernel(
                 in_=rounded[c][:].rearrange("p c t -> p (c t)"),
             )
 
-        def store_codes(cols):
-            nc.sync.dma_start(out_words[:, cols], out_codes[:, cols].bitcast(I32))
+        rows0 = held([P, PACK, WIDTH], BF16, "h_rows0")
+        rows1 = held([P, PACK, WIDTH], BF16, "h_rows1")
+        rows2 = held([P, PACK, HALF], BF16, "h_rows2")
+        hidden_rows(rows0, 0, [0, 1], "bank0")
+        hidden_rows(rows0, 0, [2, 3], "bank1")
+        hidden_rows(rows1, WIDTH, [0, 1, 2, 3], "bank2")
+        hidden_rows(rows2, HALF, [0, 1], "bank3")
+        hidden_rows(rows2, HALF, [2, 3], "bank4")
 
-        first_products("first", [(0, WIDTH, 0)])
-        first_products("middle", [(0, WIDTH, 1), (0, WIDTH, 2)])
-        first_products("border", [(0, WIDTH, 3), (WIDTH, WIDTH, 0)])
-        pick_scl(scalar_gather, 2, 0)
-        for t in range(PACK):
-            relu(0, t)
-        relu(WIDTH, 0)
-        pick_scl(nc.vector.tensor_copy, 2, 1)
-        pick_scl(nc.vector.tensor_copy, 3, 0)
-        pick_scl(nc.vector.tensor_copy, 3, 1)
-        grouped0 = group_hidden(nc.scalar.copy, 0, rows[0][:])
-        quantise_hidden(0, grouped0)
-        first_products("middle", [(WIDTH, WIDTH, t) for t in range(1, PACK)])
-        first_products("first", [(HALF, HALF, 0), (HALF, HALF, 1)])
-        first_products("last", [(HALF, HALF, 2), (HALF, HALF, 3)])
+        nc.vector.tensor_copy(scl_first[:, 2, :], looked_up(scl_sb[2][:], rg_sb, 0, HALF))
+        nc.vector.tensor_copy(
+            w2_codes[:].rearrange("p (t c i) -> p c t i", t=PACK, i=4),
+            w2w_raw[:].rearrange("p (c i t) -> p c t i", t=PACK, i=4),
+        )
+        group_hidden(0, rows0[:])
+        quantise_hidden(0)
+        scl_last = held([P, 1, HALF], F32, "scl_last", "h_rows0")
+        nc.vector.tensor_copy(scl_last[:, 0, :], looked_up(scl_sb[3][:], rg_sb, 0, HALF))
+        group_hidden(WIDTH, rows1[:])
+        scale(0, [("bank2", [scl_first]), ("bank5", [scl_last])])
+        quantise_hidden(WIDTH, "h_codes0")
+
+        scl_second.append(held([P, 1, HALF], F32, "scl_second1", "h_rows1"))
+        scalar_gather(scl_second[1][:, 0, :], looked_up(scl_sb[3][:], rg_sb, HALF, HALF))
+        shf_second = pick_shf(WIDTH, WIDTH, "xw_picked1")
+        shf_late = pick_shf(HALF, HALF, "h_grouped%d" % WIDTH)
+
+        results[0] = held([P, PACK, WIDTH], F32, "result0", "b1_sb")
+        group_hidden(HALF, rows2[:])
+        add_looked_up(0, 0)
+        quantise_hidden(HALF)
         for t in range(1, PACK):
-            relu(WIDTH, t)
-        grouped1 = group_hidden(nc.vector.tensor_copy, WIDTH, rows[WIDTH][:])
-        scale(0)
-        quantise_hidden(WIDTH, grouped1)
-        for t in range(PACK):
-            relu(HALF, t)
-        grouped2 = group_hidden(nc.scalar.copy, HALF, rows[HALF][:, :, :WIDTH])
-        grouped3 = group_hidden(nc.scalar.copy, S - WIDTH, rows[HALF][:, :, WIDTH:])
-        shift(0, held([P, PACK, WIDTH], F32, "result0"))
-        scale(1)
-        quantise_hidden(HALF, grouped2)
-        quantise_hidden(S - WIDTH, grouped3)
-        shift(1, placed([P, PACK, WIDTH], F32, "result1", LAST_ROWS_AT - PLANE // 2))
-        shf_third = held([P, PACK - 1, WIDTH], F32, "shf_third", "scaled0")
-        for t in range(PACK - 1):
-            scalar_gather(shf_third[:, t, :], shf_sb[t][:].indirect(list_slice(rg_sb, HALF, WIDTH)))
-        shf_last = held([P, PACK, WIDTH], F32, "shf_last", "h_grouped%d" % (S - WIDTH))
-        for t in range(PACK):
-            scalar_gather(shf_last[:, t, :], shf_sb[t][:].indirect(list_slice(rg_sb, S - WIDTH, WIDTH)))
-        scale(2)
-        scale(3)
-        shift(2, held([P, PACK, WIDTH], F32, "result2"), shf_third[:])
-        shift(3, held([P, PACK, WIDTH], F32, "result3"), shf_last[:])
-        round_result(nc.scalar.copy, 0, "h_codes%d" % (S - WIDTH))
+            add_looked_up(0, t)
+        store_result(0)
+        scale(1, [("bank4", [scl_first, scl_last])])
+        scale(2, [("bank6", scl_second)])
+        shift(1, shf_second[:])
+        scale(3, [("bank7", scl_second)])
+        rounded[0] = held([P, WIDTH, PACK], BF16, "rounded0")
+        nc.gpsimd.tensor_scalar(rounded[0][:], results[0][:].rearrange("p t c -> p c t"), 1.0, 0.0, MULT, ADD)
+        round_result(nc.scalar.copy, 1)
+        shift(2, shf_late[:, :, :WIDTH])
+        shift(3, shf_late[:, :, WIDTH:])
+        out_codes = held([P, S], U32, "out_codes", "scaled2")
         quantise_result(0)
-        round_result(nc.vector.tensor_copy, 3)
-        rounded[1] = held([P, WIDTH, PACK], BF16, "rounded1")
-        nc.gpsimd.tensor_scalar(rounded[1][:], results[1][:].rearrange("p t c -> p c t"), 1.0, 0.0, MULT, ADD)
         quantise_result(1)
         round_result(nc.scalar.copy, 2)
+        round_result(nc.vector.tensor_copy, 3)
         quantise_result(2)
-        store_codes(slice(0, S - WIDTH))
+        nc.sync.dma_start(out_words[:, : S - WIDTH], out_codes[:, : S - WIDTH].bitcast(I32))
         quantise_result(3)
-        store_codes(slice(S - WIDTH, S))
+        nc.sync.dma_start(out_words[:, S - WIDTH :], out_codes[:, S - WIDTH :].bitcast(I32))
         for b in range(PACK):
             queue = nc.scalar if b % 2 else nc.sync
             queue.dma_start(out_scale_rows[b], out_scales[b:P:QUADRANT, :].bitcast(I32))

@@ -129,14 +129,14 @@ def tile_picked_decode2_relu_po_kernel(
                 in_=w1_grouped[pair][:].rearrange("p t m j -> p (t m j)"),
             )
 
-        scl_first = held([P, PACK - 1, HALF], F32, "scl_first")
-        scl_second = [held([P, PACK - 1, HALF], F32, "scl_second0")]
+        scl_first = held([P, PACK, HALF], F32, "scl_first")
+        scl_second = held([P, PACK, HALF], F32, "scl_second")
 
         for pair in range(2):
             nc.vector.tensor_copy(scl_first[:, pair, :], looked_up(scl_sb[pair][:], rg_sb, 0, HALF))
             quantise_w1(pair)
         for t in range(PACK - 1):
-            scalar_gather(scl_second[0][:, t, :], looked_up(scl_sb[t][:], rg_sb, HALF, HALF))
+            scalar_gather(scl_second[:, t, :], looked_up(scl_sb[t][:], rg_sb, HALF, HALF))
 
         w2w_raw = placed([P, N], I32, "w2w_raw", ROUNDED_W1_AT[0])
         nc.sync.dma_start(w2w_raw[:], w2_words[0].rearrange("p n t -> p (n t)").bitcast(I32))
@@ -256,44 +256,40 @@ def tile_picked_decode2_relu_po_kernel(
                 in_=rounded[c][:].rearrange("p c t -> p (c t)"),
             )
 
-        rows0 = held([P, PACK, WIDTH], BF16, "h_rows0")
-        rows1 = held([P, PACK, WIDTH], BF16, "h_rows1")
-        rows2 = held([P, PACK, HALF], BF16, "h_rows2")
-        hidden_rows(rows0, 0, [0, 1], "bank0")
-        hidden_rows(rows0, 0, [2, 3], "bank1")
-        hidden_rows(rows1, WIDTH, [0, 1, 2, 3], "bank2")
-        hidden_rows(rows2, HALF, [0, 1], "bank3")
-        hidden_rows(rows2, HALF, [2, 3], "bank4")
+        rows = [held([P, PACK, HALF], BF16, "h_rows%d" % half) for half in range(2)]
+        hidden_rows(rows[0], 0, [0], "bank0")
+        hidden_rows(rows[0], 0, [1], "bank1")
+        hidden_rows(rows[0], 0, [2, 3], "bank2")
+        hidden_rows(rows[1], HALF, [0, 1], "bank3")
+        hidden_rows(rows[1], HALF, [2], "bank4")
+        hidden_rows(rows[1], HALF, [3], "bank5")
 
         nc.vector.tensor_copy(scl_first[:, 2, :], looked_up(scl_sb[2][:], rg_sb, 0, HALF))
         nc.vector.tensor_copy(
             w2_codes[:].rearrange("p (t c i) -> p c t i", t=PACK, i=4),
             w2w_raw[:].rearrange("p (c i t) -> p c t i", t=PACK, i=4),
         )
-        group_hidden(0, rows0[:])
+        nc.vector.tensor_copy(scl_first[:, 3, :], looked_up(scl_sb[3][:], rg_sb, 0, HALF))
+        group_hidden(0, rows[0][:, :, :WIDTH])
+        group_hidden(WIDTH, rows[0][:, :, WIDTH:])
         quantise_hidden(0)
-        scl_last = held([P, 1, HALF], F32, "scl_last", "h_rows0")
-        nc.vector.tensor_copy(scl_last[:, 0, :], looked_up(scl_sb[3][:], rg_sb, 0, HALF))
-        group_hidden(WIDTH, rows1[:])
-        scale(0, [("bank2", [scl_first]), ("bank5", [scl_last])])
-        quantise_hidden(WIDTH, "h_codes0")
+        quantise_hidden(WIDTH)
 
-        scl_second.append(held([P, 1, HALF], F32, "scl_second1", "h_rows1"))
-        scalar_gather(scl_second[1][:, 0, :], looked_up(scl_sb[3][:], rg_sb, HALF, HALF))
+        scalar_gather(scl_second[:, 3, :], looked_up(scl_sb[3][:], rg_sb, HALF, HALF))
         shf_second = pick_shf(WIDTH, WIDTH, "xw_picked1")
         shf_late = pick_shf(HALF, HALF, "h_grouped%d" % WIDTH)
 
-        results[0] = held([P, PACK, WIDTH], F32, "result0", "b1_sb")
-        group_hidden(HALF, rows2[:])
-        add_looked_up(0, 0)
+        group_hidden(HALF, rows[1][:])
+        scale(0, [("bank4", [scl_first])])
         quantise_hidden(HALF)
-        for t in range(1, PACK):
+        results[0] = held([P, PACK, WIDTH], F32, "result0")
+        for t in range(PACK):
             add_looked_up(0, t)
         store_result(0)
-        scale(1, [("bank4", [scl_first, scl_last])])
-        scale(2, [("bank6", scl_second)])
+        scale(1, [("bank5", [scl_first])])
+        scale(2, [("bank6", [scl_second])])
         shift(1, shf_second[:])
-        scale(3, [("bank7", scl_second)])
+        scale(3, [("bank7", [scl_second])])
         rounded[0] = held([P, WIDTH, PACK], BF16, "rounded0")
         nc.gpsimd.tensor_scalar(rounded[0][:], results[0][:].rearrange("p t c -> p c t"), 1.0, 0.0, MULT, ADD)
         round_result(nc.scalar.copy, 1)

@@ -201,11 +201,11 @@ def tile_picked_decode2_relu_po_kernel(
         out_scale_rows = out_2[0].bitcast(I32).rearrange("(q b) c -> b q c", b=PACK)
         scaled, results, rounded = {}, {}, {}
 
-        def scale(c, parts, first=0):
+        def scale(c, parts, tag=None):
             cols = slice(c * WIDTH, (c + 1) * WIDTH)
             inner = c * WIDTH % HALF
-            if first == 0:
-                scaled[c] = held([P, PACK, WIDTH], F32, "scaled%d" % c)
+            scaled[c] = held([P, PACK, WIDTH], F32, "scaled%d" % c, tag)
+            first = 0
             for bank_tag, factors in parts:
                 count = sum(picked.shape[1] for picked in factors)
                 y = psum.tile([P, count, WIDTH], F32, name="y%d_%d" % (c, first), tag=bank_tag)
@@ -277,10 +277,10 @@ def tile_picked_decode2_relu_po_kernel(
 
         scalar_gather(scl_second[:, 3, :], looked_up(scl_sb[3][:], rg_sb, HALF, HALF))
         shf_second = pick_shf(WIDTH, WIDTH, "xw_picked1")
-        shf_late = pick_shf(HALF, HALF, "h_grouped%d" % WIDTH)
 
         group_hidden(HALF, rows[1][:])
-        scale(0, [("bank4", [scl_first])])
+        shf_late = pick_shf(HALF, HALF, "h_rows1")
+        scale(0, [("bank0", [scl_first])], "b1_sb")
         quantise_hidden(HALF)
         results[0] = held([P, PACK, WIDTH], F32, "result0")
         for t in range(PACK):

@@ -26,6 +26,7 @@ HALF = 256
 WIDTH = 128
 CLEARED_BY_VECTOR = 3 * T // 4
 
+ALIGN = 256
 PLANE = 4 * U
 W1_AT = 0
 ROUNDED_W1_AT = (W1_AT + PACK * PLANE, W1_AT + (PACK + 1) * PLANE)
@@ -41,10 +42,10 @@ def tile_picked_decode2_relu_po_kernel(
         psum = ctx.enter_context(tc.psum_pool(name="psum", bufs=1))
 
         def held(shape, dtype, name, tag=None):
-            return keep.tile(shape, dtype, name=name, tag=tag or name, align_bytes=64)
+            return keep.tile(shape, dtype, name=name, tag=tag or name, align_bytes=ALIGN)
 
         def placed(shape, dtype, name, offset):
-            return shared.tile(shape, dtype, name=name, align_bytes=64, offset=offset)
+            return shared.tile(shape, dtype, name=name, align_bytes=ALIGN, offset=offset)
 
         def scalar_gather(out, window):
             nc.scalar.activation(out, window, COPY)
@@ -144,7 +145,7 @@ def tile_picked_decode2_relu_po_kernel(
         nc.sync.dma_start(scl_sb[3][:], scl_rows[3])
         shf_sb = []
         for t in range(PACK):
-            at = W1_AT + (t + 1) * PLANE if t < PACK - 1 else ROUNDED_W1_AT[1]
+            at = W1_AT + (t + 1) * PLANE if t < PACK - 1 else ROUNDED_W1_AT[1] + N
             shf_sb.append(placed([P, U], F32, "shf_sb%d" % t, at))
             nc.sync.dma_start(shf_sb[t][:], shf_rows[t])
 
@@ -155,7 +156,7 @@ def tile_picked_decode2_relu_po_kernel(
             )
 
         w2_codes = held([P, N], I32, "w2_codes")
-        w2_plane = held([P, N], U8, "w2_plane")
+        w2_plane = placed([P, N], U8, "w2_plane", ROUNDED_W1_AT[1])
         nc.gpsimd.tensor_copy(
             w2_plane[:].rearrange("p (t m) -> p t m", t=PACK),
             w2s_raw[:].rearrange("p (m t) -> p t m", t=PACK),
@@ -235,12 +236,15 @@ def tile_picked_decode2_relu_po_kernel(
 
         def shift(c, picked):
             results[c] = held([P, PACK, WIDTH], F32, "result%d" % c)
-            add_plain(c, slice(0, PACK), picked)
+            ahead = picked.shape[1]
+            add_plain(c, slice(0, ahead), picked)
+            for t in range(ahead, PACK):
+                add_looked_up(c, t)
             store_result(c)
 
-        def pick_shf(start, count, tag):
-            picked = held([P, PACK, count], F32, "shf_picked%d" % start, tag)
-            for t in range(PACK):
+        def pick_shf(start, count, tag, planes=PACK):
+            picked = held([P, planes, count], F32, "shf_picked%d" % start, tag)
+            for t in range(planes):
                 scalar_gather(picked[:, t, :], looked_up(shf_sb[t][:], rg_sb, start, count))
             return picked
 
@@ -276,20 +280,17 @@ def tile_picked_decode2_relu_po_kernel(
         quantise_hidden(WIDTH)
 
         scalar_gather(scl_second[:, 3, :], looked_up(scl_sb[3][:], rg_sb, HALF, HALF))
-        shf_second = pick_shf(WIDTH, WIDTH, "xw_picked1")
+        shf_first = pick_shf(0, HALF, "xw_picked1", 2)
 
         group_hidden(HALF, rows[1][:])
         shf_late = pick_shf(HALF, HALF, "h_rows1")
         scale(0, [("bank0", [scl_first])], "b1_sb")
         quantise_hidden(HALF)
-        results[0] = held([P, PACK, WIDTH], F32, "result0")
-        for t in range(PACK):
-            add_looked_up(0, t)
-        store_result(0)
         scale(1, [("bank5", [scl_first])])
+        shift(0, shf_first[:, :, :WIDTH])
         scale(2, [("bank6", [scl_second])])
-        shift(1, shf_second[:])
         scale(3, [("bank7", [scl_second])])
+        shift(1, shf_first[:, :, WIDTH:])
         rounded[0] = held([P, WIDTH, PACK], BF16, "rounded0")
         nc.gpsimd.tensor_scalar(rounded[0][:], results[0][:].rearrange("p t c -> p c t"), 1.0, 0.0, MULT, ADD)
         round_result(nc.scalar.copy, 1)

@@ -139,10 +139,10 @@ def tile_picked_decode2_relu_po_kernel(
         for t in range(PACK - 1):
             scalar_gather(scl_second[:, t, :], looked_up(scl_sb[t][:], rg_sb, HALF, HALF))
 
-        w2w_raw = placed([P, N], I32, "w2w_raw", ROUNDED_W1_AT[0])
-        nc.sync.dma_start(w2w_raw[:], w2_words[0].rearrange("p n t -> p (n t)").bitcast(I32))
-        scl_sb.append(placed([P, U], F32, "scl_sb3", W1_AT))
+        scl_sb.append(placed([P, U], F32, "scl_sb3", ROUNDED_W1_AT[0]))
         nc.sync.dma_start(scl_sb[3][:], scl_rows[3])
+        w2w_raw = placed([P, N], I32, "w2w_raw", W1_AT)
+        nc.sync.dma_start(w2w_raw[:], w2_words[0].rearrange("p n t -> p (n t)").bitcast(I32))
         shf_sb = []
         for t in range(PACK):
             at = W1_AT + (t + 1) * PLANE if t < PACK - 1 else ROUNDED_W1_AT[1] + N
@@ -268,12 +268,12 @@ def tile_picked_decode2_relu_po_kernel(
         hidden_rows(rows[1], HALF, [2], "bank4")
         hidden_rows(rows[1], HALF, [3], "bank5")
 
-        nc.vector.tensor_copy(scl_first[:, 2, :], looked_up(scl_sb[2][:], rg_sb, 0, HALF))
+        for t in range(2, PACK):
+            nc.vector.tensor_copy(scl_first[:, t, :], looked_up(scl_sb[t][:], rg_sb, 0, HALF))
         nc.vector.tensor_copy(
             w2_codes[:].rearrange("p (t c i) -> p c t i", t=PACK, i=4),
             w2w_raw[:].rearrange("p (c i t) -> p c t i", t=PACK, i=4),
         )
-        nc.vector.tensor_copy(scl_first[:, 3, :], looked_up(scl_sb[3][:], rg_sb, 0, HALF))
         group_hidden(0, rows[0][:, :, :WIDTH])
         group_hidden(WIDTH, rows[0][:, :, WIDTH:])
         quantise_hidden(0)
@@ -287,18 +287,18 @@ def tile_picked_decode2_relu_po_kernel(
         scale(0, [("bank0", [scl_first])], "b1_sb")
         quantise_hidden(HALF)
         scale(1, [("bank5", [scl_first])])
-        shift(0, shf_first[:, :, :WIDTH])
+        for c in range(2):
+            shift(c, shf_first[:, :, c * WIDTH : (c + 1) * WIDTH])
         scale(2, [("bank6", [scl_second])])
         scale(3, [("bank7", [scl_second])])
-        shift(1, shf_first[:, :, WIDTH:])
-        rounded[0] = held([P, WIDTH, PACK], BF16, "rounded0")
-        nc.gpsimd.tensor_scalar(rounded[0][:], results[0][:].rearrange("p t c -> p c t"), 1.0, 0.0, MULT, ADD)
-        round_result(nc.scalar.copy, 1)
+        rounded[1] = held([P, WIDTH, PACK], BF16, "rounded1")
+        nc.gpsimd.tensor_scalar(rounded[1][:], results[1][:].rearrange("p t c -> p c t"), 1.0, 0.0, MULT, ADD)
+        round_result(nc.scalar.copy, 0)
         shift(2, shf_late[:, :, :WIDTH])
         shift(3, shf_late[:, :, WIDTH:])
         out_codes = held([P, S], U32, "out_codes", "scaled2")
-        quantise_result(0)
         quantise_result(1)
+        quantise_result(0)
         round_result(nc.scalar.copy, 2)
         round_result(nc.vector.tensor_copy, 3)
         quantise_result(2)

@@ -75,7 +75,8 @@ def tile_picked_decode2_relu_po_kernel(
         xs_table = held([P, T], U8, "xs_table")
         xw_table = held([P, T], I32, "xw_table")
         w1_raw = placed([P, PACK, H], F32, "w1_raw", W1_AT)
-        b1_sb = held([P, PACK], F32, "b1_sb")
+        scl_second = held([P, PACK, HALF], F32, "scl_second")
+        b1_sb = scl_second[:, PACK - 1, :PACK]
         scl_sb = [held([P, U], F32, "scl_sb%d" % t) for t in range(PACK - 1)]
 
         nc.vector.memset(xs_table[:, :CLEARED_BY_VECTOR].bitcast(I32), 0)
@@ -91,7 +92,7 @@ def tile_picked_decode2_relu_po_kernel(
         nc.sync.dma_start(w1_raw[:], w1.rearrange("(p j) c -> p j c", j=PACK))
         nc.sync.dma_start(offs_sb[:], offs)
         nc.sync.dma_start(rg_sb[:], rg)
-        nc.sync.dma_start(b1_sb[:], b1.rearrange("(p t) o -> p (t o)", t=PACK))
+        nc.sync.dma_start(b1_sb, b1.rearrange("(p t) o -> p (t o)", t=PACK))
         nc.sync.dma_start(xs_table[0:P:BLOCK, :].bitcast(I32), x_scales[0].bitcast(I32))
         nc.sync.dma_start(scl_sb[0][:], scl_rows[0])
         nc.sync.dma_start(scl_sb[1][:], scl_rows[1])
@@ -131,7 +132,6 @@ def tile_picked_decode2_relu_po_kernel(
             )
 
         scl_first = held([P, PACK, HALF], F32, "scl_first")
-        scl_second = held([P, PACK, HALF], F32, "scl_second")
 
         for pair in range(2):
             nc.vector.tensor_copy(scl_first[:, pair, :], looked_up(scl_sb[pair][:], rg_sb, 0, HALF))
@@ -234,8 +234,8 @@ def tile_picked_decode2_relu_po_kernel(
         def store_result(c):
             nc.sync.dma_start(out_rows[:, :, c * WIDTH : (c + 1) * WIDTH], results[c][:])
 
-        def shift(c, picked):
-            results[c] = held([P, PACK, WIDTH], F32, "result%d" % c)
+        def shift(c, picked, tag=None):
+            results[c] = held([P, PACK, WIDTH], F32, "result%d" % c, tag)
             ahead = picked.shape[1]
             add_plain(c, slice(0, ahead), picked)
             for t in range(ahead, PACK):
@@ -279,16 +279,17 @@ def tile_picked_decode2_relu_po_kernel(
         quantise_hidden(0)
         quantise_hidden(WIDTH)
 
-        scalar_gather(scl_second[:, 3, :], looked_up(scl_sb[3][:], rg_sb, HALF, HALF))
-        shf_first = pick_shf(0, HALF, "xw_picked1", 2)
+        nc.vector.tensor_copy(scl_second[:, 3, :], looked_up(scl_sb[3][:], rg_sb, HALF, HALF))
+        shf_first = pick_shf(0, HALF, "h_grouped%d" % WIDTH, 3)
 
-        group_hidden(HALF, rows[1][:])
-        shf_late = pick_shf(HALF, HALF, "h_rows1")
-        scale(0, [("bank0", [scl_first])], "b1_sb")
-        quantise_hidden(HALF)
+        h_grouped[HALF] = held([P, HALF, PACK], BF16, "h_grouped%d" % HALF)
+        nc.gpsimd.tensor_scalar(h_grouped[HALF][:], rows[1][:].rearrange("p t c -> p c t"), 1.0, 0.0, MULT, ADD)
+        scale(0, [("bank4", [scl_first])])
         scale(1, [("bank5", [scl_first])])
-        for c in range(2):
-            shift(c, shf_first[:, :, c * WIDTH : (c + 1) * WIDTH])
+        shf_late = pick_shf(HALF, HALF, "h_codes%d" % WIDTH)
+        quantise_hidden(HALF)
+        shift(0, shf_first[:, :, :WIDTH], "h_rows1")
+        shift(1, shf_first[:, :, WIDTH:], "h_grouped%d" % HALF)
         scale(2, [("bank6", [scl_second])])
         scale(3, [("bank7", [scl_second])])
         rounded[1] = held([P, WIDTH, PACK], BF16, "rounded1")

@@ -19,14 +19,16 @@ COPY = mybir.ActivationFunctionType.Copy
 
 P = 128
 PACK = 4
+LAST = PACK - 1
 QUADRANT = 32
 BLOCK = 8
 LIST = 16
 HALF = 256
 WIDTH = 128
+RUN = 4
 CLEARED_BY_VECTOR = 3 * T // 4
-
 ALIGN = 256
+
 PLANE = 4 * U
 W1_AT = 0
 ROUNDED_W1_AT = (W1_AT + PACK * PLANE, W1_AT + (PACK + 1) * PLANE)
@@ -41,8 +43,8 @@ def tile_picked_decode2_relu_po_kernel(
         shared = ctx.enter_context(tc.tile_pool(name="shared", bufs=1))
         psum = ctx.enter_context(tc.psum_pool(name="psum", bufs=1))
 
-        def held(shape, dtype, name, tag=None):
-            return keep.tile(shape, dtype, name=name, tag=tag or name, align_bytes=ALIGN)
+        def held(shape, dtype, name, on=None):
+            return keep.tile(shape, dtype, name=name, tag=on or name, align_bytes=ALIGN)
 
         def placed(shape, dtype, name, offset):
             return shared.tile(shape, dtype, name=name, align_bytes=ALIGN, offset=offset)
@@ -53,17 +55,20 @@ def tile_picked_decode2_relu_po_kernel(
         def looked_up(table, lists, start, count):
             return table.indirect(lists[:, start // LIST : (start + count) // LIST])
 
-        def interleave(copy, grouped, planes):
+        def group(copy, grouped, planes):
             copy(
-                grouped.rearrange("p (c i) t -> p c t i", i=4),
-                planes.rearrange("p t (c i) -> p c t i", i=4),
+                grouped.rearrange("p (c i) t -> p c t i", i=RUN),
+                planes.rearrange("p t (c i) -> p c t i", i=RUN),
             )
 
-        def product(out, codes, plane, t, moving, moving_scales):
+        def quantise(codes, scales, grouped):
+            nc.vector.quantize_mx(out=codes.bitcast(FP8X4), scales=scales, in_=grouped)
+
+        def product(out, codes, scales, t, moving, moving_scales):
             nc.tensor.matmul_mx(
                 out=out,
                 lhsT=codes[:, t * P : (t + 1) * P].bitcast(FP8X4),
-                lhsT_scale=plane[:, t * P : (t + 1) * P],
+                lhsT_scale=scales[:, t * P : (t + 1) * P],
                 rhs=moving.bitcast(FP8X4),
                 rhs_scale=moving_scales,
                 start=True,
@@ -76,8 +81,8 @@ def tile_picked_decode2_relu_po_kernel(
         xw_table = held([P, T], I32, "xw_table")
         w1_raw = placed([P, PACK, H], F32, "w1_raw", W1_AT)
         scl_second = held([P, PACK, HALF], F32, "scl_second")
-        b1_sb = scl_second[:, PACK - 1, :PACK]
-        scl_sb = [held([P, U], F32, "scl_sb%d" % t) for t in range(PACK - 1)]
+        b1_sb = scl_second[:, LAST, :PACK]
+        scl_sb = [held([P, U], F32, "scl_sb%d" % t) for t in range(LAST)]
 
         nc.vector.memset(xs_table[:, :CLEARED_BY_VECTOR].bitcast(I32), 0)
         nc.gpsimd.memset(xs_table[:, CLEARED_BY_VECTOR:].bitcast(I32), 0)
@@ -115,37 +120,27 @@ def tile_picked_decode2_relu_po_kernel(
         w1_scales = held([P, H], U8, "w1_scales")
         w1_grouped = []
         for pair in range(2):
-            w1_grouped.append(
-                placed([P, 2, P, PACK], BF16, "w1_grouped%d" % pair, ROUNDED_W1_AT[pair])
-            )
+            w1_grouped.append(placed([P, 2, P, PACK], BF16, "w1_grouped%d" % pair, ROUNDED_W1_AT[pair]))
             nc.scalar.copy(
                 w1_grouped[pair][:].rearrange("p t m j -> p m j t"),
                 w1_raw[:].rearrange("p j (m t) -> p m j t", t=PACK)[:, :, :, 2 * pair : 2 * pair + 2],
             )
 
-        def quantise_w1(pair):
-            code_cols = slice(2 * pair * P, 2 * (pair + 1) * P)
-            nc.vector.quantize_mx(
-                out=w1_codes[:, code_cols].bitcast(FP8X4),
-                scales=w1_scales[:, code_cols],
-                in_=w1_grouped[pair][:].rearrange("p t m j -> p (t m j)"),
-            )
-
         scl_first = held([P, PACK, HALF], F32, "scl_first")
-
         for pair in range(2):
             nc.vector.tensor_copy(scl_first[:, pair, :], looked_up(scl_sb[pair][:], rg_sb, 0, HALF))
-            quantise_w1(pair)
-        for t in range(PACK - 1):
+            cols = slice(2 * pair * P, 2 * (pair + 1) * P)
+            quantise(w1_codes[:, cols], w1_scales[:, cols], w1_grouped[pair][:].rearrange("p t m j -> p (t m j)"))
+        for t in range(LAST):
             scalar_gather(scl_second[:, t, :], looked_up(scl_sb[t][:], rg_sb, HALF, HALF))
 
         scl_sb.append(placed([P, U], F32, "scl_sb3", ROUNDED_W1_AT[0]))
-        nc.sync.dma_start(scl_sb[3][:], scl_rows[3])
+        nc.sync.dma_start(scl_sb[LAST][:], scl_rows[LAST])
         w2w_raw = placed([P, N], I32, "w2w_raw", W1_AT)
         nc.sync.dma_start(w2w_raw[:], w2_words[0].rearrange("p n t -> p (n t)").bitcast(I32))
         shf_sb = []
         for t in range(PACK):
-            at = W1_AT + (t + 1) * PLANE if t < PACK - 1 else ROUNDED_W1_AT[1] + N
+            at = W1_AT + (t + 1) * PLANE if t < LAST else ROUNDED_W1_AT[1] + N
             shf_sb.append(placed([P, U], F32, "shf_sb%d" % t, at))
             nc.sync.dma_start(shf_sb[t][:], shf_rows[t])
 
@@ -162,39 +157,28 @@ def tile_picked_decode2_relu_po_kernel(
             w2s_raw[:].rearrange("p (m t) -> p t m", t=PACK),
         )
 
-        def first_products(start, width, planes, tag):
-            bank = psum.tile([P, len(planes), width], F32, name="sums%d_%d" % (start, planes[0]), tag=tag)
+        def hidden_rows(half, planes, bank):
+            sums = psum.tile([P, len(planes), HALF], F32, name="sums%d_%d" % (half, planes[0]), tag=bank)
             for i, t in enumerate(planes):
-                for lo, hi in ((start, min(start + width, HALF)), (HALF, start + width)):
-                    if hi > lo:
-                        half, inner = divmod(lo, HALF)
-                        moving = xw_picked[half][:, inner : inner + hi - lo]
-                        out = bank[:, i, lo - start : hi - start]
-                        product(out, w1_codes, w1_scales, t, moving, xs_plane[:, lo:hi])
-            return bank
-
-        def hidden_rows(rows, start, planes, tag):
-            bank = first_products(start, rows.shape[2], planes, tag)
+                scales = xs_plane[:, half * HALF : (half + 1) * HALF]
+                product(sums[:, i, :], w1_codes, w1_scales, t, xw_picked[half][:], scales)
             for i, t in enumerate(planes):
-                nc.scalar.activation(rows[:, t, :], bank[:, i, :], RELU, bias=b1_sb[:, t : t + 1])
+                nc.scalar.activation(h_rows[half][:, t, :], sums[:, i, :], RELU, bias=b1_sb[:, t : t + 1])
 
         h_scales = held([P, S], U8, "h_scales")
         h_grouped, h_codes = {}, {}
 
-        def group_hidden(start, rows):
-            h_grouped[start] = held([P, rows.shape[2], PACK], BF16, "h_grouped%d" % start)
-            interleave(nc.vector.tensor_copy, h_grouped[start][:], rows)
+        def group_hidden(c):
+            h_grouped[c] = held([P, WIDTH, PACK], BF16, "h_grouped%d" % c)
+            group(nc.vector.tensor_copy, h_grouped[c][:], h_rows[0][:, :, c * WIDTH : (c + 1) * WIDTH])
 
-        def quantise_hidden(start, tag=None):
-            width = h_grouped[start].shape[1]
-            codes = held([P, width], U32, "h_codes%d" % start, tag)
-            for at in range(0, width, WIDTH):
-                h_codes[(start + at) // WIDTH] = codes[:, at : at + WIDTH]
-            nc.vector.quantize_mx(
-                out=codes[:].bitcast(FP8X4),
-                scales=h_scales[:, start : start + width],
-                in_=h_grouped[start][:].rearrange("p c t -> p (c t)"),
-            )
+        def quantise_hidden(c):
+            width = h_grouped[c].shape[1]
+            codes = held([P, width], U32, "h_codes%d" % c)
+            for i in range(width // WIDTH):
+                h_codes[c + i] = codes[:, i * WIDTH : (i + 1) * WIDTH]
+            scales = h_scales[:, c * WIDTH : c * WIDTH + width]
+            quantise(codes[:], scales, h_grouped[c][:].rearrange("p c t -> p (c t)"))
 
         out_scales = held([P, S], U8, "out_scales")
         out_rows = out_0.rearrange("(p t) j -> p t j", t=PACK)
@@ -202,110 +186,105 @@ def tile_picked_decode2_relu_po_kernel(
         out_scale_rows = out_2[0].bitcast(I32).rearrange("(q b) c -> b q c", b=PACK)
         scaled, results, rounded = {}, {}, {}
 
-        def scale(c, parts, tag=None):
-            cols = slice(c * WIDTH, (c + 1) * WIDTH)
-            inner = c * WIDTH % HALF
-            scaled[c] = held([P, PACK, WIDTH], F32, "scaled%d" % c, tag)
-            first = 0
-            for bank_tag, factors in parts:
-                count = sum(picked.shape[1] for picked in factors)
-                y = psum.tile([P, count, WIDTH], F32, name="y%d_%d" % (c, first), tag=bank_tag)
-                for i in range(count):
-                    product(y[:, i, :], w2_codes, w2_plane, first + i, h_codes[c], h_scales[:, cols])
-                at = 0
-                for picked in factors:
-                    count = picked.shape[1]
-                    nc.vector.tensor_tensor(
-                        scaled[c][:, first : first + count, :],
-                        y[:, at : at + count, :],
-                        picked[:, :, inner : inner + WIDTH],
-                        MULT,
-                    )
-                    at = at + count
-                    first = first + count
+        def chunk_tile(name, c, on=None):
+            return held([P, PACK, WIDTH], F32, "%s%d" % (name, c), on)[:]
 
-        def add_plain(c, planes, picked):
-            nc.vector.tensor_tensor(results[c][:, planes, :], picked, scaled[c][:, planes, :], ADD)
+        def chunk_of(picked, c):
+            inner = c * WIDTH % HALF
+            return picked[:, :, inner : inner + WIDTH]
+
+        def scale(c, into, bank, picked):
+            scaled[c] = into
+            y = psum.tile([P, PACK, WIDTH], F32, name="y%d" % c, tag=bank)
+            for t in range(PACK):
+                product(y[:, t, :], w2_codes, w2_plane, t, h_codes[c], h_scales[:, c * WIDTH : (c + 1) * WIDTH])
+            nc.vector.tensor_tensor(scaled[c], y[:], chunk_of(picked, c), MULT)
 
         def add_looked_up(c, t):
             window = looked_up(shf_sb[t][:], rg_sb, c * WIDTH, WIDTH)
             nc.vector.tensor_tensor(results[c][:, t, :], window, scaled[c][:, t, :], ADD)
 
         def store_result(c):
-            nc.sync.dma_start(out_rows[:, :, c * WIDTH : (c + 1) * WIDTH], results[c][:])
+            nc.sync.dma_start(out_rows[:, :, c * WIDTH : (c + 1) * WIDTH], results[c])
 
-        def shift(c, picked, tag=None):
-            results[c] = held([P, PACK, WIDTH], F32, "result%d" % c, tag)
+        def shift(c, picked, on=None):
+            results[c] = chunk_tile("result", c, on)
             ahead = picked.shape[1]
-            add_plain(c, slice(0, ahead), picked)
+            nc.vector.tensor_tensor(results[c][:, :ahead, :], picked, scaled[c][:, :ahead, :], ADD)
             for t in range(ahead, PACK):
                 add_looked_up(c, t)
             store_result(c)
 
-        def pick_shf(start, count, tag, planes=PACK):
-            picked = held([P, planes, count], F32, "shf_picked%d" % start, tag)
-            for t in range(planes):
-                scalar_gather(picked[:, t, :], looked_up(shf_sb[t][:], rg_sb, start, count))
-            return picked
-
         def round_result(copy, c):
             rounded[c] = held([P, WIDTH, PACK], BF16, "rounded%d" % c)
-            interleave(copy, rounded[c][:], results[c][:])
+            group(copy, rounded[c][:], results[c])
 
         def quantise_result(c):
             cols = slice(c * WIDTH, (c + 1) * WIDTH)
-            nc.vector.quantize_mx(
-                out=out_codes[:, cols].bitcast(FP8X4),
-                scales=out_scales[:, cols],
-                in_=rounded[c][:].rearrange("p c t -> p (c t)"),
-            )
+            quantise(out_codes[:, cols], out_scales[:, cols], rounded[c][:].rearrange("p c t -> p (c t)"))
 
-        rows = [held([P, PACK, HALF], BF16, "h_rows%d" % half) for half in range(2)]
-        hidden_rows(rows[0], 0, [0], "bank0")
-        hidden_rows(rows[0], 0, [1], "bank1")
-        hidden_rows(rows[0], 0, [2, 3], "bank2")
-        hidden_rows(rows[1], HALF, [0, 1], "bank3")
-        hidden_rows(rows[1], HALF, [2], "bank4")
-        hidden_rows(rows[1], HALF, [3], "bank5")
+        def store_codes(cols):
+            nc.sync.dma_start(out_words[:, cols], out_codes[:, cols].bitcast(I32))
+
+        h_rows = [held([P, PACK, HALF], BF16, "h_rows%d" % half) for half in range(2)]
+        hidden_rows(0, [0], "bank0")
+        hidden_rows(0, [1], "bank1")
+        hidden_rows(0, [2, 3], "bank2")
+        hidden_rows(1, [0, 1], "bank3")
+        hidden_rows(1, [2], "bank4")
+        hidden_rows(1, [3], "bank5")
 
         for t in range(2, PACK):
             nc.vector.tensor_copy(scl_first[:, t, :], looked_up(scl_sb[t][:], rg_sb, 0, HALF))
         nc.vector.tensor_copy(
-            w2_codes[:].rearrange("p (t c i) -> p c t i", t=PACK, i=4),
-            w2w_raw[:].rearrange("p (c i t) -> p c t i", t=PACK, i=4),
+            w2_codes[:].rearrange("p (t c i) -> p c t i", t=PACK, i=RUN),
+            w2w_raw[:].rearrange("p (c i t) -> p c t i", t=PACK, i=RUN),
         )
-        group_hidden(0, rows[0][:, :, :WIDTH])
-        group_hidden(WIDTH, rows[0][:, :, WIDTH:])
-        quantise_hidden(0)
-        quantise_hidden(WIDTH)
+        for c in range(2):
+            group_hidden(c)
+        for c in range(2):
+            quantise_hidden(c)
 
-        nc.vector.tensor_copy(scl_second[:, 3, :], looked_up(scl_sb[3][:], rg_sb, HALF, HALF))
-        shf_first = pick_shf(0, HALF, "h_grouped%d" % WIDTH, 3)
+        nc.vector.tensor_copy(scl_second[:, LAST, :], looked_up(scl_sb[LAST][:], rg_sb, HALF, HALF))
 
-        h_grouped[HALF] = held([P, HALF, PACK], BF16, "h_grouped%d" % HALF)
-        nc.gpsimd.tensor_scalar(h_grouped[HALF][:], rows[1][:].rearrange("p t c -> p c t"), 1.0, 0.0, MULT, ADD)
-        scale(0, [("bank4", [scl_first])])
-        scale(1, [("bank5", [scl_first])])
-        shf_late = pick_shf(HALF, HALF, "h_codes%d" % WIDTH)
-        quantise_hidden(HALF)
-        shift(0, shf_first[:, :, :WIDTH], "h_rows1")
-        shift(1, shf_first[:, :, WIDTH:], "h_grouped%d" % HALF)
-        scale(2, [("bank6", [scl_second])])
-        scale(3, [("bank7", [scl_second])])
-        rounded[1] = held([P, WIDTH, PACK], BF16, "rounded1")
-        nc.gpsimd.tensor_scalar(rounded[1][:], results[1][:].rearrange("p t c -> p c t"), 1.0, 0.0, MULT, ADD)
-        round_result(nc.scalar.copy, 0)
-        shift(2, shf_late[:, :, :WIDTH])
-        shift(3, shf_late[:, :, WIDTH:])
+        first = held([P, PACK * WIDTH + LAST * HALF], F32, "first", "h_grouped1")
+        shf_first = first[:, PACK * WIDTH :].rearrange("p (t c) -> p t c", c=HALF)
+        for t in range(2):
+            scalar_gather(shf_first[:, t, :], looked_up(shf_sb[t][:], rg_sb, 0, HALF))
+        scalar_gather(shf_first[:, 2, WIDTH:], looked_up(shf_sb[2][:], rg_sb, WIDTH, WIDTH))
+
+        h_grouped[2] = held([P, HALF, PACK], BF16, "h_grouped2")
+        nc.gpsimd.tensor_scalar(h_grouped[2][:], h_rows[1][:].rearrange("p t c -> p c t"), 1.0, 0.0, MULT, ADD)
+        scale(0, first[:, : PACK * WIDTH].rearrange("p (t c) -> p t c", c=WIDTH), "bank4", scl_first)
+        scale(1, chunk_tile("scaled", 1), "bank5", scl_first)
+
+        shf_second = held([P, PACK, HALF], F32, "shf_second", "h_codes1")
+        for t in range(PACK):
+            scalar_gather(shf_second[:, t, :], looked_up(shf_sb[t][:], rg_sb, HALF, HALF))
+
+        quantise_hidden(2)
+        shift(0, chunk_of(shf_first, 0)[:, :2, :], "h_rows1")
+
+        results[1] = first[:, WIDTH : (PACK + 1) * WIDTH].rearrange("p (t c) -> p t c", c=WIDTH)
+        add_looked_up(1, LAST)
+        nc.gpsimd.tensor_tensor(results[1][:, :LAST, :], chunk_of(shf_first, 1), scaled[1][:, :LAST, :], ADD)
+        store_result(1)
+        scale(2, chunk_tile("scaled", 2), "bank6", scl_second)
+        scale(3, chunk_tile("scaled", 3), "bank7", scl_second)
+        for c in range(2):
+            round_result(nc.scalar.copy, c)
+        for c in range(2, PACK):
+            shift(c, chunk_of(shf_second, c))
+
         out_codes = held([P, S], U32, "out_codes", "scaled2")
-        quantise_result(1)
-        quantise_result(0)
+        for c in range(2):
+            quantise_result(c)
         round_result(nc.scalar.copy, 2)
         round_result(nc.vector.tensor_copy, 3)
         quantise_result(2)
-        nc.sync.dma_start(out_words[:, : S - WIDTH], out_codes[:, : S - WIDTH].bitcast(I32))
+        store_codes(slice(0, S - WIDTH))
         quantise_result(3)
-        nc.sync.dma_start(out_words[:, S - WIDTH :], out_codes[:, S - WIDTH :].bitcast(I32))
+        store_codes(slice(S - WIDTH, S))
         for b in range(PACK):
             queue = nc.scalar if b % 2 else nc.sync
             queue.dma_start(out_scale_rows[b], out_scales[b:P:QUADRANT, :].bitcast(I32))

from contextlib import ExitStack

import concourse.mybir as mybir

K, T, S, H, N, U = 512, 2048, 512, 512, 512, 512
FLOPS = 2 * K * H * S + 2 * H * N * S

F32 = mybir.dt.float32
BF16 = mybir.dt.bfloat16
I32 = mybir.dt.int32
U32 = mybir.dt.uint32
U16 = mybir.dt.uint16
U8 = mybir.dt.uint8
FP8X4 = mybir.dt.float8_e4m3fn_x4
MULT = mybir.AluOpType.mult
ADD = mybir.AluOpType.add
RELU = mybir.ActivationFunctionType.Relu
COPY = mybir.ActivationFunctionType.Copy

P = 128
PACK = 4
LAST = PACK - 1
QUADRANT = 32
BLOCK = 8
LIST = 16
HALF = 256
WIDTH = 128
RUN = 4
CLEARED_BY_VECTOR = 3 * T // 4
ALIGN = 256

PLANE = 4 * U
W1_AT = 0
ROUNDED_W1_AT = (W1_AT + PACK * PLANE, W1_AT + (PACK + 1) * PLANE)


def tile_picked_decode2_relu_po_kernel(
    tc, x_words, x_scales, w1, b1, w2_words, w2_scales, scl, shf, offs, rg, out_0, out_1, out_2
):
    nc = tc.nc
    with ExitStack() as ctx:
        keep = ctx.enter_context(tc.tile_pool(name="keep", bufs=1))
        shared = ctx.enter_context(tc.tile_pool(name="shared", bufs=1))
        psum = ctx.enter_context(tc.psum_pool(name="psum", bufs=1))

        def held(shape, dtype, name, on=None):
            return keep.tile(shape, dtype, name=name, tag=on or name, align_bytes=ALIGN)

        def placed(shape, dtype, name, offset):
            return shared.tile(shape, dtype, name=name, align_bytes=ALIGN, offset=offset)

        def scalar_gather(out, window):
            nc.scalar.activation(out, window, COPY)

        def looked_up(table, lists, start, count):
            return table.indirect(lists[:, start // LIST : (start + count) // LIST])

        def group(copy, grouped, planes):
            copy(
                grouped.rearrange("p (c i) t -> p c t i", i=RUN),
                planes.rearrange("p t (c i) -> p c t i", i=RUN),
            )

        def quantise(codes, scales, grouped):
            nc.vector.quantize_mx(out=codes.bitcast(FP8X4), scales=scales, in_=grouped)

        def product(out, codes, scales, t, moving, moving_scales):
            nc.tensor.matmul_mx(
                out=out,
                lhsT=codes[:, t * P : (t + 1) * P].bitcast(FP8X4),
                lhsT_scale=scales[:, t * P : (t + 1) * P],
                rhs=moving.bitcast(FP8X4),
                rhs_scale=moving_scales,
                start=True,
                stop=True,
            )

        offs_sb = held([P, S // LIST], U16, "offs_sb")
        rg_sb = held([P, S // LIST], U16, "rg_sb")
        xs_table = held([P, T], U8, "xs_table")
        xw_table = held([P, T], I32, "xw_table")
        w1_raw = placed([P, PACK, H], F32, "w1_raw", W1_AT)
        scl_second = held([P, PACK, HALF], F32, "scl_second")
        b1_sb = scl_second[:, LAST, :PACK]
        scl_sb = [held([P, U], F32, "scl_sb%d" % t) for t in range(LAST)]

        nc.vector.memset(xs_table[:, :CLEARED_BY_VECTOR].bitcast(I32), 0)
        nc.gpsimd.memset(xs_table[:, CLEARED_BY_VECTOR:].bitcast(I32), 0)

        xs_plane = held([P, S], U8, "xs_plane")
        nc.vector.memset(xs_plane[:].bitcast(I32), 0)

        w2s_rows = w2_scales[0].bitcast(I32).rearrange("(q b) c -> b q c", b=PACK)
        scl_rows = scl.rearrange("(p t) u -> t p u", t=PACK)
        shf_rows = shf.rearrange("(p t) u -> t p u", t=PACK)

        nc.sync.dma_start(w1_raw[:], w1.rearrange("(p j) c -> p j c", j=PACK))
        nc.sync.dma_start(offs_sb[:], offs)
        nc.sync.dma_start(rg_sb[:], rg)
        nc.sync.dma_start(b1_sb, b1.rearrange("(p t) o -> p (t o)", t=PACK))
        nc.sync.dma_start(xs_table[0:P:BLOCK, :].bitcast(I32), x_scales[0].bitcast(I32))
        nc.sync.dma_start(scl_sb[0][:], scl_rows[0])
        nc.sync.dma_start(scl_sb[1][:], scl_rows[1])
        nc.sync.dma_start(xw_table[:], x_words[0].rearrange("p n t -> p (n t)").bitcast(I32))
        nc.sync.dma_start(scl_sb[2][:], scl_rows[2])

        w2s_raw = held([P, N], U8, "w2s_raw")
        nc.gpsimd.memset(w2s_raw[:].bitcast(I32), 0)
        for b in range(PACK):
            nc.gpsimd.dma_start(w2s_raw[b:P:QUADRANT, :].bitcast(I32), w2s_rows[b])

        xs_picked = held([P, S], U8, "xs_picked")
        nc.vector.tensor_copy(xs_picked[:], xs_table[:].indirect(offs_sb[:]))
        for b in range(PACK):
            nc.sync.dma_start(
                xs_plane[b:P:QUADRANT, :].bitcast(I32), xs_picked[BLOCK * b : P : QUADRANT, :].bitcast(I32)
            )

        w1_codes = held([P, H], U32, "w1_codes")
        w1_scales = held([P, H], U8, "w1_scales")
        w1_grouped = []
        for pair in range(2):
            w1_grouped.append(placed([P, 2, P, PACK], BF16, "w1_grouped%d" % pair, ROUNDED_W1_AT[pair]))
            nc.scalar.copy(
                w1_grouped[pair][:].rearrange("p t m j -> p m j t"),
                w1_raw[:].rearrange("p j (m t) -> p m j t", t=PACK)[:, :, :, 2 * pair : 2 * pair + 2],
            )

        scl_first = held([P, PACK, HALF], F32, "scl_first")
        for pair in range(2):
            nc.vector.tensor_copy(scl_first[:, pair, :], looked_up(scl_sb[pair][:], rg_sb, 0, HALF))
            cols = slice(2 * pair * P, 2 * (pair + 1) * P)
            quantise(w1_codes[:, cols], w1_scales[:, cols], w1_grouped[pair][:].rearrange("p t m j -> p (t m j)"))
        for t in range(LAST):
            scalar_gather(scl_second[:, t, :], looked_up(scl_sb[t][:], rg_sb, HALF, HALF))

        scl_sb.append(placed([P, U], F32, "scl_sb3", ROUNDED_W1_AT[0]))
        nc.sync.dma_start(scl_sb[LAST][:], scl_rows[LAST])
        w2w_raw = placed([P, N], I32, "w2w_raw", W1_AT)
        nc.sync.dma_start(w2w_raw[:], w2_words[0].rearrange("p n t -> p (n t)").bitcast(I32))
        shf_sb = []
        for t in range(PACK):
            at = W1_AT + (t + 1) * PLANE if t < LAST else ROUNDED_W1_AT[1] + N
            shf_sb.append(placed([P, U], F32, "shf_sb%d" % t, at))
            nc.sync.dma_start(shf_sb[t][:], shf_rows[t])

        xw_picked = [held([P, HALF], U32, "xw_picked%d" % half) for half in range(2)]
        for half in range(2):
            nc.vector.tensor_copy(
                xw_picked[half][:], looked_up(xw_table[:].bitcast(U32), offs_sb, half * HALF, HALF)
            )

        w2_codes = held([P, N], I32, "w2_codes")
        w2_plane = placed([P, N], U8, "w2_plane", ROUNDED_W1_AT[1])
        nc.gpsimd.tensor_copy(
            w2_plane[:].rearrange("p (t m) -> p t m", t=PACK),
            w2s_raw[:].rearrange("p (m t) -> p t m", t=PACK),
        )

        def hidden_rows(half, planes, bank):
            sums = psum.tile([P, len(planes), HALF], F32, name="sums%d_%d" % (half, planes[0]), tag=bank)
            for i, t in enumerate(planes):
                scales = xs_plane[:, half * HALF : (half + 1) * HALF]
                product(sums[:, i, :], w1_codes, w1_scales, t, xw_picked[half][:], scales)
            for i, t in enumerate(planes):
                nc.scalar.activation(h_rows[half][:, t, :], sums[:, i, :], RELU, bias=b1_sb[:, t : t + 1])

        h_scales = held([P, S], U8, "h_scales")
        h_grouped, h_codes = {}, {}

        def group_hidden(c):
            h_grouped[c] = held([P, WIDTH, PACK], BF16, "h_grouped%d" % c)
            group(nc.vector.tensor_copy, h_grouped[c][:], h_rows[0][:, :, c * WIDTH : (c + 1) * WIDTH])

        def quantise_hidden(c):
            width = h_grouped[c].shape[1]
            codes = held([P, width], U32, "h_codes%d" % c)
            for i in range(width // WIDTH):
                h_codes[c + i] = codes[:, i * WIDTH : (i + 1) * WIDTH]
            scales = h_scales[:, c * WIDTH : c * WIDTH + width]
            quantise(codes[:], scales, h_grouped[c][:].rearrange("p c t -> p (c t)"))

        out_scales = held([P, S], U8, "out_scales")
        out_rows = out_0.rearrange("(p t) j -> p t j", t=PACK)
        out_words = out_1[0].rearrange("p n t -> p (n t)").bitcast(I32)
        out_scale_rows = out_2[0].bitcast(I32).rearrange("(q b) c -> b q c", b=PACK)
        scaled, results, rounded = {}, {}, {}

        def chunk_tile(name, c, on=None):
            return held([P, PACK, WIDTH], F32, "%s%d" % (name, c), on)[:]

        def chunk_of(picked, c):
            inner = c * WIDTH % HALF
            return picked[:, :, inner : inner + WIDTH]

        def scale(c, into, bank, picked):
            scaled[c] = into
            y = psum.tile([P, PACK, WIDTH], F32, name="y%d" % c, tag=bank)
            for t in range(PACK):
                product(y[:, t, :], w2_codes, w2_plane, t, h_codes[c], h_scales[:, c * WIDTH : (c + 1) * WIDTH])
            nc.vector.tensor_tensor(scaled[c], y[:], chunk_of(picked, c), MULT)

        def add_looked_up(c, t):
            window = looked_up(shf_sb[t][:], rg_sb, c * WIDTH, WIDTH)
            nc.vector.tensor_tensor(results[c][:, t, :], window, scaled[c][:, t, :], ADD)

        def store_result(c):
            nc.sync.dma_start(out_rows[:, :, c * WIDTH : (c + 1) * WIDTH], results[c])

        def shift(c, picked, on=None):
            results[c] = chunk_tile("result", c, on)
            ahead = picked.shape[1]
            nc.vector.tensor_tensor(results[c][:, :ahead, :], picked, scaled[c][:, :ahead, :], ADD)
            for t in range(ahead, PACK):
                add_looked_up(c, t)
            store_result(c)

        def round_result(copy, c):
            rounded[c] = held([P, WIDTH, PACK], BF16, "rounded%d" % c)
            group(copy, rounded[c][:], results[c])

        def quantise_result(c):
            cols = slice(c * WIDTH, (c + 1) * WIDTH)
            quantise(out_codes[:, cols], out_scales[:, cols], rounded[c][:].rearrange("p c t -> p (c t)"))

        def store_codes(cols):
            nc.sync.dma_start(out_words[:, cols], out_codes[:, cols].bitcast(I32))

        h_rows = [held([P, PACK, HALF], BF16, "h_rows%d" % half) for half in range(2)]
        hidden_rows(0, [0], "bank0")
        hidden_rows(0, [1], "bank1")
        hidden_rows(0, [2, 3], "bank2")
        hidden_rows(1, [0, 1], "bank3")
        hidden_rows(1, [2], "bank4")
        hidden_rows(1, [3], "bank5")

        for t in range(2, PACK):
            nc.vector.tensor_copy(scl_first[:, t, :], looked_up(scl_sb[t][:], rg_sb, 0, HALF))
        nc.vector.tensor_copy(
            w2_codes[:].rearrange("p (t c i) -> p c t i", t=PACK, i=RUN),
            w2w_raw[:].rearrange("p (c i t) -> p c t i", t=PACK, i=RUN),
        )
        for c in range(2):
            group_hidden(c)
        for c in range(2):
            quantise_hidden(c)

        nc.vector.tensor_copy(scl_second[:, LAST, :], looked_up(scl_sb[LAST][:], rg_sb, HALF, HALF))

        first = held([P, PACK * WIDTH + LAST * HALF], F32, "first", "h_grouped1")
        shf_first = first[:, PACK * WIDTH :].rearrange("p (t c) -> p t c", c=HALF)
        for t in range(2):
            scalar_gather(shf_first[:, t, :], looked_up(shf_sb[t][:], rg_sb, 0, HALF))
        scalar_gather(shf_first[:, 2, WIDTH:], looked_up(shf_sb[2][:], rg_sb, WIDTH, WIDTH))

        h_grouped[2] = held([P, HALF, PACK], BF16, "h_grouped2")
        nc.gpsimd.tensor_scalar(h_grouped[2][:], h_rows[1][:].rearrange("p t c -> p c t"), 1.0, 0.0, MULT, ADD)
        scale(0, first[:, : PACK * WIDTH].rearrange("p (t c) -> p t c", c=WIDTH), "bank4", scl_first)
        scale(1, chunk_tile("scaled", 1), "bank5", scl_first)

        shf_second = held([P, PACK, HALF], F32, "shf_second", "h_codes1")
        for t in range(PACK):
            scalar_gather(shf_second[:, t, :], looked_up(shf_sb[t][:], rg_sb, HALF, HALF))

        quantise_hidden(2)
        shift(0, chunk_of(shf_first, 0)[:, :2, :], "h_rows1")

        results[1] = first[:, WIDTH : (PACK + 1) * WIDTH].rearrange("p (t c) -> p t c", c=WIDTH)
        add_looked_up(1, LAST)
        nc.gpsimd.tensor_tensor(results[1][:, :LAST, :], chunk_of(shf_first, 1), scaled[1][:, :LAST, :], ADD)
        store_result(1)
        scale(2, chunk_tile("scaled", 2), "bank6", scl_second)
        scale(3, chunk_tile("scaled", 3), "bank7", scl_second)
        for c in range(2):
            round_result(nc.scalar.copy, c)
        for c in range(2, PACK):
            shift(c, chunk_of(shf_second, c))

        out_codes = held([P, S], U32, "out_codes", "scaled2")
        for c in range(2):
            quantise_result(c)
        round_result(nc.scalar.copy, 2)
        round_result(nc.vector.tensor_copy, 3)
        quantise_result(2)
        store_codes(slice(0, S - WIDTH))
        quantise_result(3)
        store_codes(slice(S - WIDTH, S))
        for b in range(PACK):
            queue = nc.scalar if b % 2 else nc.sync
            queue.dma_start(out_scale_rows[b], out_scales[b:P:QUADRANT, :].bitcast(I32))
